import numpy as np
import ml_dtypes


def mxq(x, axis, fmt="e4m3"):
    dtype, down = {"e4m3": (ml_dtypes.float8_e4m3fn, 7), "e5m2": (ml_dtypes.float8_e5m2, 14)}[fmt]
    v = np.moveaxis(np.asarray(x, np.float32).astype(ml_dtypes.bfloat16).astype(np.float64), axis, -1)
    blocks = v.reshape(v.shape[:-1] + (-1, 32))
    amax = np.abs(blocks).max(-1, keepdims=True)
    byte = np.maximum(np.where(amax > 0, np.frexp(amax)[1] - 1 + 127, 0) - down, 1)
    scale = np.exp2(byte - 127.0)
    codes = (blocks / scale).astype(np.float32).astype(dtype).astype(np.float64)
    return np.moveaxis((codes * scale).reshape(v.shape), -1, axis)


WIDE = False


def mx_kscale(k):
    if not WIDE:
        return np.ones(k)
    levels = np.array([10, -10, 5, -5, 0])
    if k % 512:
        return np.exp2(np.random.permutation(np.resize(levels, k // 32))).repeat(32)
    a = np.empty((k // 512, 16))
    for p in range(k // 512):
        a[p, :8] = np.random.permutation(np.resize(levels, 8))
        for g in range(8):
            far = levels[np.abs(levels - a[p, g]) >= 10]
            a[p, g + 8] = far[np.random.randint(len(far))]
    return np.exp2(a.ravel()).repeat(32)


def f64(x):
    return np.asarray(x).astype(np.float64)


def striped(idx):
    return np.tile(idx.reshape(-1, 16).T, (8, 1)).astype(np.uint16)


def unstriped(offs):
    return offs[:16].T.reshape(-1).astype(np.int64)


E2M1 = np.array([0.0, 0.5, 1.0, 1.5, 2.0, 3.0, 4.0, 6.0, -0.0, -0.5, -1.0, -1.5, -2.0, -3.0, -4.0, -6.0])


def pack_weight(w, fmt):
    k, n = w.shape
    w = f64(np.asarray(w, np.float32).astype(ml_dtypes.bfloat16)).reshape(k // 32, 32, n)
    amax = np.abs(w).max(1)
    if fmt == "e4m3":
        byte = np.frexp(amax)[1] - 1 + 127 - 7
    else:
        mant, ex = np.frexp(amax / 6.0)
        byte = np.where(mant > 0.5, ex, ex - 1) + 127
    byte = np.clip(np.where(amax > 0, byte, 1), 1, 254)
    scaled = (w * np.exp2(127.0 - byte)[:, None, :]).reshape(k, n).astype(np.float32)
    by_word = np.ascontiguousarray(scaled.reshape(k // 512, 128, 4, n).transpose(0, 1, 3, 2))
    if fmt == "e4m3":
        words = by_word.astype(ml_dtypes.float8_e4m3fn).view(np.uint8)
    else:
        c = by_word.astype(ml_dtypes.float4_e2m1fn).view(np.uint8) & 0xF
        words = (c[..., 0::2] | (c[..., 1::2] << 4)).reshape(k // 512, 128, 2 * n)
    return np.ascontiguousarray(words), np.ascontiguousarray(byte.astype(np.uint8).reshape(k // 512, 16, n))


def unpack_weight(words, scales, fmt):
    g, _, n = scales.shape
    words = np.ascontiguousarray(words).reshape(g, 128, n, -1)
    if fmt == "e4m3":
        vals = words.view(ml_dtypes.float8_e4m3fn).astype(np.float64)
    else:
        nib = np.empty((g, 128, n, 4), np.uint8)
        nib[..., 0::2] = words & 0xF
        nib[..., 1::2] = words >> 4
        vals = E2M1[nib]
    vals = vals * np.repeat(np.exp2(scales.astype(np.float64) - 127.0), 8, axis=1)[..., None]
    return vals.transpose(0, 1, 3, 2).reshape(g * 512, n)


def relu2(v):
    return np.maximum(v, 0.0) ** 2


K, T, E, C, H, N = 1024, 512, 4, 256, 512, 384


def by_expert(wq, xq):
    return np.concatenate([wq[e].T @ xq[:, e * C:(e + 1) * C] for e in range(E)], axis=1)


def setup_inputs():
    n = np.random.standard_normal
    s = mx_kscale(K)[:, None]
    u = mx_kscale(H)
    first = np.random.permutation(np.repeat(np.arange(E), T // E))
    second = (first + 1 + np.random.permutation(np.repeat(np.arange(E - 1), -(-T // (E - 1)))[:T])) % E
    while np.bincount(second, minlength=E).max() != T // E:
        load = np.bincount(second, minlength=E); hi, lo = int(load.argmax()), int(load.argmin())
        t = np.flatnonzero((second == hi) & (first != lo))[0]; second[t] = lo
    slot_token = np.empty(E * C, np.int64); pos = np.empty((2, T), np.int64); fill = np.zeros(E, np.int64)
    place = np.stack([np.random.permutation(C) for _ in range(E)])
    for r, deal in enumerate((first, second)):
        for t in np.random.permutation(T):
            e = deal[t]; j = e * C + place[e, fill[e]]; fill[e] += 1; slot_token[j] = t; pos[r, t] = j
    g = np.random.uniform(0.2, 0.8, T)
    w1 = [pack_weight(m, "e2m1") for m in n((E + 1, K, H)) / np.sqrt(K) / s[None] * u[None, None, :]]
    w2 = [pack_weight(m, "e2m1") for m in n((E + 1, H, N)) / np.sqrt(H) / u[None, :, None] ** 2]
    return {
        "xT": (n((K, T)) * s).astype(np.float32),
        "w1_words": np.stack([m[0] for m in w1]),
        "w1_scales": np.stack([m[1] for m in w1]),
        "w2_words": np.stack([m[0] for m in w2]),
        "w2_scales": np.stack([m[1] for m in w2]),
        "gate": np.stack([np.tile(g, (N, 1)), np.tile(1.0 - g, (N, 1))]).astype(np.float32),
        "offs": striped(slot_token),
        "pos1": striped(pos[0]),
        "pos2": striped(pos[1]),
    }


def reference(xT, w1_words, w1_scales, w2_words, w2_scales, gate, offs, pos1, pos2):
    idx = unstriped(offs)
    w1 = np.stack([unpack_weight(w1_words[e], w1_scales[e], "e2m1") for e in range(E + 1)])
    w2 = np.stack([unpack_weight(w2_words[e], w2_scales[e], "e2m1") for e in range(E + 1)])
    w1q, w2q = w1, w2
    xs = mxq(f64(xT), 0, "e4m3")
    hs = relu2(w1q[E].T @ xs)
    ys = w2q[E].T @ mxq(hs, 0, "e4m3")
    xq = mxq(f64(xT)[:, idx], 0, "e4m3")
    h = relu2(by_expert(w1q, xq))
    y = by_expert(w2q, mxq(h, 0, "e4m3"))
    return ys + f64(gate[0]) * y[:, unstriped(pos1)] + f64(gate[1]) * y[:, unstriped(pos2)]

@@ -1,0 +1,314 @@
+from contextlib import ExitStack
+
+import concourse.mybir as mybir
+from concourse.masks import make_identity
+
+K, T, E, C, H, N = 1024, 512, 4, 256, 512, 384
+FLOPS = 2 * (E * C + T) * H * (K + N)
+
+F32 = mybir.dt.float32
+BF16 = mybir.dt.bfloat16
+I32 = mybir.dt.int32
+U32 = mybir.dt.uint32
+U16 = mybir.dt.uint16
+U8 = mybir.dt.uint8
+FP8X4 = mybir.dt.float8_e4m3fn_x4
+FP4X4 = mybir.dt.float4_e2m1fn_x4
+RELU = mybir.ActivationFunctionType.Relu
+SQUARE = mybir.ActivationFunctionType.Square
+COPY = mybir.ActivationFunctionType.Copy
+MULT = mybir.AluOpType.mult
+ADD = mybir.AluOpType.add
+
+P = 128
+S = K // 512
+NC = N // P
+
+
+def tile_moe_shr_mlp_relu2_kernel(
+    tc, xT, w1_words, w1_scales, w2_words, w2_scales, gate, offs, pos1, pos2, out
+):
+    nc = tc.nc
+    with ExitStack() as ctx:
+        keep = ctx.enter_context(tc.tile_pool(name="keep", bufs=1))
+        work = ctx.enter_context(tc.tile_pool(name="work", bufs=3))
+        pa = ctx.enter_context(tc.psum_pool(name="pa", bufs=3))
+        pt = ctx.enter_context(tc.psum_pool(name="pt", bufs=3))
+        py = ctx.enter_context(tc.psum_pool(name="py", bufs=2))
+
+        offs_sb = keep.tile([P, E * C // 16], U16, name="offs_sb")
+        pos_sb = [keep.tile([P, T // 16], U16, name=f"pos_sb{r}") for r in range(2)]
+        ident = keep.tile([P, P], F32, name="ident")
+        x = [keep.tile([P, 4, T], F32, name=f"x{s}") for s in range(S)]
+        pairs = keep.tile([P, 2 * S, 2 * T], BF16, name="pairs", align_bytes=64)
+        w1 = keep.tile([P, (E + 1) * S, 2 * H], U8, name="w1", align_bytes=64)
+        w1s = keep.tile([P, (E + 1) * S, H], U8, name="w1s", align_bytes=64)
+        w2 = keep.tile([P, E + 1, 2 * N], U8, name="w2", align_bytes=64)
+        w2s = keep.tile([P, E + 1, N], U8, name="w2s", align_bytes=64)
+        gt = keep.tile([P, 2, NC, T], F32, name="gt")
+        y = [keep.tile([P, E * C], F32, name=f"y{c}") for c in range(NC)]
+        warm = keep.tile([P, 1], F32, name="warm")
+
+        nc.vector.memset(warm[:], 0.0)
+        nc.scalar.activation(warm[:], warm[:], RELU)
+        nc.gpsimd.memset(w1s[:].bitcast(I32), 0)
+        nc.gpsimd.memset(w2s[:].bitcast(I32), 0)
+        make_identity(nc, ident[:])
+
+        xv = xT.rearrange("(s p d) t -> s p d t", s=S, d=4)
+        for s in range(S):
+            for u in range(2):
+                nc.sync.dma_start(out=x[s][:, 2 * u : 2 * u + 2, :], in_=xv[s, :, 2 * u : 2 * u + 2, :])
+                if s == 0 and u == 0:
+                    nc.sync.dma_start(offs_sb[:], offs)
+        sv1 = w1_scales.rearrange("e s (q r) i -> q r (e s) i", q=4)
+        sv2 = w2_scales.rearrange("e s (q r) i -> q r (e s) i", q=4)
+        for q in range(4):
+            nc.sync.dma_start(out=w1s[32 * q : 32 * q + 4, :, :].bitcast(I32), in_=sv1[q].bitcast(I32))
+        order = [0, 1, 2, E, 3]
+        for e in order[:2]:
+            nc.sync.dma_start(out=w1[:, S * e : S * e + S, :].bitcast(I32), in_=w1_words[e].rearrange("s p b -> p s b").bitcast(I32))
+        for q in range(4):
+            nc.sync.dma_start(out=w2s[32 * q : 32 * q + 4, :, :].bitcast(I32), in_=sv2[q].bitcast(I32))
+        for e in order[2:]:
+            nc.sync.dma_start(out=w1[:, S * e : S * e + S, :].bitcast(I32), in_=w1_words[e].rearrange("s p b -> p s b").bitcast(I32))
+        nc.sync.dma_start(out=w2[:].bitcast(I32), in_=w2_words.rearrange("e s p b -> p (e s) b").bitcast(I32))
+        for r, lst in enumerate((pos1, pos2)):
+            nc.sync.dma_start(pos_sb[r][:], lst)
+        for c in range(NC):
+            nc.sync.dma_start(out=gt[:, :, c, :], in_=gate.rearrange("g (c p) t -> c p g t", p=P)[c])
+
+        hc = keep.tile([P, T], U32, name="hc", align_bytes=64)
+        hss = keep.tile([P, T], U8, name="hss", align_bytes=64)
+
+        def cast_pairs(j):
+            s, u = divmod(j, 2)
+            dst = pairs[:, j, :].rearrange("p (t d) -> p t d", d=2)
+            src = x[s][:, 2 * u : 2 * u + 2, :].rearrange("p d t -> p t d")
+            if j == 0:
+                nc.vector.tensor_copy(out=dst, in_=src)
+            else:
+                nc.scalar.activation(dst, src, COPY)
+
+        def new_gathered():
+            return work.tile([P, 2 * S, 2 * C], BF16, name="g", align_bytes=64, bufs=2)
+
+        def gather(e, g, j):
+            nc.vector.tensor_copy(
+                g[:, j, :].bitcast(U32),
+                pairs[:, j, :].bitcast(U32).indirect(offs_sb[:, e * C // 16 : (e + 1) * C // 16]),
+            )
+
+        def new_codes():
+            gi = work.tile([P, S, 4 * C], BF16, name="gi", align_bytes=64, bufs=1)
+            xc = work.tile([P, S, C], U32, name="xc", align_bytes=64)
+            xsc = work.tile([P, S, C], U8, name="xsc", align_bytes=64)
+            return gi, xc, xsc
+
+        def interleave_on_scalar(g, gi, s):
+            nc.scalar.copy(
+                gi[:, s, :].rearrange("p (c u d) -> p c u d", u=2, d=2),
+                g[:, 2 * s : 2 * s + 2, :].rearrange("p u (c d) -> p c u d", d=2),
+            )
+
+        def interleave(g, gi, s0, s1):
+            nc.vector.tensor_copy(
+                out=gi[:, s0:s1, :].bitcast(I32).rearrange("p s (c u) -> p s c u", u=2),
+                in_=g[:, 2 * s0 : 2 * s1, :].bitcast(I32).rearrange("p (s u) c -> p s c u", u=2),
+            )
+
+        def quantize(gi, xc, xsc, s0, s1):
+            nc.vector.quantize_mx(
+                out=xc[:, s0:s1, :].rearrange("p s c -> p (s c)").bitcast(FP8X4),
+                scales=xsc[:, s0:s1, :].rearrange("p s c -> p (s c)"),
+                in_=gi[:, s0:s1, :].rearrange("p s c -> p (s c)"),
+            )
+
+        def start1(k):
+            acc[k] = [pa.tile([P, H], F32, name="a") for m in range(2)]
+
+        def pass1(k, e, xc, xsc, c0, s, ms=(0, 1)):
+            for m in ms:
+                cols = slice(c0 + P * m, c0 + P * (m + 1))
+                nc.tensor.matmul_mx(
+                    out=acc[k][m][:],
+                    lhsT=xc[:, s, cols].bitcast(FP8X4),
+                    lhsT_scale=xsc[:, s, cols],
+                    rhs=w1[:, S * e + s, :].bitcast(FP4X4),
+                    rhs_scale=w1s[:, S * e + s, :],
+                    start=(s == 0),
+                    stop=(s == S - 1),
+                )
+
+        def relu(k, vector_tiles=()):
+            rs[k] = []
+            for m in range(2):
+                r = work.tile([P, 4, P], F32, name="r", bufs=8)
+                src = acc[k][m][:].rearrange("m (p t) -> m t p", t=4)
+                if m in vector_tiles:
+                    nc.vector.tensor_scalar(r[:], src, 0.0, None, mybir.AluOpType.max)
+                else:
+                    nc.scalar.activation(r[:], src, RELU)
+                rs[k].append(r)
+
+        def first(k, e, xc, xsc, c0, vector_tiles=()):
+            start1(k)
+            for m in range(2):
+                for s in range(S):
+                    pass1(k, e, xc, xsc, c0, s, (m,))
+            relu(k, vector_tiles)
+
+        def turn(k, hi):
+            for m in range(2):
+                tp = pt.tile([P, 4, P], F32, name="tp")
+                for q in range(4):
+                    nc.tensor.transpose(tp[:, q, :], rs[k][m][:, q, :], ident[:])
+                nc.scalar.activation(hi[:, m, :].rearrange("p (r t) -> p r t", t=4), tp[:].rearrange("p t r -> p r t"), SQUARE)
+
+        def quantize_h(hi, hq, hs):
+            nc.vector.quantize_mx(out=hq.bitcast(FP8X4), scales=hs, in_=hi.rearrange("p m c -> p (m c)"))
+
+        def turned(e):
+            his[e] = work.tile([P, 2, 4 * P], BF16, name="hi", align_bytes=64)
+            turn(e, his[e][:])
+
+        def hidden(e):
+            hqs[e] = (work.tile([P, C], U32, name="hq", align_bytes=64, bufs=4), work.tile([P, C], U8, name="hs", align_bytes=64, bufs=4))
+            quantize_h(his[e][:], hqs[e][0][:], hqs[e][1][:])
+
+        def layer2(e, dst, n, hq, hs):
+            nc.tensor.matmul_mx(
+                out=dst,
+                lhsT=w2[:, e, 2 * P * n : 2 * P * (n + 1)].bitcast(FP4X4),
+                lhsT_scale=w2s[:, e, P * n : P * (n + 1)],
+                rhs=hq.bitcast(FP8X4),
+                rhs_scale=hs,
+                start=True,
+                stop=True,
+            )
+
+        def results(e0, *ns):
+            for n in ns:
+                yp = py.tile([P, 2, C], F32, name="yp")
+                for e in range(e0, e0 + 2):
+                    layer2(e, yp[:, e - e0, :], n, hqs[e][0][:], hqs[e][1][:])
+                dst = y[n][:, e0 * C : (e0 + 2) * C]
+                src = yp[:].rearrange("p e c -> p (e c)")
+                if n == 0 or (e0, n) == (0, 1):
+                    nc.vector.tensor_copy(dst, src)
+                else:
+                    nc.scalar.copy(dst, src)
+
+        acc, rs, his, hqs = {}, {}, {}, {}
+        g = [new_gathered() for e in range(2)]
+        codes = []
+
+        def more():
+            g.append(new_gathered())
+
+        def gath(e, *js):
+            for j in js:
+                gather(e, g[e], j)
+
+        def inter(e, s0, s1):
+            if e == len(codes):
+                codes.append(new_codes())
+            interleave(g[e], codes[e][0], s0, s1)
+
+        def quant(e, s0, s1):
+            quantize(codes[e][0], codes[e][1], codes[e][2], s0, s1)
+
+        def routed(e, vector_tiles=()):
+            first(e, e, codes[e][1], codes[e][2], 0, vector_tiles)
+
+        for j in range(2 * S):
+            cast_pairs(j)
+        gath(0, 0)
+        gath(1, 0)
+        gath(0, 1)
+        gath(1, 1)
+        codes.append(new_codes())
+        interleave_on_scalar(g[0], codes[0][0], 0)
+        gath(0, 2, 3)
+        inter(0, 1, 2)
+        gath(1, 2, 3)
+        quant(0, 0, 1)
+        start1(0)
+        pass1(0, 0, codes[0][1], codes[0][2], 0, 0)
+        quant(0, 1, 2)
+        pass1(0, 0, codes[0][1], codes[0][2], 0, 1)
+        relu(0)
+        inter(1, 0, 2)
+        more()
+        gath(2, 0)
+        quant(1, 0, 2)
+        routed(1)
+        gath(2, 1, 2)
+        turned(0)
+        gath(2, 3)
+        inter(2, 0, 2)
+        more()
+        gath(3, 0)
+        quant(2, 0, 2)
+        routed(2)
+        gath(3, 1, 2)
+        inter(3, 0, 1)
+        gath(3, 3)
+        turned(1)
+        quant(3, 0, 1)
+        inter(3, 1, 2)
+        quant(3, 1, 2)
+        start1(3)
+        for s in range(S):
+            pass1(3, 3, codes[3][1], codes[3][2], 0, s)
+        relu(3)
+        hidden(0)
+        hidden(1)
+        xs = work.tile([P, S, 4 * T], BF16, name="gi", align_bytes=64, bufs=1)
+        sc = keep.tile([P, S, T], U32, name="sc", align_bytes=64)
+        ss = keep.tile([P, S, T], U8, name="ss", align_bytes=64)
+        for s in range(S):
+            interleave(pairs, xs, s, s + 1)
+        for s in range(S):
+            nc.vector.quantize_mx(out=sc[:, s, :].bitcast(FP8X4), scales=ss[:, s, :], in_=xs[:, s, :])
+        for e in (2, 3):
+            turned(e)
+            hidden(e)
+        results(0, 0, 1)
+        results(2, 0, 1)
+        for half in range(2):
+            first(E + half, E, sc, ss, C * half)
+        hsi = keep.tile([P, 4, 4 * P], BF16, name="hsi", align_bytes=64)
+        for half in range(2):
+            turn(E + half, hsi[:, 2 * half : 2 * half + 2, :])
+        quantize_h(hsi[:], hc[:], hss[:])
+        results(0, 2)
+        results(2, 2)
+
+        t1, t2 = [], []
+        for n in range(NC):
+            for r, ts in enumerate((t1, t2)):
+                t = keep.tile([P, T], F32, name=f"t{r}{n}")
+                nc.vector.tensor_tensor(t[:], y[n][:].indirect(pos_sb[r][:]), gt[:, r, n, :], MULT)
+                ts.append(t)
+        ysp = []
+        for n in range(NC):
+            ysp.append(pa.tile([P, T], F32, name="a"))
+            layer2(E, ysp[n][:], n, hc[:], hss[:])
+        t3 = [keep.tile([P, T], F32, name=f"t3{n}") for n in range(NC)]
+        o = [keep.tile([P, T], F32, name=f"o{n}") for n in range(NC)]
+
+        def plus_shared(n):
+            nc.vector.tensor_tensor(t3[n][:], t1[n][:], ysp[n][:], ADD)
+
+        def finish(n, c0, c1, engine):
+            engine.tensor_tensor(o[n][:, c0:c1], t2[n][:, c0:c1], t3[n][:, c0:c1], ADD)
+            nc.sync.dma_start(out=out[P * n : P * (n + 1), c0:c1], in_=o[n][:, c0:c1])
+
+        plus_shared(0)
+        finish(0, 0, T, nc.gpsimd)
+        plus_shared(1)
+        plus_shared(2)
+        finish(1, 0, T, nc.vector)
+        finish(2, 0, T // 2, nc.vector)
+        finish(2, T // 2, T, nc.vector)

@@ -31,284 +31,333 @@ def tile_moe_shr_mlp_relu2_kernel(
     nc = tc.nc
     with ExitStack() as ctx:
         keep = ctx.enter_context(tc.tile_pool(name="keep", bufs=1))
-        work = ctx.enter_context(tc.tile_pool(name="work", bufs=3))
-        pa = ctx.enter_context(tc.psum_pool(name="pa", bufs=3))
-        pt = ctx.enter_context(tc.psum_pool(name="pt", bufs=3))
-        py = ctx.enter_context(tc.psum_pool(name="py", bufs=2))
+        psum = ctx.enter_context(tc.psum_pool(name="psum", bufs=1))
+        A0, A1, A2, T0, T1, T2, Y0, Y1 = [psum.tile([P, 512], F32, name=f"bank{b}") for b in range(8)]
 
         offs_sb = keep.tile([P, E * C // 16], U16, name="offs_sb")
         pos_sb = [keep.tile([P, T // 16], U16, name=f"pos_sb{r}") for r in range(2)]
         ident = keep.tile([P, P], F32, name="ident")
-        x = [keep.tile([P, 4, T], F32, name=f"x{s}") for s in range(S)]
-        pairs = keep.tile([P, 2 * S, 2 * T], BF16, name="pairs", align_bytes=64)
-        w1 = keep.tile([P, (E + 1) * S, 2 * H], U8, name="w1", align_bytes=64)
+        planes = [1, 0, 3, 2]
+        cuts = {j: 2 if j in (planes[0], planes[-1]) else 1 for j in planes}
+        x = [[keep.tile([P, 2, T // cuts[j]], F32, name=f"x{j}{h}") for h in range(cuts[j])] for j in range(2 * S)]
+        pairs = [keep.tile([P, 4 * T], BF16, name=f"pairs{s}", align_bytes=64) for s in range(S)]
+        w1 = [keep.tile([P, S, 2 * H], U8, name=f"w1_{e}", align_bytes=64) for e in range(E + 1)]
         w1s = keep.tile([P, (E + 1) * S, H], U8, name="w1s", align_bytes=64)
         w2 = keep.tile([P, E + 1, 2 * N], U8, name="w2", align_bytes=64)
         w2s = keep.tile([P, E + 1, N], U8, name="w2s", align_bytes=64)
-        gt = keep.tile([P, 2, NC, T], F32, name="gt")
+        gt = keep.tile([P, 2, T], F32, name="gt")
         y = [keep.tile([P, E * C], F32, name=f"y{c}") for c in range(NC)]
         warm = keep.tile([P, 1], F32, name="warm")
 
         nc.vector.memset(warm[:], 0.0)
         nc.scalar.activation(warm[:], warm[:], RELU)
-        nc.gpsimd.memset(w1s[:].bitcast(I32), 0)
-        nc.gpsimd.memset(w2s[:].bitcast(I32), 0)
+        nc.vector.memset(w1s[:].bitcast(I32), 0)
+        nc.vector.memset(w2s[:].bitcast(I32), 0)
         make_identity(nc, ident[:])
 
         xv = xT.rearrange("(s p d) t -> s p d t", s=S, d=4)
-        for s in range(S):
-            for u in range(2):
-                nc.sync.dma_start(out=x[s][:, 2 * u : 2 * u + 2, :], in_=xv[s, :, 2 * u : 2 * u + 2, :])
-                if s == 0 and u == 0:
-                    nc.sync.dma_start(offs_sb[:], offs)
+        for j in planes:
+            s, u = divmod(j, 2)
+            width = T // cuts[j]
+            for h in range(cuts[j]):
+                nc.sync.dma_start(out=x[j][h][:], in_=xv[s, :, 2 * u : 2 * u + 2, width * h : width * (h + 1)])
+            if j == planes[0]:
+                nc.sync.dma_start(offs_sb[:], offs)
         sv1 = w1_scales.rearrange("e s (q r) i -> q r (e s) i", q=4)
         sv2 = w2_scales.rearrange("e s (q r) i -> q r (e s) i", q=4)
-        for q in range(4):
-            nc.sync.dma_start(out=w1s[32 * q : 32 * q + 4, :, :].bitcast(I32), in_=sv1[q].bitcast(I32))
-        order = [0, 1, 2, E, 3]
-        for e in order[:2]:
-            nc.sync.dma_start(out=w1[:, S * e : S * e + S, :].bitcast(I32), in_=w1_words[e].rearrange("s p b -> p s b").bitcast(I32))
+
+        def load_w1(e):
+            nc.sync.dma_start(out=w1[e][:].bitcast(I32), in_=w1_words[e].rearrange("s p b -> p s b").bitcast(I32))
+
+        def load_w1_scales(e0, e1):
+            for q in range(4):
+                nc.sync.dma_start(
+                    out=w1s[32 * q : 32 * q + 4, S * e0 : S * e1, :].bitcast(I32), in_=sv1[q, :, S * e0 : S * e1, :].bitcast(I32)
+                )
+
+        load_w1(0)
+        load_w1_scales(0, 2)
+        load_w1(1)
+        load_w1_scales(2, E + 1)
+        for e in range(2, E):
+            load_w1(e)
         for q in range(4):
             nc.sync.dma_start(out=w2s[32 * q : 32 * q + 4, :, :].bitcast(I32), in_=sv2[q].bitcast(I32))
-        for e in order[2:]:
-            nc.sync.dma_start(out=w1[:, S * e : S * e + S, :].bitcast(I32), in_=w1_words[e].rearrange("s p b -> p s b").bitcast(I32))
         nc.sync.dma_start(out=w2[:].bitcast(I32), in_=w2_words.rearrange("e s p b -> p (e s) b").bitcast(I32))
+        load_w1(E)
         for r, lst in enumerate((pos1, pos2)):
             nc.sync.dma_start(pos_sb[r][:], lst)
-        for c in range(NC):
-            nc.sync.dma_start(out=gt[:, :, c, :], in_=gate.rearrange("g (c p) t -> c p g t", p=P)[c])
+        nc.sync.dma_start(out=gt[:], in_=gate[:, 0:P, :].rearrange("g p t -> p g t"))
 
+        def plane(j):
+            s, u = divmod(j, 2)
+            return pairs[s][:, 2 * T * u : 2 * T * (u + 1)]
+
+        def cast(j, on_vector):
+            width = 2 * T // cuts[j]
+            for h in range(cuts[j]):
+                dst = plane(j)[:, width * h : width * (h + 1)].rearrange("p (t d) -> p t d", d=2)
+                src = x[j][h][:].rearrange("p d t -> p t d")
+                if on_vector:
+                    nc.vector.tensor_copy(out=dst, in_=src)
+                else:
+                    nc.scalar.activation(dst, src, COPY)
+
+        ga = keep.tile([P, 2 * C], U32, name="ga")
+        gc = keep.tile([P, 2 * C], U32, name="gc")
+        gd = keep.tile([P, 2 * C], U32, name="gd")
+        ring0 = keep.tile([P, 3 * C], U32, name="ring0", align_bytes=64)
+        gi = {(e, s): keep.tile([P, 2 * C], U32, name=f"gi{e}{s}", align_bytes=64)[:] for e in range(E) for s in range(S) if (e, s) not in ((0, 1), (1, 1), (2, 0))}
+        ring1 = keep.tile([P, 4 * C], U32, name="ring1", align_bytes=64)
+
+        def halves(ap):
+            return ap.rearrange("p (u c) -> p u c", u=2)
+
+        room = {
+            (0, 0): halves(ga[:]), (1, 0): halves(gc[:]), (2, 0): halves(ring0[:, C : 3 * C]), (3, 0): halves(ring1[:, C : 3 * C]),
+            (0, 1): halves(gd[:]), (1, 1): halves(ga[:]), (2, 1): halves(gd[:]), (3, 1): halves(gd[:]),
+        }
+        woven = dict(gi)
+        woven[0, 1] = ring0[:, 0 : 2 * C]
+        woven[2, 0] = ring1[:, 0 : 2 * C]
+        woven[1, 1] = ring1[:, 2 * C : 4 * C]
+        xc = [keep.tile([P, S * C], U32, name=f"xc{e}", align_bytes=64)[:] for e in (0, 1, 3)]
+        xsc = [keep.tile([P, S * C], U8, name=f"xsc{e}", align_bytes=64) for e in range(E)]
+        xs = keep.tile([P, S * 4 * T], BF16, name="xs", align_bytes=64)
+        sc = keep.tile([P, S * T], U32, name="sc", align_bytes=64)
+        ss = keep.tile([P, S * T], U8, name="ss", align_bytes=64)
+        hi = [keep.tile([P, 4 * C], BF16, name=f"hi{e}", align_bytes=64)[:] for e in range(E)]
+        xc.insert(2, sc[:, T - C : T + C])
+        hq = [keep.tile([P, C], U32, name=f"hq{e}", align_bytes=64) for e in range(E)]
+        hs = [keep.tile([P, C], U8, name=f"hs{e}", align_bytes=64) for e in range(E)]
+        hsi = keep.tile([P, 4 * T], BF16, name="hsi", align_bytes=64)
         hc = keep.tile([P, T], U32, name="hc", align_bytes=64)
         hss = keep.tile([P, T], U8, name="hss", align_bytes=64)
+        rs = [keep.tile([P, 4 * P], F32, name=f"r{k}")[:] for k in range(12)]
 
-        def cast_pairs(j):
+        def gather(j, e):
             s, u = divmod(j, 2)
-            dst = pairs[:, j, :].rearrange("p (t d) -> p t d", d=2)
-            src = x[s][:, 2 * u : 2 * u + 2, :].rearrange("p d t -> p t d")
-            if j == 0:
-                nc.vector.tensor_copy(out=dst, in_=src)
+            nc.vector.tensor_copy(room[e, s][:, u, :], plane(j).bitcast(U32).indirect(offs_sb[:, e * C // 16 : (e + 1) * C // 16]))
+
+        def weave(e, s, on_vector=True):
+            if on_vector:
+                nc.vector.tensor_copy(
+                    out=woven[e, s].bitcast(I32).rearrange("p (c u) -> p c u", u=2),
+                    in_=room[e, s].bitcast(I32).rearrange("p u c -> p c u"),
+                )
             else:
-                nc.scalar.activation(dst, src, COPY)
+                nc.scalar.copy(woven[e, s].rearrange("p (c u) -> p c u", u=2), room[e, s].rearrange("p u c -> p c u"))
 
-        def new_gathered():
-            return work.tile([P, 2 * S, 2 * C], BF16, name="g", align_bytes=64, bufs=2)
-
-        def gather(e, g, j):
-            nc.vector.tensor_copy(
-                g[:, j, :].bitcast(U32),
-                pairs[:, j, :].bitcast(U32).indirect(offs_sb[:, e * C // 16 : (e + 1) * C // 16]),
-            )
-
-        def new_codes():
-            gi = work.tile([P, S, 4 * C], BF16, name="gi", align_bytes=64, bufs=1)
-            xc = work.tile([P, S, C], U32, name="xc", align_bytes=64)
-            xsc = work.tile([P, S, C], U8, name="xsc", align_bytes=64)
-            return gi, xc, xsc
-
-        def interleave_on_scalar(g, gi, s):
+        def weave_shared(s, t0=0, t1=T):
             nc.scalar.copy(
-                gi[:, s, :].rearrange("p (c u d) -> p c u d", u=2, d=2),
-                g[:, 2 * s : 2 * s + 2, :].rearrange("p u (c d) -> p c u d", d=2),
+                xs[:, 4 * (T * s + t0) : 4 * (T * s + t1)].bitcast(U32).rearrange("p (t u) -> p t u", u=2),
+                pairs[s][:].bitcast(U32).rearrange("p (u t) -> p t u", u=2)[:, t0:t1, :],
             )
 
-        def interleave(g, gi, s0, s1):
-            nc.vector.tensor_copy(
-                out=gi[:, s0:s1, :].bitcast(I32).rearrange("p s (c u) -> p s c u", u=2),
-                in_=g[:, 2 * s0 : 2 * s1, :].bitcast(I32).rearrange("p (s u) c -> p s c u", u=2),
-            )
-
-        def quantize(gi, xc, xsc, s0, s1):
+        def quant(e, s):
             nc.vector.quantize_mx(
-                out=xc[:, s0:s1, :].rearrange("p s c -> p (s c)").bitcast(FP8X4),
-                scales=xsc[:, s0:s1, :].rearrange("p s c -> p (s c)"),
-                in_=gi[:, s0:s1, :].rearrange("p s c -> p (s c)"),
+                out=xc[e][:, C * s : C * (s + 1)].bitcast(FP8X4),
+                scales=xsc[e][:, C * s : C * (s + 1)],
+                in_=woven[e, s].bitcast(BF16),
             )
 
-        def start1(k):
-            acc[k] = [pa.tile([P, H], F32, name="a") for m in range(2)]
-
-        def pass1(k, e, xc, xsc, c0, s, ms=(0, 1)):
-            for m in ms:
-                cols = slice(c0 + P * m, c0 + P * (m + 1))
+        def first(k, bank, passes=(0, 1)):
+            e = min(k // 2, E)
+            for s in passes:
+                if e < E:
+                    cols = slice(C * s + P * (k % 2), C * s + P * (k % 2 + 1))
+                    codes, scales = xc[e], xsc[e]
+                else:
+                    cols = slice(T * s + P * (k - 2 * E), T * s + P * (k - 2 * E + 1))
+                    codes, scales = sc, ss
                 nc.tensor.matmul_mx(
-                    out=acc[k][m][:],
-                    lhsT=xc[:, s, cols].bitcast(FP8X4),
-                    lhsT_scale=xsc[:, s, cols],
-                    rhs=w1[:, S * e + s, :].bitcast(FP4X4),
+                    out=bank[:],
+                    lhsT=codes[:, cols].bitcast(FP8X4),
+                    lhsT_scale=scales[:, cols],
+                    rhs=w1[e][:, s, :].bitcast(FP4X4),
                     rhs_scale=w1s[:, S * e + s, :],
                     start=(s == 0),
                     stop=(s == S - 1),
                 )
 
-        def relu(k, vector_tiles=()):
-            rs[k] = []
-            for m in range(2):
-                r = work.tile([P, 4, P], F32, name="r", bufs=8)
-                src = acc[k][m][:].rearrange("m (p t) -> m t p", t=4)
-                if m in vector_tiles:
-                    nc.vector.tensor_scalar(r[:], src, 0.0, None, mybir.AluOpType.max)
-                else:
-                    nc.scalar.activation(r[:], src, RELU)
-                rs[k].append(r)
+        def relu(k, bank, on_vector=False):
+            dst = rs[k].rearrange("m (t p) -> m t p", t=4)
+            src = bank[:].rearrange("m (p t) -> m t p", t=4)
+            if on_vector:
+                nc.vector.tensor_scalar(dst, src, 0.0, None, mybir.AluOpType.max)
+            else:
+                nc.scalar.activation(dst, src, RELU)
 
-        def first(k, e, xc, xsc, c0, vector_tiles=()):
-            start1(k)
-            for m in range(2):
-                for s in range(S):
-                    pass1(k, e, xc, xsc, c0, s, (m,))
-            relu(k, vector_tiles)
+        def turn(k, bank):
+            for q in range(4):
+                nc.tensor.transpose(bank[:, P * q : P * (q + 1)], rs[k][:, P * q : P * (q + 1)], ident[:])
 
-        def turn(k, hi):
-            for m in range(2):
-                tp = pt.tile([P, 4, P], F32, name="tp")
-                for q in range(4):
-                    nc.tensor.transpose(tp[:, q, :], rs[k][m][:, q, :], ident[:])
-                nc.scalar.activation(hi[:, m, :].rearrange("p (r t) -> p r t", t=4), tp[:].rearrange("p t r -> p r t"), SQUARE)
+        def square(k, bank):
+            if k < 2 * E:
+                dst = hi[k // 2][:, 4 * P * (k % 2) : 4 * P * (k % 2 + 1)]
+            else:
+                dst = hsi[:, 4 * P * (k - 2 * E) : 4 * P * (k - 2 * E + 1)]
+            nc.scalar.activation(dst.rearrange("p (r t) -> p r t", t=4), bank[:].rearrange("p (t r) -> p r t", t=4), SQUARE)
 
-        def quantize_h(hi, hq, hs):
-            nc.vector.quantize_mx(out=hq.bitcast(FP8X4), scales=hs, in_=hi.rearrange("p m c -> p (m c)"))
+        def hidden(e, c0=0, c1=C):
+            nc.vector.quantize_mx(out=hq[e][:, c0:c1].bitcast(FP8X4), scales=hs[e][:, c0:c1], in_=hi[e][:, 4 * c0 : 4 * c1])
 
-        def turned(e):
-            his[e] = work.tile([P, 2, 4 * P], BF16, name="hi", align_bytes=64)
-            turn(e, his[e][:])
-
-        def hidden(e):
-            hqs[e] = (work.tile([P, C], U32, name="hq", align_bytes=64, bufs=4), work.tile([P, C], U8, name="hs", align_bytes=64, bufs=4))
-            quantize_h(his[e][:], hqs[e][0][:], hqs[e][1][:])
-
-        def layer2(e, dst, n, hq, hs):
+        def second(e, dst, n, codes, scales):
             nc.tensor.matmul_mx(
                 out=dst,
                 lhsT=w2[:, e, 2 * P * n : 2 * P * (n + 1)].bitcast(FP4X4),
                 lhsT_scale=w2s[:, e, P * n : P * (n + 1)],
-                rhs=hq.bitcast(FP8X4),
-                rhs_scale=hs,
+                rhs=codes.bitcast(FP8X4),
+                rhs_scale=scales,
                 start=True,
                 stop=True,
             )
 
-        def results(e0, *ns):
-            for n in ns:
-                yp = py.tile([P, 2, C], F32, name="yp")
-                for e in range(e0, e0 + 2):
-                    layer2(e, yp[:, e - e0, :], n, hqs[e][0][:], hqs[e][1][:])
-                dst = y[n][:, e0 * C : (e0 + 2) * C]
-                src = yp[:].rearrange("p e c -> p (e c)")
-                if n == 0 or (e0, n) == (0, 1):
-                    nc.vector.tensor_copy(dst, src)
-                else:
-                    nc.scalar.copy(dst, src)
+        def two(e0, n, bank):
+            for e in (e0 + 1, e0):
+                second(e, bank[:, C * (e - e0) : C * (e - e0 + 1)], n, hq[e][:], hs[e][:])
 
-        acc, rs, his, hqs = {}, {}, {}, {}
-        g = [new_gathered() for e in range(2)]
-        codes = []
+        def fetch(e0, n, bank, on_vector=False, c0=0, c1=2 * C):
+            if on_vector:
+                nc.vector.tensor_copy(y[n][:, e0 * C + c0 : e0 * C + c1], bank[:, c0:c1])
+            else:
+                nc.scalar.copy(y[n][:, e0 * C + c0 : e0 * C + c1], bank[:, c0:c1])
 
-        def more():
-            g.append(new_gathered())
-
-        def gath(e, *js):
-            for j in js:
-                gather(e, g[e], j)
-
-        def inter(e, s0, s1):
-            if e == len(codes):
-                codes.append(new_codes())
-            interleave(g[e], codes[e][0], s0, s1)
-
-        def quant(e, s0, s1):
-            quantize(codes[e][0], codes[e][1], codes[e][2], s0, s1)
-
-        def routed(e, vector_tiles=()):
-            first(e, e, codes[e][1], codes[e][2], 0, vector_tiles)
-
-        for j in range(2 * S):
-            cast_pairs(j)
-        gath(0, 0)
-        gath(1, 0)
-        gath(0, 1)
-        gath(1, 1)
-        codes.append(new_codes())
-        interleave_on_scalar(g[0], codes[0][0], 0)
-        gath(0, 2, 3)
-        inter(0, 1, 2)
-        gath(1, 2, 3)
-        quant(0, 0, 1)
-        start1(0)
-        pass1(0, 0, codes[0][1], codes[0][2], 0, 0)
-        quant(0, 1, 2)
-        pass1(0, 0, codes[0][1], codes[0][2], 0, 1)
-        relu(0)
-        inter(1, 0, 2)
-        more()
-        gath(2, 0)
-        quant(1, 0, 2)
-        routed(1)
-        gath(2, 1, 2)
-        turned(0)
-        gath(2, 3)
-        inter(2, 0, 2)
-        more()
-        gath(3, 0)
-        quant(2, 0, 2)
-        routed(2)
-        gath(3, 1, 2)
-        inter(3, 0, 1)
-        gath(3, 3)
-        turned(1)
-        quant(3, 0, 1)
-        inter(3, 1, 2)
-        quant(3, 1, 2)
-        start1(3)
-        for s in range(S):
-            pass1(3, 3, codes[3][1], codes[3][2], 0, s)
-        relu(3)
+        cast(1, True)
+        for j in planes[1:]:
+            cast(j, False)
+        for j, e in ((1, 0), (1, 1), (1, 2), (0, 0), (0, 1)):
+            gather(j, e)
+        weave(0, 0)
+        gather(3, 0)
+        quant(0, 0)
+        first(0, A0, (0,))
+        first(1, A1, (0,))
+        gather(3, 1)
+        gather(2, 0)
+        gather(2, 1)
+        weave(1, 0, False)
+        weave_shared(0)
+        weave_shared(1)
+        quant(1, 0)
+        first(2, A2, (0,))
+        first(3, Y0, (0,))
+        weave(0, 1)
+        weave(1, 1)
+        quant(0, 1)
+        quant(1, 1)
+        for k, bank in enumerate((A0, A1, A2, Y0)):
+            first(k, bank, (1,))
+        gather(0, 2)
+        gather(3, 2)
+        weave(2, 0)
+        gather(2, 2)
+        gather(1, 3)
+        weave(2, 1)
+        quant(2, 0)
+        quant(2, 1)
+        gather(0, 3)
+        gather(3, 3)
+        gather(2, 3)
+        weave(3, 0)
+        weave(3, 1)
+        quant(3, 0)
+        quant(3, 1)
+        for k, (bank, turned) in enumerate(((A0, T0), (A1, T1), (A2, T2), (Y0, Y1))):
+            relu(k, bank)
+            turn(k, turned)
+        first(4, Y0)
+        square(0, T0)
+        first(5, T0)
+        square(1, T1)
+        square(2, T2)
+        square(3, Y1)
+        relu(4, Y0)
+        turn(4, A0)
+        relu(5, T0)
+        turn(5, A1)
+        first(6, T0)
+        square(4, A0)
+        first(7, A0)
+        square(5, A1)
         hidden(0)
         hidden(1)
-        xs = work.tile([P, S, 4 * T], BF16, name="gi", align_bytes=64, bufs=1)
-        sc = keep.tile([P, S, T], U32, name="sc", align_bytes=64)
-        ss = keep.tile([P, S, T], U8, name="ss", align_bytes=64)
         for s in range(S):
-            interleave(pairs, xs, s, s + 1)
-        for s in range(S):
-            nc.vector.quantize_mx(out=sc[:, s, :].bitcast(FP8X4), scales=ss[:, s, :], in_=xs[:, s, :])
-        for e in (2, 3):
-            turned(e)
-            hidden(e)
-        results(0, 0, 1)
-        results(2, 0, 1)
-        for half in range(2):
-            first(E + half, E, sc, ss, C * half)
-        hsi = keep.tile([P, 4, 4 * P], BF16, name="hsi", align_bytes=64)
-        for half in range(2):
-            turn(E + half, hsi[:, 2 * half : 2 * half + 2, :])
-        quantize_h(hsi[:], hc[:], hss[:])
-        results(0, 2)
-        results(2, 2)
+            nc.vector.quantize_mx(
+                out=sc[:, T * s : T * (s + 1)].bitcast(FP8X4), scales=ss[:, T * s : T * (s + 1)], in_=xs[:, 4 * T * s : 4 * T * (s + 1)]
+            )
+        relu(6, T0)
+        turn(6, A2)
+        relu(7, A0)
+        turn(7, T0)
+        two(0, 0, A1)
+        square(6, A2)
+        square(7, T0)
+        hidden(2)
+        hidden(3, 0, P)
+        second(3, T1[:, C : C + P], 0, hq[3][:, 0:P], hs[3][:, 0:P])
+        second(2, T1[:, 0:C], 0, hq[2][:], hs[2][:])
+        hidden(3, P, C)
+        second(3, T2[:, C + P : 2 * C], 0, hq[3][:, P:C], hs[3][:, P:C])
+        fetch(0, 0, A1, True)
+        fetch(2, 0, T1, True, 0, C + P)
+        fetch(2, 0, T2, True, C + P, 2 * C)
+        first(8, A0)
+        two(0, 1, A1)
+        fetch(0, 1, A1)
+        relu(8, A0)
+        two(0, 2, A2)
+        two(2, 1, Y0)
+        two(2, 2, Y1)
+        first(9, A0)
+        turn(8, T1)
+        first(10, A1)
+        fetch(0, 2, A2)
+        relu(9, A0)
+        fetch(2, 1, Y0)
+        turn(9, T2)
+        first(11, A0)
+        fetch(2, 2, Y1)
+        relu(10, A1)
+        turn(10, T0)
+        square(8, T1)
+        relu(11, A0)
+        turn(11, T1)
+        square(9, T2)
+        square(10, T0)
+        square(11, T1)
 
-        t1, t2 = [], []
-        for n in range(NC):
-            for r, ts in enumerate((t1, t2)):
-                t = keep.tile([P, T], F32, name=f"t{r}{n}")
-                nc.vector.tensor_tensor(t[:], y[n][:].indirect(pos_sb[r][:]), gt[:, r, n, :], MULT)
-                ts.append(t)
-        ysp = []
-        for n in range(NC):
-            ysp.append(pa.tile([P, T], F32, name="a"))
-            layer2(E, ysp[n][:], n, hc[:], hss[:])
-        t3 = [keep.tile([P, T], F32, name=f"t3{n}") for n in range(NC)]
+        t = [[keep.tile([P, T], F32, name=f"t{r}{n}")[:] for r in range(2)] for n in range(NC)]
+        t[2] = [hsi[:, 2 * T * r : 2 * T * (r + 1)].bitcast(F32) for r in range(2)]
+        both = [keep.tile([P, T], F32, name=f"both{n}") for n in range(NC)]
         o = [keep.tile([P, T], F32, name=f"o{n}") for n in range(NC)]
+        ysp = [Y0, Y1, A2]
 
-        def plus_shared(n):
-            nc.vector.tensor_tensor(t3[n][:], t1[n][:], ysp[n][:], ADD)
+        def back(n, r):
+            nc.vector.tensor_tensor(t[n][r], y[n][:].indirect(pos_sb[r][:]), gt[:, r, :], MULT)
 
-        def finish(n, c0, c1, engine):
-            engine.tensor_tensor(o[n][:, c0:c1], t2[n][:, c0:c1], t3[n][:, c0:c1], ADD)
+        def store(n, c0, c1):
             nc.sync.dma_start(out=out[P * n : P * (n + 1), c0:c1], in_=o[n][:, c0:c1])
 
-        plus_shared(0)
-        finish(0, 0, T, nc.gpsimd)
-        plus_shared(1)
-        plus_shared(2)
-        finish(1, 0, T, nc.vector)
-        finish(2, 0, T // 2, nc.vector)
-        finish(2, T // 2, T, nc.vector)
+        back(0, 0)
+        back(0, 1)
+        back(1, 0)
+        back(1, 1)
+        nc.vector.tensor_tensor(both[0][:], t[0][0], t[0][1], ADD)
+        nc.vector.tensor_tensor(both[1][:], t[1][0], t[1][1], ADD)
+        nc.vector.quantize_mx(out=hc[:].bitcast(FP8X4), scales=hss[:], in_=hsi[:])
+        for n in range(NC):
+            second(E, ysp[n][:], n, hc[:], hss[:])
+        back(2, 0)
+        nc.vector.tensor_tensor(o[0][:], both[0][:], ysp[0][:], ADD)
+        store(0, 0, T)
+        nc.vector.tensor_tensor(o[1][:], both[1][:], ysp[1][:], ADD)
+        store(1, 0, T)
+        nc.vector.tensor_tensor(both[2][:], t[2][0], ysp[2][:], ADD)
+        for c0 in (0, T // 2):
+            nc.vector.tensor_tensor(
+                t[2][1][:, c0 : c0 + T // 2], y[2][:].indirect(pos_sb[1][:, c0 // 16 : (c0 + T // 2) // 16]), gt[:, 1, c0 : c0 + T // 2], MULT
+            )
+        for c0 in (0, T // 2):
+            nc.vector.tensor_tensor(o[2][:, c0 : c0 + T // 2], both[2][:, c0 : c0 + T // 2], t[2][1][:, c0 : c0 + T // 2], ADD)
+            store(2, c0, c0 + T // 2)

@@ -180,6 +180,17 @@ def tile_moe_shr_mlp_relu2_kernel(
                     stop=(s == S - 1),
                 )
 
+        def keep_warm(bank):
+            nc.tensor.matmul_mx(
+                out=bank[:],
+                lhsT=xc[0][:, 0:P].bitcast(FP8X4),
+                lhsT_scale=xsc[0][:, 0:P],
+                rhs=w1[0][:, 0, :].bitcast(FP4X4),
+                rhs_scale=w1s[:, 0, :],
+                start=True,
+                stop=True,
+            )
+
         def relu(k, bank, on_vector=False):
             dst = rs[k].rearrange("m (t p) -> m t p", t=4)
             src = bank[:].rearrange("m (p t) -> m t p", t=4)
@@ -233,6 +244,8 @@ def tile_moe_shr_mlp_relu2_kernel(
         quant(0, 0)
         first(0, A0, (0,))
         first(1, A1, (0,))
+        keep_warm(T0)
+        keep_warm(T1)
         gather(3, 1)
         gather(2, 0)
         gather(2, 1)
@@ -252,9 +265,9 @@ def tile_moe_shr_mlp_relu2_kernel(
         gather(3, 2)
         weave(2, 0)
         gather(2, 2)
-        gather(1, 3)
-        weave(2, 1)
         quant(2, 0)
+        weave(2, 1)
+        gather(1, 3)
         quant(2, 1)
         gather(0, 3)
         gather(3, 3)
@@ -263,20 +276,30 @@ def tile_moe_shr_mlp_relu2_kernel(
         weave(3, 1)
         quant(3, 0)
         quant(3, 1)
-        for k, (bank, turned) in enumerate(((A0, T0), (A1, T1), (A2, T2), (Y0, Y1))):
-            relu(k, bank)
-            turn(k, turned)
-        first(4, Y0)
+        relu(0, A0)
+        turn(0, T0)
+        keep_warm(A0)
+        relu(1, A1)
+        turn(1, T1)
+        first(4, A1, (0,))
+        relu(2, A2)
+        turn(2, T2)
+        first(5, A2, (0,))
+        relu(3, Y0)
+        turn(3, Y1)
+        first(4, A1, (1,))
+        first(5, A2, (1,))
         square(0, T0)
-        first(5, T0)
         square(1, T1)
+        keep_warm(T1)
         square(2, T2)
+        keep_warm(T2)
         square(3, Y1)
-        relu(4, Y0)
+        relu(4, A1)
         turn(4, A0)
-        relu(5, T0)
+        relu(5, A2)
         turn(5, A1)
-        first(6, T0)
+        first(6, A2)
         square(4, A0)
         first(7, A0)
         square(5, A1)
@@ -286,7 +309,7 @@ def tile_moe_shr_mlp_relu2_kernel(
             nc.vector.quantize_mx(
                 out=sc[:, T * s : T * (s + 1)].bitcast(FP8X4), scales=ss[:, T * s : T * (s + 1)], in_=xs[:, 4 * T * s : 4 * T * (s + 1)]
             )
-        relu(6, T0)
+        relu(6, A2)
         turn(6, A2)
         relu(7, A0)
         turn(7, T0)

@@ -134,6 +134,7 @@ def tile_moe_shr_mlp_relu2_kernel(
         hc = keep.tile([P, T], U32, name="hc", align_bytes=64)
         hss = keep.tile([P, T], U8, name="hss", align_bytes=64)
         rs = [keep.tile([P, 4 * P], F32, name=f"r{k}")[:] for k in range(12)]
+        rs[8] = rs[7]
 
         def gather(j, e):
             s, u = divmod(j, 2)
@@ -282,26 +283,26 @@ def tile_moe_shr_mlp_relu2_kernel(
         relu(1, A1)
         turn(1, T1)
         first(4, A1, (0,))
+        first(5, A0, (0,))
         relu(2, A2)
         turn(2, T2)
-        first(5, A2, (0,))
         relu(3, Y0)
         turn(3, Y1)
         first(4, A1, (1,))
-        first(5, A2, (1,))
+        first(5, A0, (1,))
         square(0, T0)
         square(1, T1)
         keep_warm(T1)
         square(2, T2)
         keep_warm(T2)
-        square(3, Y1)
         relu(4, A1)
-        turn(4, A0)
-        relu(5, A2)
+        turn(4, A2)
+        relu(5, A0)
         turn(5, A1)
-        first(6, A2)
-        square(4, A0)
-        first(7, A0)
+        first(6, A0)
+        square(3, Y1)
+        square(4, A2)
+        first(7, A2)
         square(5, A1)
         hidden(0)
         hidden(1)
@@ -309,12 +310,13 @@ def tile_moe_shr_mlp_relu2_kernel(
             nc.vector.quantize_mx(
                 out=sc[:, T * s : T * (s + 1)].bitcast(FP8X4), scales=ss[:, T * s : T * (s + 1)], in_=xs[:, 4 * T * s : 4 * T * (s + 1)]
             )
-        relu(6, A2)
-        turn(6, A2)
-        relu(7, A0)
+        relu(6, A0)
+        turn(6, Y0)
+        first(8, A0)
+        relu(7, A2)
         turn(7, T0)
         two(0, 0, A1)
-        square(6, A2)
+        square(6, Y0)
         square(7, T0)
         hidden(2)
         hidden(3, 0, P)
@@ -325,36 +327,45 @@ def tile_moe_shr_mlp_relu2_kernel(
         fetch(0, 0, A1, True)
         fetch(2, 0, T1, True, 0, C + P)
         fetch(2, 0, T2, True, C + P, 2 * C)
-        first(8, A0)
         two(0, 1, A1)
-        fetch(0, 1, A1)
+        fetch(0, 1, A1, True)
+        first(9, A2)
+        first(10, Y0)
         relu(8, A0)
-        two(0, 2, A2)
-        two(2, 1, Y0)
-        two(2, 2, Y1)
-        first(9, A0)
-        turn(8, T1)
-        first(10, A1)
-        fetch(0, 2, A2)
-        relu(9, A0)
-        fetch(2, 1, Y0)
-        turn(9, T2)
+        two(2, 1, T0)
         first(11, A0)
-        fetch(2, 2, Y1)
-        relu(10, A1)
-        turn(10, T0)
-        square(8, T1)
+        relu(9, A2)
+        turn(8, Y1)
+        turn(9, T1)
+        relu(10, Y0)
+        turn(10, T2)
+        fetch(2, 1, T0)
         relu(11, A0)
-        turn(11, T1)
-        square(9, T2)
-        square(10, T0)
-        square(11, T1)
+        turn(11, A2)
+        two(0, 2, Y0)
+        two(2, 2, A0)
+        square(8, Y1)
+        square(9, T1)
+        square(10, T2)
+        square(11, A2)
+        fetch(0, 2, Y0)
+        fetch(2, 2, A0)
 
         t = [[keep.tile([P, T], F32, name=f"t{r}{n}")[:] for r in range(2)] for n in range(NC)]
-        t[2] = [hsi[:, 2 * T * r : 2 * T * (r + 1)].bitcast(F32) for r in range(2)]
+        t[1][1], t[2][0] = [hsi[:, 2 * T * r : 2 * T * (r + 1)].bitcast(F32) for r in range(2)]
+        t[2][1] = t[1][0]
         both = [keep.tile([P, T], F32, name=f"both{n}") for n in range(NC)]
         o = [keep.tile([P, T], F32, name=f"o{n}") for n in range(NC)]
-        ysp = [Y0, Y1, A2]
+        ysp = [T0, A1, T1]
+        turned = keep.tile([P, T], F32, name="turned")
+        ys_turned = keep.tile([P, T], F32, name="ys_turned")
+
+        def turn_sum(bank, first_blocks, second_blocks):
+            for q in range(4):
+                dst = bank[:, P * q : P * (q + 1)]
+                nc.tensor.matmul(dst, first_blocks[:, P * q : P * (q + 1)], ident[:], start=True, stop=False, is_transpose=True)
+                nc.tensor.matmul(dst, second_blocks[:, P * q : P * (q + 1)], ident[:], start=False, stop=True, is_transpose=True)
+
 
         def back(n, r):
             nc.vector.tensor_tensor(t[n][r], y[n][:].indirect(pos_sb[r][:]), gt[:, r, :], MULT)
@@ -364,19 +375,32 @@ def tile_moe_shr_mlp_relu2_kernel(
 
         back(0, 0)
         back(0, 1)
+        turn_sum(Y1, t[0][1], t[0][0])
+        nc.scalar.copy(turned[:], Y1[:])
         back(1, 0)
-        back(1, 1)
-        nc.vector.tensor_tensor(both[0][:], t[0][0], t[0][1], ADD)
-        nc.vector.tensor_tensor(both[1][:], t[1][0], t[1][1], ADD)
         nc.vector.quantize_mx(out=hc[:].bitcast(FP8X4), scales=hss[:], in_=hsi[:])
-        for n in range(NC):
+        for q in range(4):
+            nc.tensor.matmul_mx(
+                out=ysp[0][:, P * q : P * (q + 1)],
+                lhsT=hc[:, P * q : P * (q + 1)].bitcast(FP8X4),
+                lhsT_scale=hss[:, P * q : P * (q + 1)],
+                rhs=w2[:, E, 0 : 2 * P].bitcast(FP4X4),
+                rhs_scale=w2s[:, E, 0:P],
+                start=True,
+                stop=True,
+            )
+        for n in (1, 2):
             second(E, ysp[n][:], n, hc[:], hss[:])
-        back(2, 0)
-        nc.vector.tensor_tensor(o[0][:], both[0][:], ysp[0][:], ADD)
+        nc.scalar.copy(ys_turned[:], ysp[0][:])
+        turn_sum(Y1, ys_turned[:], turned[:])
+        nc.scalar.copy(o[0][:], Y1[:])
         store(0, 0, T)
+        back(1, 1)
+        back(2, 0)
+        nc.vector.tensor_tensor(both[1][:], t[1][0], t[1][1], ADD)
+        nc.vector.tensor_tensor(both[2][:], t[2][0], ysp[2][:], ADD)
         nc.vector.tensor_tensor(o[1][:], both[1][:], ysp[1][:], ADD)
         store(1, 0, T)
-        nc.vector.tensor_tensor(both[2][:], t[2][0], ysp[2][:], ADD)
         for c0 in (0, T // 2):
             nc.vector.tensor_tensor(
                 t[2][1][:, c0 : c0 + T // 2], y[2][:].indirect(pos_sb[1][:, c0 // 16 : (c0 + T // 2) // 16]), gt[:, 1, c0 : c0 + T // 2], MULT

@@ -324,17 +324,17 @@ def tile_moe_shr_mlp_relu2_kernel(
         second(2, T1[:, 0:C], 0, hq[2][:], hs[2][:])
         hidden(3, P, C)
         second(3, T2[:, C + P : 2 * C], 0, hq[3][:, P:C], hs[3][:, P:C])
-        fetch(0, 0, A1, True)
+        fetch(0, 0, A1)
         fetch(2, 0, T1, True, 0, C + P)
         fetch(2, 0, T2, True, C + P, 2 * C)
-        two(0, 1, A1)
-        fetch(0, 1, A1, True)
         first(9, A2)
+        two(0, 1, A1)
         first(10, Y0)
         relu(8, A0)
         two(2, 1, T0)
         first(11, A0)
         relu(9, A2)
+        fetch(0, 1, A1)
         turn(8, Y1)
         turn(9, T1)
         relu(10, Y0)
@@ -352,9 +352,9 @@ def tile_moe_shr_mlp_relu2_kernel(
         fetch(2, 2, A0)
 
         t = [[keep.tile([P, T], F32, name=f"t{r}{n}")[:] for r in range(2)] for n in range(NC)]
-        t[1][1], t[2][0] = [hsi[:, 2 * T * r : 2 * T * (r + 1)].bitcast(F32) for r in range(2)]
-        t[2][1] = t[1][0]
+        t[2] = [hsi[:, 0 : 2 * T].bitcast(F32), t[1][0]]
         both = [keep.tile([P, T], F32, name=f"both{n}") for n in range(NC)]
+        both[1] = hsi[:, 2 * T : 4 * T].bitcast(F32)
         o = [keep.tile([P, T], F32, name=f"o{n}") for n in range(NC)]
         ysp = [T0, A1, T1]
         turned = keep.tile([P, T], F32, name="turned")
@@ -377,7 +377,10 @@ def tile_moe_shr_mlp_relu2_kernel(
         back(0, 1)
         turn_sum(Y1, t[0][1], t[0][0])
         nc.scalar.copy(turned[:], Y1[:])
+        keep_warm(A2)
+        keep_warm(A2)
         back(1, 0)
+        back(1, 1)
         nc.vector.quantize_mx(out=hc[:].bitcast(FP8X4), scales=hss[:], in_=hsi[:])
         for q in range(4):
             nc.tensor.matmul_mx(
@@ -394,13 +397,12 @@ def tile_moe_shr_mlp_relu2_kernel(
         nc.scalar.copy(ys_turned[:], ysp[0][:])
         turn_sum(Y1, ys_turned[:], turned[:])
         nc.scalar.copy(o[0][:], Y1[:])
-        store(0, 0, T)
-        back(1, 1)
+        nc.scalar.dma_start(out=out[0:P, :], in_=o[0][:])
+        nc.vector.tensor_tensor(both[1], t[1][0], t[1][1], ADD)
         back(2, 0)
-        nc.vector.tensor_tensor(both[1][:], t[1][0], t[1][1], ADD)
-        nc.vector.tensor_tensor(both[2][:], t[2][0], ysp[2][:], ADD)
-        nc.vector.tensor_tensor(o[1][:], both[1][:], ysp[1][:], ADD)
+        nc.vector.tensor_tensor(o[1][:], both[1], ysp[1][:], ADD)
         store(1, 0, T)
+        nc.vector.tensor_tensor(both[2][:], t[2][0], ysp[2][:], ADD)
         for c0 in (0, T // 2):
             nc.vector.tensor_tensor(
                 t[2][1][:, c0 : c0 + T // 2], y[2][:].indirect(pos_sb[1][:, c0 // 16 : (c0 + T // 2) // 16]), gt[:, 1, c0 : c0 + T // 2], MULT

@@ -21,8 +21,16 @@ MULT = mybir.AluOpType.mult
 ADD = mybir.AluOpType.add
 
 P = 128
-S = K // 512
-NC = N // P
+D = 4
+PASSES = K // (P * D)
+BLOCKS = N // P
+SHARED = E
+ROUTED_TILES = E * C // P
+TILES = ROUTED_TILES + T // P
+PER_COLUMN = 16
+BANK = 512
+HALF = T // 2
+PLANES = (1, 0, 3, 2)
 
 
 def tile_moe_shr_mlp_relu2_kernel(
@@ -32,381 +40,344 @@ def tile_moe_shr_mlp_relu2_kernel(
     with ExitStack() as ctx:
         keep = ctx.enter_context(tc.tile_pool(name="keep", bufs=1))
         psum = ctx.enter_context(tc.psum_pool(name="psum", bufs=1))
-        A0, A1, A2, T0, T1, T2, Y0, Y1 = [psum.tile([P, 512], F32, name=f"bank{b}") for b in range(8)]
+        b0, b1, b2, b3, b4, b5, b6, b7 = [psum.tile([P, BANK], F32, name=f"bank{b}") for b in range(8)]
 
-        offs_sb = keep.tile([P, E * C // 16], U16, name="offs_sb")
-        pos_sb = [keep.tile([P, T // 16], U16, name=f"pos_sb{r}") for r in range(2)]
+        def sbuf(name, columns, dtype):
+            return keep.tile([P, columns], dtype, name=name, align_bytes=64)[:]
+
+        pieces = {j: 2 if j in (PLANES[0], PLANES[-1]) else 1 for j in PLANES}
+        offs_sb = keep.tile([P, E * C // PER_COLUMN], U16, name="offs_sb")
+        pos_sb = [keep.tile([P, T // PER_COLUMN], U16, name=f"pos_sb{r}") for r in range(2)]
         ident = keep.tile([P, P], F32, name="ident")
-        planes = [1, 0, 3, 2]
-        cuts = {j: 2 if j in (planes[0], planes[-1]) else 1 for j in planes}
-        x = [[keep.tile([P, 2, T // cuts[j]], F32, name=f"x{j}{h}") for h in range(cuts[j])] for j in range(2 * S)]
-        pairs = [keep.tile([P, 4 * T], BF16, name=f"pairs{s}", align_bytes=64) for s in range(S)]
-        w1 = [keep.tile([P, S, 2 * H], U8, name=f"w1_{e}", align_bytes=64) for e in range(E + 1)]
-        w1s = keep.tile([P, (E + 1) * S, H], U8, name="w1s", align_bytes=64)
+        x = {j: [keep.tile([P, 2, T // pieces[j]], F32, name=f"x{j}{h}") for h in range(pieces[j])] for j in PLANES}
+        w1 = [keep.tile([P, PASSES, 2 * H], U8, name=f"w1_{e}", align_bytes=64) for e in range(E + 1)]
+        w1_sc = keep.tile([P, (E + 1) * PASSES, H], U8, name="w1_sc", align_bytes=64)
         w2 = keep.tile([P, E + 1, 2 * N], U8, name="w2", align_bytes=64)
-        w2s = keep.tile([P, E + 1, N], U8, name="w2s", align_bytes=64)
-        gt = keep.tile([P, 2, T], F32, name="gt")
-        y = [keep.tile([P, E * C], F32, name=f"y{c}") for c in range(NC)]
-        warm = keep.tile([P, 1], F32, name="warm")
+        w2_sc = keep.tile([P, E + 1, N], U8, name="w2_sc", align_bytes=64)
+        gates = keep.tile([P, 2, T], F32, name="gates")
+        table_load = keep.tile([P, 1], F32, name="table_load")
 
-        nc.vector.memset(warm[:], 0.0)
-        nc.scalar.activation(warm[:], warm[:], RELU)
-        nc.vector.memset(w1s[:].bitcast(I32), 0)
-        nc.vector.memset(w2s[:].bitcast(I32), 0)
+        pairs = [sbuf(f"pairs{s}", 2 * 2 * T, BF16) for s in range(PASSES)]
+        room_a, room_b, room_c = [sbuf(f"room_{n}", 2 * C, U32) for n in "abc"]
+        strip_a, strip_b = sbuf("strip_a", 3 * C, U32), sbuf("strip_b", 4 * C, U32)
+        woven = {(e, s): sbuf(f"woven{e}{s}", 2 * C, U32) for e, s in ((0, 0), (1, 0), (3, 0), (2, 1), (3, 1))}
+        woven[0, 1] = strip_a[:, 0 : 2 * C]
+        woven[2, 0] = strip_b[:, 0 : 2 * C]
+        woven[1, 1] = strip_b[:, 2 * C : 4 * C]
+        room = {
+            (0, 0): room_a,
+            (1, 0): room_b,
+            (2, 0): strip_a[:, C : 3 * C],
+            (3, 0): strip_b[:, C : 3 * C],
+            (0, 1): room_c,
+            (1, 1): room_a,
+            (2, 1): room_c,
+            (3, 1): room_c,
+        }
+        shared_woven = sbuf("shared_woven", PASSES * D * T, BF16)
+        shared_codes = sbuf("shared_codes", PASSES * T, U32)
+        shared_sc = sbuf("shared_sc", PASSES * T, U8)
+        x_codes = {e: sbuf(f"x_codes{e}", PASSES * C, U32) for e in (0, 1, 3)}
+        x_codes[2] = shared_codes[:, T - C : T + C]
+        x_sc = [sbuf(f"x_sc{e}", PASSES * C, U8) for e in range(E)]
+
+        relued = [sbuf(f"relued{k}", H, F32) for k in range(TILES - 1)]
+        relued.insert(ROUTED_TILES, relued[ROUTED_TILES - 1])
+        hidden = [sbuf(f"hidden{e}", D * C, BF16) for e in range(E)] + [sbuf("hidden_shared", D * T, BF16)]
+        h_codes = [sbuf(f"h_codes{e}", C, U32) for e in range(E)] + [sbuf("h_codes_shared", T, U32)]
+        h_sc = [sbuf(f"h_sc{e}", C, U8) for e in range(E)] + [sbuf("h_sc_shared", T, U8)]
+
+        y = [keep.tile([P, E * C], F32, name=f"y{n}") for n in range(BLOCKS)]
+        gated = [[sbuf(f"gated{n}{r}", T, F32) for r in range(2)] for n in range(2)]
+        gated.append([hidden[SHARED][:, 0 : 2 * T].bitcast(F32), gated[1][0]])
+        routed_sum1 = hidden[SHARED][:, 2 * T : 4 * T].bitcast(F32)
+        part_sum2 = sbuf("part_sum2", T, F32)
+        routed_sum0_turned = sbuf("routed_sum0_turned", T, F32)
+        shared_out0_turned = sbuf("shared_out0_turned", T, F32)
+        result = [sbuf(f"result{n}", T, F32) for n in range(BLOCKS)]
+
+        nc.vector.memset(table_load[:], 0.0)
+        nc.scalar.activation(table_load[:], table_load[:], RELU)
+        nc.vector.memset(w1_sc[:].bitcast(I32), 0)
+        nc.vector.memset(w2_sc[:].bitcast(I32), 0)
         make_identity(nc, ident[:])
 
-        xv = xT.rearrange("(s p d) t -> s p d t", s=S, d=4)
-        for j in planes:
+        x_rows = xT.rearrange("(s p d) t -> s p d t", s=PASSES, d=D)
+        for j in PLANES:
             s, u = divmod(j, 2)
-            width = T // cuts[j]
-            for h in range(cuts[j]):
-                nc.sync.dma_start(out=x[j][h][:], in_=xv[s, :, 2 * u : 2 * u + 2, width * h : width * (h + 1)])
-            if j == planes[0]:
+            width = T // pieces[j]
+            for h in range(pieces[j]):
+                nc.sync.dma_start(out=x[j][h][:], in_=x_rows[s, :, 2 * u : 2 * u + 2, width * h : width * (h + 1)])
+            if j == PLANES[0]:
                 nc.sync.dma_start(offs_sb[:], offs)
-        sv1 = w1_scales.rearrange("e s (q r) i -> q r (e s) i", q=4)
-        sv2 = w2_scales.rearrange("e s (q r) i -> q r (e s) i", q=4)
 
-        def load_w1(e):
+        def load_words(e):
             nc.sync.dma_start(out=w1[e][:].bitcast(I32), in_=w1_words[e].rearrange("s p b -> p s b").bitcast(I32))
 
-        def load_w1_scales(e0, e1):
+        def load_scales(dst, scales, first, last):
+            rows = scales.rearrange("e s (q r) i -> q r (e s) i", q=4)
             for q in range(4):
-                nc.sync.dma_start(
-                    out=w1s[32 * q : 32 * q + 4, S * e0 : S * e1, :].bitcast(I32), in_=sv1[q, :, S * e0 : S * e1, :].bitcast(I32)
-                )
+                nc.sync.dma_start(out=dst[32 * q : 32 * q + 4, first:last, :].bitcast(I32), in_=rows[q, :, first:last, :].bitcast(I32))
 
-        load_w1(0)
-        load_w1_scales(0, 2)
-        load_w1(1)
-        load_w1_scales(2, E + 1)
+        load_words(0)
+        load_scales(w1_sc, w1_scales, 0, 2 * PASSES)
+        load_words(1)
+        load_scales(w1_sc, w1_scales, 2 * PASSES, (E + 1) * PASSES)
         for e in range(2, E):
-            load_w1(e)
-        for q in range(4):
-            nc.sync.dma_start(out=w2s[32 * q : 32 * q + 4, :, :].bitcast(I32), in_=sv2[q].bitcast(I32))
+            load_words(e)
+        load_scales(w2_sc, w2_scales, 0, E + 1)
         nc.sync.dma_start(out=w2[:].bitcast(I32), in_=w2_words.rearrange("e s p b -> p (e s) b").bitcast(I32))
-        load_w1(E)
-        for r, lst in enumerate((pos1, pos2)):
-            nc.sync.dma_start(pos_sb[r][:], lst)
-        nc.sync.dma_start(out=gt[:], in_=gate[:, 0:P, :].rearrange("g p t -> p g t"))
+        load_words(SHARED)
+        for r, positions in enumerate((pos1, pos2)):
+            nc.sync.dma_start(pos_sb[r][:], positions)
+        nc.sync.dma_start(out=gates[:], in_=gate[:, 0:P, :].rearrange("g p t -> p g t"))
 
         def plane(j):
             s, u = divmod(j, 2)
             return pairs[s][:, 2 * T * u : 2 * T * (u + 1)]
 
-        def cast(j, on_vector):
-            width = 2 * T // cuts[j]
-            for h in range(cuts[j]):
-                dst = plane(j)[:, width * h : width * (h + 1)].rearrange("p (t d) -> p t d", d=2)
-                src = x[j][h][:].rearrange("p d t -> p t d")
-                if on_vector:
-                    nc.vector.tensor_copy(out=dst, in_=src)
-                else:
-                    nc.scalar.activation(dst, src, COPY)
-
-        ga = keep.tile([P, 2 * C], U32, name="ga")
-        gc = keep.tile([P, 2 * C], U32, name="gc")
-        gd = keep.tile([P, 2 * C], U32, name="gd")
-        ring0 = keep.tile([P, 3 * C], U32, name="ring0", align_bytes=64)
-        gi = {(e, s): keep.tile([P, 2 * C], U32, name=f"gi{e}{s}", align_bytes=64)[:] for e in range(E) for s in range(S) if (e, s) not in ((0, 1), (1, 1), (2, 0))}
-        ring1 = keep.tile([P, 4 * C], U32, name="ring1", align_bytes=64)
-
-        def halves(ap):
-            return ap.rearrange("p (u c) -> p u c", u=2)
-
-        room = {
-            (0, 0): halves(ga[:]), (1, 0): halves(gc[:]), (2, 0): halves(ring0[:, C : 3 * C]), (3, 0): halves(ring1[:, C : 3 * C]),
-            (0, 1): halves(gd[:]), (1, 1): halves(ga[:]), (2, 1): halves(gd[:]), (3, 1): halves(gd[:]),
-        }
-        woven = dict(gi)
-        woven[0, 1] = ring0[:, 0 : 2 * C]
-        woven[2, 0] = ring1[:, 0 : 2 * C]
-        woven[1, 1] = ring1[:, 2 * C : 4 * C]
-        xc = [keep.tile([P, S * C], U32, name=f"xc{e}", align_bytes=64)[:] for e in (0, 1, 3)]
-        xsc = [keep.tile([P, S * C], U8, name=f"xsc{e}", align_bytes=64) for e in range(E)]
-        xs = keep.tile([P, S * 4 * T], BF16, name="xs", align_bytes=64)
-        sc = keep.tile([P, S * T], U32, name="sc", align_bytes=64)
-        ss = keep.tile([P, S * T], U8, name="ss", align_bytes=64)
-        hi = [keep.tile([P, 4 * C], BF16, name=f"hi{e}", align_bytes=64)[:] for e in range(E)]
-        xc.insert(2, sc[:, T - C : T + C])
-        hq = [keep.tile([P, C], U32, name=f"hq{e}", align_bytes=64) for e in range(E)]
-        hs = [keep.tile([P, C], U8, name=f"hs{e}", align_bytes=64) for e in range(E)]
-        hsi = keep.tile([P, 4 * T], BF16, name="hsi", align_bytes=64)
-        hc = keep.tile([P, T], U32, name="hc", align_bytes=64)
-        hss = keep.tile([P, T], U8, name="hss", align_bytes=64)
-        rs = [keep.tile([P, 4 * P], F32, name=f"r{k}")[:] for k in range(12)]
-        rs[8] = rs[7]
+        def cast_views(j):
+            width = 2 * T // pieces[j]
+            return [
+                (plane(j)[:, width * h : width * (h + 1)].rearrange("p (t d) -> p t d", d=2), x[j][h][:].rearrange("p d t -> p t d"))
+                for h in range(pieces[j])
+            ]
 
         def gather(j, e):
             s, u = divmod(j, 2)
-            nc.vector.tensor_copy(room[e, s][:, u, :], plane(j).bitcast(U32).indirect(offs_sb[:, e * C // 16 : (e + 1) * C // 16]))
+            slots = offs_sb[:, e * C // PER_COLUMN : (e + 1) * C // PER_COLUMN]
+            nc.vector.tensor_copy(room[e, s][:, C * u : C * (u + 1)], plane(j).bitcast(U32).indirect(slots))
 
-        def weave(e, s, on_vector=True):
-            if on_vector:
-                nc.vector.tensor_copy(
-                    out=woven[e, s].bitcast(I32).rearrange("p (c u) -> p c u", u=2),
-                    in_=room[e, s].bitcast(I32).rearrange("p u c -> p c u"),
-                )
-            else:
-                nc.scalar.copy(woven[e, s].rearrange("p (c u) -> p c u", u=2), room[e, s].rearrange("p u c -> p c u"))
+        def weave_views(dst, src, dtype):
+            return dst.bitcast(dtype).rearrange("p (c u) -> p c u", u=2), src.bitcast(dtype).rearrange("p (u c) -> p c u", u=2)
 
-        def weave_shared(s, t0=0, t1=T):
-            nc.scalar.copy(
-                xs[:, 4 * (T * s + t0) : 4 * (T * s + t1)].bitcast(U32).rearrange("p (t u) -> p t u", u=2),
-                pairs[s][:].bitcast(U32).rearrange("p (u t) -> p t u", u=2)[:, t0:t1, :],
-            )
+        def weave(e, s):
+            nc.vector.tensor_copy(*weave_views(woven[e, s], room[e, s], I32))
 
-        def quant(e, s):
-            nc.vector.quantize_mx(
-                out=xc[e][:, C * s : C * (s + 1)].bitcast(FP8X4),
-                scales=xsc[e][:, C * s : C * (s + 1)],
-                in_=woven[e, s].bitcast(BF16),
-            )
+        def quantise(codes, scales, values):
+            nc.vector.quantize_mx(out=codes.bitcast(FP8X4), scales=scales, in_=values)
 
-        def first(k, bank, passes=(0, 1)):
-            e = min(k // 2, E)
-            for s in passes:
-                if e < E:
-                    cols = slice(C * s + P * (k % 2), C * s + P * (k % 2 + 1))
-                    codes, scales = xc[e], xsc[e]
-                else:
-                    cols = slice(T * s + P * (k - 2 * E), T * s + P * (k - 2 * E + 1))
-                    codes, scales = sc, ss
-                nc.tensor.matmul_mx(
-                    out=bank[:],
-                    lhsT=codes[:, cols].bitcast(FP8X4),
-                    lhsT_scale=scales[:, cols],
-                    rhs=w1[e][:, s, :].bitcast(FP4X4),
-                    rhs_scale=w1s[:, S * e + s, :],
-                    start=(s == 0),
-                    stop=(s == S - 1),
-                )
+        def quantise_slots(e, s):
+            quantise(x_codes[e][:, C * s : C * (s + 1)], x_sc[e][:, C * s : C * (s + 1)], woven[e, s].bitcast(BF16))
 
-        def keep_warm(bank):
+        def quantise_hidden(e, first, last):
+            quantise(h_codes[e][:, first:last], h_sc[e][:, first:last], hidden[e][:, D * first : D * last])
+
+        def expert_and_column(k):
+            return divmod(P * k, C) if k < ROUTED_TILES else (SHARED, P * (k - ROUTED_TILES))
+
+        def first_pass(k, s, bank, start, stop):
+            e, column = expert_and_column(k)
+            codes, scales, width = (x_codes[e], x_sc[e], C) if e < E else (shared_codes, shared_sc, T)
+            columns = slice(width * s + column, width * s + column + P)
             nc.tensor.matmul_mx(
                 out=bank[:],
-                lhsT=xc[0][:, 0:P].bitcast(FP8X4),
-                lhsT_scale=xsc[0][:, 0:P],
-                rhs=w1[0][:, 0, :].bitcast(FP4X4),
-                rhs_scale=w1s[:, 0, :],
-                start=True,
-                stop=True,
+                lhsT=codes[:, columns].bitcast(FP8X4),
+                lhsT_scale=scales[:, columns],
+                rhs=w1[e][:, s, :].bitcast(FP4X4),
+                rhs_scale=w1_sc[:, PASSES * e + s, :],
+                start=start,
+                stop=stop,
             )
 
-        def relu(k, bank, on_vector=False):
-            dst = rs[k].rearrange("m (t p) -> m t p", t=4)
-            src = bank[:].rearrange("m (p t) -> m t p", t=4)
-            if on_vector:
-                nc.vector.tensor_scalar(dst, src, 0.0, None, mybir.AluOpType.max)
-            else:
-                nc.scalar.activation(dst, src, RELU)
+        def first_product(k, bank, passes=range(PASSES)):
+            for s in passes:
+                first_pass(k, s, bank, start=(s == 0), stop=(s == PASSES - 1))
+
+        def keep_warm(bank):
+            first_pass(0, 0, bank, start=True, stop=True)
+
+        def relu(k, bank):
+            nc.scalar.activation(relued[k].rearrange("m (d p) -> m d p", d=D), bank[:].rearrange("m (p d) -> m d p", d=D), RELU)
 
         def turn(k, bank):
-            for q in range(4):
-                nc.tensor.transpose(bank[:, P * q : P * (q + 1)], rs[k][:, P * q : P * (q + 1)], ident[:])
+            for d in range(D):
+                nc.tensor.transpose(bank[:, P * d : P * (d + 1)], relued[k][:, P * d : P * (d + 1)], ident[:])
 
         def square(k, bank):
-            if k < 2 * E:
-                dst = hi[k // 2][:, 4 * P * (k % 2) : 4 * P * (k % 2 + 1)]
-            else:
-                dst = hsi[:, 4 * P * (k - 2 * E) : 4 * P * (k - 2 * E + 1)]
-            nc.scalar.activation(dst.rearrange("p (r t) -> p r t", t=4), bank[:].rearrange("p (t r) -> p r t", t=4), SQUARE)
+            e, column = expert_and_column(k)
+            dst = hidden[e][:, D * column : D * (column + P)]
+            nc.scalar.activation(dst.rearrange("p (m d) -> p m d", d=D), bank[:].rearrange("p (d m) -> p m d", d=D), SQUARE)
 
-        def hidden(e, c0=0, c1=C):
-            nc.vector.quantize_mx(out=hq[e][:, c0:c1].bitcast(FP8X4), scales=hs[e][:, c0:c1], in_=hi[e][:, 4 * c0 : 4 * c1])
-
-        def second(e, dst, n, codes, scales):
+        def second_product(e, n, dst, first, last):
             nc.tensor.matmul_mx(
                 out=dst,
                 lhsT=w2[:, e, 2 * P * n : 2 * P * (n + 1)].bitcast(FP4X4),
-                lhsT_scale=w2s[:, e, P * n : P * (n + 1)],
-                rhs=codes.bitcast(FP8X4),
-                rhs_scale=scales,
+                lhsT_scale=w2_sc[:, e, P * n : P * (n + 1)],
+                rhs=h_codes[e][:, first:last].bitcast(FP8X4),
+                rhs_scale=h_sc[e][:, first:last],
                 start=True,
                 stop=True,
             )
 
-        def two(e0, n, bank):
-            for e in (e0 + 1, e0):
-                second(e, bank[:, C * (e - e0) : C * (e - e0 + 1)], n, hq[e][:], hs[e][:])
+        def second_pair(e, n, bank):
+            second_product(e + 1, n, bank[:, C : 2 * C], 0, C)
+            second_product(e, n, bank[:, 0:C], 0, C)
 
-        def fetch(e0, n, bank, on_vector=False, c0=0, c1=2 * C):
-            if on_vector:
-                nc.vector.tensor_copy(y[n][:, e0 * C + c0 : e0 * C + c1], bank[:, c0:c1])
-            else:
-                nc.scalar.copy(y[n][:, e0 * C + c0 : e0 * C + c1], bank[:, c0:c1])
+        def fetch_pair(e, n, bank):
+            nc.scalar.copy(y[n][:, e * C : (e + 2) * C], bank[:])
 
-        cast(1, True)
-        for j in planes[1:]:
-            cast(j, False)
-        for j, e in ((1, 0), (1, 1), (1, 2), (0, 0), (0, 1)):
-            gather(j, e)
+        def gather_back(n, r, first, last):
+            positions = pos_sb[r][:, first // PER_COLUMN : last // PER_COLUMN]
+            nc.vector.tensor_tensor(gated[n][r][:, first:last], y[n][:].indirect(positions), gates[:, r, first:last], MULT)
+
+        def turn_and_add(bank, later, earlier):
+            for c in range(0, T, P):
+                nc.tensor.matmul(bank[:, c : c + P], later[:, c : c + P], ident[:], start=True, stop=False, is_transpose=True)
+                nc.tensor.matmul(bank[:, c : c + P], earlier[:, c : c + P], ident[:], start=False, stop=True, is_transpose=True)
+
+        def add(dst, left, right):
+            nc.vector.tensor_tensor(dst, left, right, ADD)
+
+        for dst, src in cast_views(PLANES[0]):
+            nc.vector.tensor_copy(out=dst, in_=src)
+        for j in PLANES[1:]:
+            for dst, src in cast_views(j):
+                nc.scalar.activation(dst, src, COPY)
+        for e in range(3):
+            gather(1, e)
+        for e in range(2):
+            gather(0, e)
         weave(0, 0)
         gather(3, 0)
-        quant(0, 0)
-        first(0, A0, (0,))
-        first(1, A1, (0,))
-        keep_warm(T0)
-        keep_warm(T1)
+        quantise_slots(0, 0)
+        first_product(0, b0, [0])
+        first_product(1, b1, [0])
+        for bank in (b3, b4, b5):
+            keep_warm(bank)
         gather(3, 1)
-        gather(2, 0)
-        gather(2, 1)
-        weave(1, 0, False)
-        weave_shared(0)
-        weave_shared(1)
-        quant(1, 0)
-        first(2, A2, (0,))
-        first(3, Y0, (0,))
-        weave(0, 1)
-        weave(1, 1)
-        quant(0, 1)
-        quant(1, 1)
-        for k, bank in enumerate((A0, A1, A2, Y0)):
-            first(k, bank, (1,))
+        for e in range(2):
+            gather(2, e)
+        nc.scalar.copy(*weave_views(woven[1, 0], room[1, 0], U32))
+        for s in range(PASSES):
+            nc.scalar.copy(*weave_views(shared_woven[:, D * T * s : D * T * (s + 1)], pairs[s], U32))
+        quantise_slots(1, 0)
+        first_product(2, b2, [0])
+        first_product(3, b6, [0])
+        for e in range(2):
+            weave(e, 1)
+        for e in range(2):
+            quantise_slots(e, 1)
+        for k, bank in enumerate((b0, b1, b2, b6)):
+            first_product(k, bank, [1])
         gather(0, 2)
         gather(3, 2)
         weave(2, 0)
         gather(2, 2)
-        quant(2, 0)
+        quantise_slots(2, 0)
         weave(2, 1)
         gather(1, 3)
-        quant(2, 1)
-        gather(0, 3)
-        gather(3, 3)
-        gather(2, 3)
-        weave(3, 0)
-        weave(3, 1)
-        quant(3, 0)
-        quant(3, 1)
-        relu(0, A0)
-        turn(0, T0)
-        keep_warm(A0)
-        relu(1, A1)
-        turn(1, T1)
-        first(4, A1, (0,))
-        first(5, A0, (0,))
-        relu(2, A2)
-        turn(2, T2)
-        relu(3, Y0)
-        turn(3, Y1)
-        first(4, A1, (1,))
-        first(5, A0, (1,))
-        square(0, T0)
-        square(1, T1)
-        keep_warm(T1)
-        square(2, T2)
-        keep_warm(T2)
-        relu(4, A1)
-        turn(4, A2)
-        relu(5, A0)
-        turn(5, A1)
-        first(6, A0)
-        square(3, Y1)
-        square(4, A2)
-        first(7, A2)
-        square(5, A1)
-        hidden(0)
-        hidden(1)
-        for s in range(S):
-            nc.vector.quantize_mx(
-                out=sc[:, T * s : T * (s + 1)].bitcast(FP8X4), scales=ss[:, T * s : T * (s + 1)], in_=xs[:, 4 * T * s : 4 * T * (s + 1)]
-            )
-        relu(6, A0)
-        turn(6, Y0)
-        first(8, A0)
-        relu(7, A2)
-        turn(7, T0)
-        two(0, 0, A1)
-        square(6, Y0)
-        square(7, T0)
-        hidden(2)
-        hidden(3, 0, P)
-        second(3, T1[:, C : C + P], 0, hq[3][:, 0:P], hs[3][:, 0:P])
-        second(2, T1[:, 0:C], 0, hq[2][:], hs[2][:])
-        hidden(3, P, C)
-        second(3, T2[:, C + P : 2 * C], 0, hq[3][:, P:C], hs[3][:, P:C])
-        fetch(0, 0, A1)
-        fetch(2, 0, T1, True, 0, C + P)
-        fetch(2, 0, T2, True, C + P, 2 * C)
-        first(9, A2)
-        two(0, 1, A1)
-        first(10, Y0)
-        relu(8, A0)
-        two(2, 1, T0)
-        first(11, A0)
-        relu(9, A2)
-        fetch(0, 1, A1)
-        turn(8, Y1)
-        turn(9, T1)
-        relu(10, Y0)
-        turn(10, T2)
-        fetch(2, 1, T0)
-        relu(11, A0)
-        turn(11, A2)
-        two(0, 2, Y0)
-        two(2, 2, A0)
-        square(8, Y1)
-        square(9, T1)
-        square(10, T2)
-        square(11, A2)
-        fetch(0, 2, Y0)
-        fetch(2, 2, A0)
+        quantise_slots(2, 1)
+        for j in (0, 3, 2):
+            gather(j, 3)
+        for s in range(PASSES):
+            weave(3, s)
+        for s in range(PASSES):
+            quantise_slots(3, s)
 
-        t = [[keep.tile([P, T], F32, name=f"t{r}{n}")[:] for r in range(2)] for n in range(NC)]
-        t[2] = [hsi[:, 0 : 2 * T].bitcast(F32), t[1][0]]
-        both = [keep.tile([P, T], F32, name=f"both{n}") for n in range(NC)]
-        both[1] = hsi[:, 2 * T : 4 * T].bitcast(F32)
-        o = [keep.tile([P, T], F32, name=f"o{n}") for n in range(NC)]
-        ysp = [T0, A1, T1]
-        turned = keep.tile([P, T], F32, name="turned")
-        ys_turned = keep.tile([P, T], F32, name="ys_turned")
+        relu(0, b0)
+        turn(0, b3)
+        keep_warm(b0)
+        relu(1, b1)
+        turn(1, b4)
+        first_product(4, b1, [0])
+        first_product(5, b0, [0])
+        relu(2, b2)
+        turn(2, b5)
+        relu(3, b6)
+        turn(3, b7)
+        first_product(4, b1, [1])
+        first_product(5, b0, [1])
+        square(0, b3)
+        square(1, b4)
+        keep_warm(b4)
+        square(2, b5)
+        keep_warm(b5)
+        relu(4, b1)
+        turn(4, b2)
+        relu(5, b0)
+        turn(5, b1)
+        first_product(6, b0)
+        square(3, b7)
+        square(4, b2)
+        first_product(7, b2)
+        square(5, b1)
+        for e in range(2):
+            quantise_hidden(e, 0, C)
+        for s in range(PASSES):
+            tokens = slice(T * s, T * (s + 1))
+            quantise(shared_codes[:, tokens], shared_sc[:, tokens], shared_woven[:, D * T * s : D * T * (s + 1)])
+        relu(6, b0)
+        turn(6, b6)
+        first_product(8, b0)
+        relu(7, b2)
+        turn(7, b3)
+        second_pair(0, 0, b1)
+        square(6, b6)
+        square(7, b3)
 
-        def turn_sum(bank, first_blocks, second_blocks):
-            for q in range(4):
-                dst = bank[:, P * q : P * (q + 1)]
-                nc.tensor.matmul(dst, first_blocks[:, P * q : P * (q + 1)], ident[:], start=True, stop=False, is_transpose=True)
-                nc.tensor.matmul(dst, second_blocks[:, P * q : P * (q + 1)], ident[:], start=False, stop=True, is_transpose=True)
+        quantise_hidden(2, 0, C)
+        quantise_hidden(3, 0, P)
+        second_product(3, 0, b4[:, C : C + P], 0, P)
+        second_product(2, 0, b4[:, 0:C], 0, C)
+        quantise_hidden(3, P, C)
+        second_product(3, 0, b5[:, C + P : 2 * C], P, C)
+        fetch_pair(0, 0, b1)
+        nc.vector.tensor_copy(y[0][:, 2 * C : 3 * C + P], b4[:, 0 : C + P])
+        nc.vector.tensor_copy(y[0][:, 3 * C + P : 4 * C], b5[:, C + P : 2 * C])
 
+        first_product(9, b2)
+        second_pair(0, 1, b1)
+        first_product(10, b6)
+        relu(8, b0)
+        second_pair(2, 1, b3)
+        first_product(11, b0)
+        relu(9, b2)
+        fetch_pair(0, 1, b1)
+        turn(8, b7)
+        turn(9, b4)
+        relu(10, b6)
+        turn(10, b5)
+        fetch_pair(2, 1, b3)
+        relu(11, b0)
+        turn(11, b2)
+        second_pair(0, 2, b6)
+        second_pair(2, 2, b0)
+        for k, bank in zip(range(ROUTED_TILES, TILES), (b7, b4, b5, b2)):
+            square(k, bank)
+        fetch_pair(0, 2, b6)
+        fetch_pair(2, 2, b0)
 
-        def back(n, r):
-            nc.vector.tensor_tensor(t[n][r], y[n][:].indirect(pos_sb[r][:]), gt[:, r, :], MULT)
-
-        def store(n, c0, c1):
-            nc.sync.dma_start(out=out[P * n : P * (n + 1), c0:c1], in_=o[n][:, c0:c1])
-
-        back(0, 0)
-        back(0, 1)
-        turn_sum(Y1, t[0][1], t[0][0])
-        nc.scalar.copy(turned[:], Y1[:])
-        keep_warm(A2)
-        keep_warm(A2)
-        back(1, 0)
-        back(1, 1)
-        nc.vector.quantize_mx(out=hc[:].bitcast(FP8X4), scales=hss[:], in_=hsi[:])
-        for q in range(4):
+        for r in range(2):
+            gather_back(0, r, 0, T)
+        turn_and_add(b7, gated[0][1], gated[0][0])
+        nc.scalar.copy(routed_sum0_turned, b7[:])
+        for r in range(2):
+            gather_back(1, r, 0, T)
+        quantise_hidden(SHARED, 0, T)
+        for c in range(0, T, P):
             nc.tensor.matmul_mx(
-                out=ysp[0][:, P * q : P * (q + 1)],
-                lhsT=hc[:, P * q : P * (q + 1)].bitcast(FP8X4),
-                lhsT_scale=hss[:, P * q : P * (q + 1)],
-                rhs=w2[:, E, 0 : 2 * P].bitcast(FP4X4),
-                rhs_scale=w2s[:, E, 0:P],
+                out=b3[:, c : c + P],
+                lhsT=h_codes[SHARED][:, c : c + P].bitcast(FP8X4),
+                lhsT_scale=h_sc[SHARED][:, c : c + P],
+                rhs=w2[:, SHARED, 0 : 2 * P].bitcast(FP4X4),
+                rhs_scale=w2_sc[:, SHARED, 0:P],
                 start=True,
                 stop=True,
             )
-        for n in (1, 2):
-            second(E, ysp[n][:], n, hc[:], hss[:])
-        nc.scalar.copy(ys_turned[:], ysp[0][:])
-        turn_sum(Y1, ys_turned[:], turned[:])
-        nc.scalar.copy(o[0][:], Y1[:])
-        nc.scalar.dma_start(out=out[0:P, :], in_=o[0][:])
-        nc.vector.tensor_tensor(both[1], t[1][0], t[1][1], ADD)
-        back(2, 0)
-        nc.vector.tensor_tensor(o[1][:], both[1], ysp[1][:], ADD)
-        store(1, 0, T)
-        nc.vector.tensor_tensor(both[2][:], t[2][0], ysp[2][:], ADD)
-        for c0 in (0, T // 2):
-            nc.vector.tensor_tensor(
-                t[2][1][:, c0 : c0 + T // 2], y[2][:].indirect(pos_sb[1][:, c0 // 16 : (c0 + T // 2) // 16]), gt[:, 1, c0 : c0 + T // 2], MULT
-            )
-        for c0 in (0, T // 2):
-            nc.vector.tensor_tensor(o[2][:, c0 : c0 + T // 2], both[2][:, c0 : c0 + T // 2], t[2][1][:, c0 : c0 + T // 2], ADD)
-            store(2, c0, c0 + T // 2)
+        second_product(SHARED, 1, b1[:], 0, T)
+        second_product(SHARED, 2, b4[:], 0, T)
+        nc.scalar.copy(shared_out0_turned, b3[:])
+        turn_and_add(b7, shared_out0_turned, routed_sum0_turned)
+        nc.scalar.copy(result[0], b7[:])
+        nc.scalar.dma_start(out=out[0:P, :], in_=result[0])
+        add(routed_sum1, gated[1][0], gated[1][1])
+        gather_back(2, 0, 0, T)
+        add(result[1], routed_sum1, b1[:])
+        nc.sync.dma_start(out=out[P : 2 * P, :], in_=result[1])
+        add(part_sum2, gated[2][0], b4[:])
+        for c in (0, HALF):
+            gather_back(2, 1, c, c + HALF)
+        for c in (0, HALF):
+            add(result[2][:, c : c + HALF], part_sum2[:, c : c + HALF], gated[2][1][:, c : c + HALF])
+            nc.sync.dma_start(out=out[2 * P : 3 * P, c : c + HALF], in_=result[2][:, c : c + HALF])

@@ -49,7 +49,7 @@ def tile_moe_shr_mlp_relu2_kernel(
         offs_sb = keep.tile([P, E * C // PER_COLUMN], U16, name="offs_sb")
         pos_sb = [keep.tile([P, T // PER_COLUMN], U16, name=f"pos_sb{r}") for r in range(2)]
         ident = keep.tile([P, P], F32, name="ident")
-        x = {j: [keep.tile([P, 2, T // pieces[j]], F32, name=f"x{j}{h}") for h in range(pieces[j])] for j in PLANES}
+        x = {j: [keep.tile([P, 2, T // pieces[j]], F32, name=f"x{j}{h}", tag=f"x{j}{h}", align_bytes=64) for h in range(pieces[j])] for j in PLANES}
         w1 = [keep.tile([P, PASSES, 2 * H], U8, name=f"w1_{e}", align_bytes=64) for e in range(E + 1)]
         w1_sc = keep.tile([P, (E + 1) * PASSES, H], U8, name="w1_sc", align_bytes=64)
         w2 = keep.tile([P, E + 1, 2 * N], U8, name="w2", align_bytes=64)
@@ -58,42 +58,43 @@ def tile_moe_shr_mlp_relu2_kernel(
         table_load = keep.tile([P, 1], F32, name="table_load")
 
         pairs = [sbuf(f"pairs{s}", 2 * 2 * T, BF16) for s in range(PASSES)]
-        room_a, room_b, room_c = [sbuf(f"room_{n}", 2 * C, U32) for n in "abc"]
-        strip_a, strip_b = sbuf("strip_a", 3 * C, U32), sbuf("strip_b", 4 * C, U32)
-        woven = {(e, s): sbuf(f"woven{e}{s}", 2 * C, U32) for e, s in ((0, 0), (1, 0), (3, 0), (2, 1), (3, 1))}
-        woven[0, 1] = strip_a[:, 0 : 2 * C]
-        woven[2, 0] = strip_b[:, 0 : 2 * C]
-        woven[1, 1] = strip_b[:, 2 * C : 4 * C]
+        relued = {k: sbuf(f"relued{k}", H, F32) for k in range(TILES) if k not in (0, 2)}
+        for k in (0, 2):
+            relued[k] = keep.tile([P, H], F32, name=f"relued{k}", tag=f"relued{k}", align_bytes=64)[:]
+        strip = sbuf("strip", 7 * C, U32)
+        woven = {(e, s): sbuf(f"woven{e}{s}", 2 * C, U32) for e, s in ((0, 0), (1, 0), (0, 1), (2, 0), (3, 0))}
+        woven[1, 1] = sbuf("woven11", 2 * C, U32)
+        woven[2, 1] = strip[:, 3 * C : 5 * C]
+        woven[3, 1] = relued[3].bitcast(U32)
         room = {
-            (0, 0): room_a,
-            (1, 0): room_b,
-            (2, 0): strip_a[:, C : 3 * C],
-            (3, 0): strip_b[:, C : 3 * C],
-            (0, 1): room_c,
-            (1, 1): room_a,
-            (2, 1): room_c,
-            (3, 1): room_c,
+            (0, 0): sbuf("first_room", 2 * C, U32),
+            (1, 0): strip[:, 0 : 2 * C],
+            (1, 1): strip[:, 0 : 2 * C],
+            (0, 1): strip[:, 2 * C : 4 * C],
+            (2, 0): strip[:, 3 * C : 5 * C],
+            (3, 0): strip[:, C : 3 * C],
+            (2, 1): woven[1, 1],
+            (3, 1): strip[:, C : 3 * C],
         }
-        shared_woven = sbuf("shared_woven", PASSES * D * T, BF16)
         shared_codes = sbuf("shared_codes", PASSES * T, U32)
         shared_sc = sbuf("shared_sc", PASSES * T, U8)
-        x_codes = {e: sbuf(f"x_codes{e}", PASSES * C, U32) for e in (0, 1, 3)}
-        x_codes[2] = shared_codes[:, T - C : T + C]
-        x_sc = [sbuf(f"x_sc{e}", PASSES * C, U8) for e in range(E)]
+        x_codes = {(e, s): sbuf(f"x_codes{e}{s}", C, U32) for e in range(E) for s in range(PASSES) if (e, s) not in ((2, 1), (3, 1))}
+        x_codes[2, 1] = shared_codes[:, 0:C]
+        x_codes[3, 1] = shared_codes[:, T : T + C]
+        x_sc = {(e, s): sbuf(f"x_sc{e}{s}", C, U8) for e in range(E) for s in range(PASSES) if (e, s) not in ((0, 0), (2, 0), (2, 1))}
+        x_sc[0, 0] = keep.tile([P, C], U8, name="x_sc00", tag="x30", align_bytes=64)[:]
 
-        relued = [sbuf(f"relued{k}", H, F32) for k in range(TILES - 1)]
-        relued.insert(ROUTED_TILES, relued[ROUTED_TILES - 1])
         hidden = [sbuf(f"hidden{e}", D * C, BF16) for e in range(E)] + [sbuf("hidden_shared", D * T, BF16)]
+        shared_woven = [sbuf(f"shared_woven{s}", D * T, BF16) for s in range(PASSES)]
         h_codes = [sbuf(f"h_codes{e}", C, U32) for e in range(E)] + [sbuf("h_codes_shared", T, U32)]
         h_sc = [sbuf(f"h_sc{e}", C, U8) for e in range(E)] + [sbuf("h_sc_shared", T, U8)]
 
         y = [keep.tile([P, E * C], F32, name=f"y{n}") for n in range(BLOCKS)]
-        gated = [[sbuf(f"gated{n}{r}", T, F32) for r in range(2)] for n in range(2)]
-        gated.append([hidden[SHARED][:, 0 : 2 * T].bitcast(F32), gated[1][0]])
-        routed_sum1 = hidden[SHARED][:, 2 * T : 4 * T].bitcast(F32)
+        gated = [[sbuf(f"gated{n}{r}", T, F32) for r in range(2)] for n in range(BLOCKS)]
         part_sum2 = sbuf("part_sum2", T, F32)
-        routed_sum0_turned = sbuf("routed_sum0_turned", T, F32)
-        shared_out0_turned = sbuf("shared_out0_turned", T, F32)
+        routed_sum1 = hidden[SHARED][:, 0 : 2 * T].bitcast(F32)
+        routed_turned = [sbuf(f"routed_turned{n}", T, F32) for n in range(2)]
+        shared_turned = [sbuf(f"shared_turned{n}", T, F32) for n in range(2)]
         result = [sbuf(f"result{n}", T, F32) for n in range(BLOCKS)]
 
         nc.vector.memset(table_load[:], 0.0)
@@ -158,7 +159,11 @@ def tile_moe_shr_mlp_relu2_kernel(
             nc.vector.quantize_mx(out=codes.bitcast(FP8X4), scales=scales, in_=values)
 
         def quantise_slots(e, s):
-            quantise(x_codes[e][:, C * s : C * (s + 1)], x_sc[e][:, C * s : C * (s + 1)], woven[e, s].bitcast(BF16))
+            quantise(x_codes[e, s], x_sc[e, s], woven[e, s].bitcast(BF16))
+
+        def quantise_shared(s):
+            tokens = slice(T * s, T * (s + 1))
+            quantise(shared_codes[:, tokens], shared_sc[:, tokens], shared_woven[s])
 
         def quantise_hidden(e, first, last):
             quantise(h_codes[e][:, first:last], h_sc[e][:, first:last], hidden[e][:, D * first : D * last])
@@ -168,8 +173,8 @@ def tile_moe_shr_mlp_relu2_kernel(
 
         def first_pass(k, s, bank, start, stop):
             e, column = expert_and_column(k)
-            codes, scales, width = (x_codes[e], x_sc[e], C) if e < E else (shared_codes, shared_sc, T)
-            columns = slice(width * s + column, width * s + column + P)
+            codes, scales, first = (x_codes[e, s], x_sc[e, s], column) if e < E else (shared_codes, shared_sc, T * s + column)
+            columns = slice(first, first + P)
             nc.tensor.matmul_mx(
                 out=bank[:],
                 lhsT=codes[:, columns].bitcast(FP8X4),
@@ -189,6 +194,12 @@ def tile_moe_shr_mlp_relu2_kernel(
 
         def relu(k, bank):
             nc.scalar.activation(relued[k].rearrange("m (d p) -> m d p", d=D), bank[:].rearrange("m (p d) -> m d p", d=D), RELU)
+
+        def relu_on_vector(k, bank):
+            nc.vector.tensor_scalar_max(relued[k].rearrange("m (d p) -> m d p", d=D), bank[:].rearrange("m (p d) -> m d p", d=D), 0.0)
+
+        def weave_on_scalar(e, s):
+            nc.scalar.copy(*weave_views(woven[e, s], room[e, s], U32))
 
         def turn(k, bank):
             for d in range(D):
@@ -217,14 +228,26 @@ def tile_moe_shr_mlp_relu2_kernel(
         def fetch_pair(e, n, bank):
             nc.scalar.copy(y[n][:, e * C : (e + 2) * C], bank[:])
 
-        def gather_back(n, r, first, last):
+        def gather_back(dst, n, r, first, last):
             positions = pos_sb[r][:, first // PER_COLUMN : last // PER_COLUMN]
-            nc.vector.tensor_tensor(gated[n][r][:, first:last], y[n][:].indirect(positions), gates[:, r, first:last], MULT)
+            nc.vector.tensor_tensor(dst, y[n][:].indirect(positions), gates[:, r, first:last], MULT)
 
-        def turn_and_add(bank, later, earlier):
-            for c in range(0, T, P):
+        def turn_and_add(bank, later, earlier, width):
+            for c in range(0, width, P):
                 nc.tensor.matmul(bank[:, c : c + P], later[:, c : c + P], ident[:], start=True, stop=False, is_transpose=True)
                 nc.tensor.matmul(bank[:, c : c + P], earlier[:, c : c + P], ident[:], start=False, stop=True, is_transpose=True)
+
+        def shared_turned_product(n, bank):
+            for c in range(0, T, P):
+                nc.tensor.matmul_mx(
+                    out=bank[:, c : c + P],
+                    lhsT=h_codes[SHARED][:, c : c + P].bitcast(FP8X4),
+                    lhsT_scale=h_sc[SHARED][:, c : c + P],
+                    rhs=w2[:, SHARED, 2 * P * n : 2 * P * (n + 1)].bitcast(FP4X4),
+                    rhs_scale=w2_sc[:, SHARED, P * n : P * (n + 1)],
+                    start=True,
+                    stop=True,
+                )
 
         def add(dst, left, right):
             nc.vector.tensor_tensor(dst, left, right, ADD)
@@ -243,141 +266,127 @@ def tile_moe_shr_mlp_relu2_kernel(
         quantise_slots(0, 0)
         first_product(0, b0, [0])
         first_product(1, b1, [0])
-        for bank in (b3, b4, b5):
-            keep_warm(bank)
+        keep_warm(b3)
+        weave_on_scalar(1, 0)
+        nc.scalar.copy(*weave_views(shared_woven[0], pairs[0], U32))
+        gather(2, 0)
+        weave_on_scalar(0, 1)
+        nc.scalar.copy(*weave_views(shared_woven[1], pairs[1], U32))
         gather(3, 1)
-        for e in range(2):
-            gather(2, e)
-        nc.scalar.copy(*weave_views(woven[1, 0], room[1, 0], U32))
-        for s in range(PASSES):
-            nc.scalar.copy(*weave_views(shared_woven[:, D * T * s : D * T * (s + 1)], pairs[s], U32))
         quantise_slots(1, 0)
         first_product(2, b2, [0])
         first_product(3, b6, [0])
-        for e in range(2):
-            weave(e, 1)
-        for e in range(2):
-            quantise_slots(e, 1)
-        for k, bank in enumerate((b0, b1, b2, b6)):
-            first_product(k, bank, [1])
+        gather(2, 1)
+        weave_on_scalar(1, 1)
+        quantise_slots(0, 1)
+        first_product(0, b0, [1])
+        first_product(1, b1, [1])
         gather(0, 2)
-        gather(3, 2)
-        weave(2, 0)
-        gather(2, 2)
-        quantise_slots(2, 0)
-        weave(2, 1)
         gather(1, 3)
-        quantise_slots(2, 1)
-        for j in (0, 3, 2):
-            gather(j, 3)
-        for s in range(PASSES):
-            weave(3, s)
-        for s in range(PASSES):
-            quantise_slots(3, s)
-
+        quantise_slots(1, 1)
+        gather(0, 3)
         relu(0, b0)
         turn(0, b3)
-        keep_warm(b0)
+        first_product(2, b2, [1])
+        first_product(3, b6, [1])
         relu(1, b1)
         turn(1, b4)
-        first_product(4, b1, [0])
-        first_product(5, b0, [0])
+        weave_on_scalar(2, 0)
+        weave_on_scalar(3, 0)
+        gather(3, 2)
+        gather(2, 2)
+        x_sc[2, 0] = keep.tile([P, C], U8, name="x_sc20", tag="relued0", align_bytes=64)[:]
+        quantise_slots(2, 0)
+        quantise_slots(3, 0)
+        first_product(4, b0, [0])
+        first_product(5, b1, [0])
         relu(2, b2)
         turn(2, b5)
         relu(3, b6)
         turn(3, b7)
-        first_product(4, b1, [1])
-        first_product(5, b0, [1])
+        first_product(6, b6, [0])
         square(0, b3)
+        first_product(7, b3, [0])
+        gather(3, 3)
+        weave(2, 1)
+        gather(2, 3)
+        x_sc[2, 1] = keep.tile([P, C], U8, name="x_sc21", tag="relued2", align_bytes=64)[:]
+        quantise_slots(2, 1)
+        weave(3, 1)
         square(1, b4)
-        keep_warm(b4)
+        quantise_hidden(0, 0, C)
+        quantise_slots(3, 1)
         square(2, b5)
-        keep_warm(b5)
-        relu(4, b1)
-        turn(4, b2)
-        relu(5, b0)
-        turn(5, b1)
-        first_product(6, b0)
         square(3, b7)
-        square(4, b2)
-        first_product(7, b2)
-        square(5, b1)
-        for e in range(2):
-            quantise_hidden(e, 0, C)
-        for s in range(PASSES):
-            tokens = slice(T * s, T * (s + 1))
-            quantise(shared_codes[:, tokens], shared_sc[:, tokens], shared_woven[:, D * T * s : D * T * (s + 1)])
-        relu(6, b0)
-        turn(6, b6)
+        for k, bank in ((4, b0), (5, b1), (6, b6), (7, b3)):
+            first_product(k, bank, [1])
+        relu(4, b0)
+        turn(4, b2)
+        relu(5, b1)
+        turn(5, b4)
+        quantise_shared(0)
+        relu_on_vector(6, b6)
+        quantise_hidden(1, 0, C)
+        turn(6, b5)
+        second_pair(0, 0, b6)
+        relu(7, b3)
+        turn(7, b7)
+        second_pair(0, 1, b3)
+        quantise_shared(1)
         first_product(8, b0)
-        relu(7, b2)
-        turn(7, b3)
-        second_pair(0, 0, b1)
-        square(6, b6)
-        square(7, b3)
-
+        first_product(9, b1)
+        nc.vector.tensor_copy(y[0][:, 0 : 2 * C], b6[:])
+        for k, bank in ((4, b2), (5, b4), (6, b5), (7, b7)):
+            square(k, bank)
         quantise_hidden(2, 0, C)
         quantise_hidden(3, 0, P)
-        second_product(3, 0, b4[:, C : C + P], 0, P)
-        second_product(2, 0, b4[:, 0:C], 0, C)
+        second_product(2, 0, b2[:, 0:C], 0, C)
+        second_product(3, 0, b2[:, C : C + P], 0, P)
         quantise_hidden(3, P, C)
-        second_product(3, 0, b5[:, C + P : 2 * C], P, C)
-        fetch_pair(0, 0, b1)
-        nc.vector.tensor_copy(y[0][:, 2 * C : 3 * C + P], b4[:, 0 : C + P])
-        nc.vector.tensor_copy(y[0][:, 3 * C + P : 4 * C], b5[:, C + P : 2 * C])
-
-        first_product(9, b2)
-        second_pair(0, 1, b1)
-        first_product(10, b6)
+        second_product(3, 0, b4[:, C + P : 2 * C], P, C)
+        nc.vector.tensor_copy(y[0][:, 2 * C : 3 * C + P], b2[:, 0 : C + P])
+        nc.vector.tensor_copy(y[0][:, 3 * C + P : 4 * C], b4[:, C + P : 2 * C])
         relu(8, b0)
-        second_pair(2, 1, b3)
-        first_product(11, b0)
-        relu(9, b2)
-        fetch_pair(0, 1, b1)
-        turn(8, b7)
-        turn(9, b4)
-        relu(10, b6)
-        turn(10, b5)
-        fetch_pair(2, 1, b3)
-        relu(11, b0)
-        turn(11, b2)
-        second_pair(0, 2, b6)
-        second_pair(2, 2, b0)
-        for k, bank in zip(range(ROUTED_TILES, TILES), (b7, b4, b5, b2)):
+        first_product(10, b0)
+        relu(9, b1)
+        first_product(11, b1)
+        second_pair(2, 1, b6)
+        turn(8, b5)
+        turn(9, b7)
+        fetch_pair(0, 1, b3)
+        second_pair(0, 2, b3)
+        relu(10, b0)
+        turn(10, b2)
+        relu(11, b1)
+        turn(11, b4)
+        fetch_pair(2, 1, b6)
+        second_pair(2, 2, b6)
+        for k, bank in ((8, b5), (9, b7), (10, b2), (11, b4)):
             square(k, bank)
-        fetch_pair(0, 2, b6)
-        fetch_pair(2, 2, b0)
+        fetch_pair(0, 2, b3)
+        fetch_pair(2, 2, b6)
 
         for r in range(2):
-            gather_back(0, r, 0, T)
-        turn_and_add(b7, gated[0][1], gated[0][0])
-        nc.scalar.copy(routed_sum0_turned, b7[:])
+            gather_back(gated[0][r], 0, r, 0, T)
+        turn_and_add(b2, gated[0][1], gated[0][0], T)
+        nc.scalar.copy(routed_turned[0], b2[:])
         for r in range(2):
-            gather_back(1, r, 0, T)
+            gather_back(gated[1][r], 1, r, 0, T)
         quantise_hidden(SHARED, 0, T)
-        for c in range(0, T, P):
-            nc.tensor.matmul_mx(
-                out=b3[:, c : c + P],
-                lhsT=h_codes[SHARED][:, c : c + P].bitcast(FP8X4),
-                lhsT_scale=h_sc[SHARED][:, c : c + P],
-                rhs=w2[:, SHARED, 0 : 2 * P].bitcast(FP4X4),
-                rhs_scale=w2_sc[:, SHARED, 0:P],
-                start=True,
-                stop=True,
-            )
+        shared_turned_product(0, b0)
         second_product(SHARED, 1, b1[:], 0, T)
-        second_product(SHARED, 2, b4[:], 0, T)
-        nc.scalar.copy(shared_out0_turned, b3[:])
-        turn_and_add(b7, shared_out0_turned, routed_sum0_turned)
+        second_product(SHARED, 2, b5[:], 0, T)
+        nc.scalar.copy(shared_turned[0], b0[:])
+        turn_and_add(b7, shared_turned[0], routed_turned[0], T)
         nc.scalar.copy(result[0], b7[:])
         nc.scalar.dma_start(out=out[0:P, :], in_=result[0])
         add(routed_sum1, gated[1][0], gated[1][1])
-        gather_back(2, 0, 0, T)
+        gather_back(gated[2][0], 2, 0, 0, T)
         add(result[1], routed_sum1, b1[:])
         nc.sync.dma_start(out=out[P : 2 * P, :], in_=result[1])
-        add(part_sum2, gated[2][0], b4[:])
+        gather_back(gated[2][1], 2, 1, 0, T)
         for c in (0, HALF):
-            gather_back(2, 1, c, c + HALF)
+            add(part_sum2[:, c : c + HALF], gated[2][0][:, c : c + HALF], b5[:, c : c + HALF])
         for c in (0, HALF):
             add(result[2][:, c : c + HALF], part_sum2[:, c : c + HALF], gated[2][1][:, c : c + HALF])
             nc.sync.dma_start(out=out[2 * P : 3 * P, c : c + HALF], in_=result[2][:, c : c + HALF])

@@ -58,30 +58,30 @@ def tile_moe_shr_mlp_relu2_kernel(
         table_load = keep.tile([P, 1], F32, name="table_load")
 
         pairs = [sbuf(f"pairs{s}", 2 * 2 * T, BF16) for s in range(PASSES)]
-        relued = {k: sbuf(f"relued{k}", H, F32) for k in range(TILES) if k not in (0, 2)}
-        for k in (0, 2):
-            relued[k] = keep.tile([P, H], F32, name=f"relued{k}", tag=f"relued{k}", align_bytes=64)[:]
-        strip = sbuf("strip", 7 * C, U32)
-        woven = {(e, s): sbuf(f"woven{e}{s}", 2 * C, U32) for e, s in ((0, 0), (1, 0), (0, 1), (2, 0), (3, 0))}
-        woven[1, 1] = sbuf("woven11", 2 * C, U32)
+        relued = {k: sbuf(f"relued{k}", H, F32) for k in range(TILES) if k != 2}
+        relued[2] = keep.tile([P, H], F32, name="relued2", tag="relued2", align_bytes=64)[:]
+        strip = sbuf("strip", 8 * C, U32)
+        woven = {(e, s): sbuf(f"woven{e}{s}", 2 * C, U32) for e, s in ((0, 0), (1, 0), (0, 1), (3, 0))}
+        woven[2, 0] = strip[:, 0 : 2 * C]
         woven[2, 1] = strip[:, 3 * C : 5 * C]
+        woven[1, 1] = strip[:, 6 * C : 8 * C]
         woven[3, 1] = relued[3].bitcast(U32)
         room = {
             (0, 0): sbuf("first_room", 2 * C, U32),
-            (1, 0): strip[:, 0 : 2 * C],
-            (1, 1): strip[:, 0 : 2 * C],
-            (0, 1): strip[:, 2 * C : 4 * C],
-            (2, 0): strip[:, 3 * C : 5 * C],
-            (3, 0): strip[:, C : 3 * C],
-            (2, 1): woven[1, 1],
+            (1, 0): strip[:, C : 3 * C],
+            (1, 1): strip[:, C : 3 * C],
+            (0, 1): strip[:, 3 * C : 5 * C],
+            (2, 0): strip[:, 4 * C : 6 * C],
+            (3, 0): strip[:, 2 * C : 4 * C],
+            (2, 1): strip[:, 5 * C : 7 * C],
             (3, 1): strip[:, C : 3 * C],
         }
         shared_codes = sbuf("shared_codes", PASSES * T, U32)
         shared_sc = sbuf("shared_sc", PASSES * T, U8)
         x_codes = {(e, s): sbuf(f"x_codes{e}{s}", C, U32) for e in range(E) for s in range(PASSES) if (e, s) not in ((2, 1), (3, 1))}
-        x_codes[2, 1] = shared_codes[:, 0:C]
-        x_codes[3, 1] = shared_codes[:, T : T + C]
-        x_sc = {(e, s): sbuf(f"x_sc{e}{s}", C, U8) for e in range(E) for s in range(PASSES) if (e, s) not in ((0, 0), (2, 0), (2, 1))}
+        x_codes[2, 1] = sbuf("x_codes21", C, U32)
+        x_codes[3, 1] = shared_codes[:, T - C // 2 : T + C // 2]
+        x_sc = {(e, s): sbuf(f"x_sc{e}{s}", C, U8) for e in range(E) for s in range(PASSES) if (e, s) not in ((0, 0), (2, 1))}
         x_sc[0, 0] = keep.tile([P, C], U8, name="x_sc00", tag="x30", align_bytes=64)[:]
 
         hidden = [sbuf(f"hidden{e}", D * C, BF16) for e in range(E)] + [sbuf("hidden_shared", D * T, BF16)]
@@ -286,30 +286,29 @@ def tile_moe_shr_mlp_relu2_kernel(
         quantise_slots(1, 1)
         gather(0, 3)
         relu(0, b0)
-        turn(0, b3)
         first_product(2, b2, [1])
         first_product(3, b6, [1])
         relu(1, b1)
+        turn(0, b1)
         turn(1, b4)
         weave_on_scalar(2, 0)
         weave_on_scalar(3, 0)
         gather(3, 2)
-        gather(2, 2)
-        x_sc[2, 0] = keep.tile([P, C], U8, name="x_sc20", tag="relued0", align_bytes=64)[:]
         quantise_slots(2, 0)
+        gather(2, 2)
+        gather(2, 3)
         quantise_slots(3, 0)
         first_product(4, b0, [0])
-        first_product(5, b1, [0])
+        first_product(5, b3, [0])
         relu(2, b2)
         turn(2, b5)
         relu(3, b6)
         turn(3, b7)
         first_product(6, b6, [0])
-        square(0, b3)
-        first_product(7, b3, [0])
-        gather(3, 3)
+        square(0, b1)
+        first_product(7, b1, [0])
         weave(2, 1)
-        gather(2, 3)
+        gather(3, 3)
         x_sc[2, 1] = keep.tile([P, C], U8, name="x_sc21", tag="relued2", align_bytes=64)[:]
         quantise_slots(2, 1)
         weave(3, 1)
@@ -318,75 +317,78 @@ def tile_moe_shr_mlp_relu2_kernel(
         quantise_slots(3, 1)
         square(2, b5)
         square(3, b7)
-        for k, bank in ((4, b0), (5, b1), (6, b6), (7, b3)):
+        for k, bank in ((4, b0), (5, b3), (6, b6), (7, b1)):
             first_product(k, bank, [1])
         relu(4, b0)
         turn(4, b2)
-        relu(5, b1)
+        relu(5, b3)
         turn(5, b4)
-        quantise_shared(0)
-        relu_on_vector(6, b6)
         quantise_hidden(1, 0, C)
-        turn(6, b5)
-        second_pair(0, 0, b6)
-        relu(7, b3)
+        relu_on_vector(6, b6)
+        turn(6, b3)
+        relu(7, b1)
         turn(7, b7)
-        second_pair(0, 1, b3)
+        second_pair(0, 0, b1)
+        quantise_shared(0)
         quantise_shared(1)
-        first_product(8, b0)
-        first_product(9, b1)
-        nc.vector.tensor_copy(y[0][:, 0 : 2 * C], b6[:])
-        for k, bank in ((4, b2), (5, b4), (6, b5), (7, b7)):
+        square(4, b2)
+        first_product(8, b2)
+        for k, bank in ((5, b4), (6, b3), (7, b7)):
             square(k, bank)
         quantise_hidden(2, 0, C)
         quantise_hidden(3, 0, P)
-        second_product(2, 0, b2[:, 0:C], 0, C)
-        second_product(3, 0, b2[:, C : C + P], 0, P)
+        second_product(2, 0, b0[:, 0:C], 0, C)
+        second_product(3, 0, b0[:, C : C + P], 0, P)
+        first_product(9, b7)
         quantise_hidden(3, P, C)
-        second_product(3, 0, b4[:, C + P : 2 * C], P, C)
-        nc.vector.tensor_copy(y[0][:, 2 * C : 3 * C + P], b2[:, 0 : C + P])
-        nc.vector.tensor_copy(y[0][:, 3 * C + P : 4 * C], b4[:, C + P : 2 * C])
-        relu(8, b0)
-        first_product(10, b0)
-        relu(9, b1)
-        first_product(11, b1)
-        second_pair(2, 1, b6)
+        second_product(3, 0, b5[:, C + P : 2 * C], P, C)
+        nc.vector.tensor_copy(y[0][:, 2 * C : 3 * C + P], b0[:, 0 : C + P])
+        nc.vector.tensor_copy(y[0][:, 3 * C + P : 4 * C], b5[:, C + P : 2 * C])
+        fetch_pair(0, 0, b1)
+        second_pair(0, 1, b1)
+        second_pair(2, 1, b4)
+        relu(8, b2)
+        first_product(10, b2)
+        relu(9, b7)
+        first_product(11, b7)
+        fetch_pair(0, 1, b1)
         turn(8, b5)
-        turn(9, b7)
-        fetch_pair(0, 1, b3)
-        second_pair(0, 2, b3)
-        relu(10, b0)
-        turn(10, b2)
-        relu(11, b1)
-        turn(11, b4)
-        fetch_pair(2, 1, b6)
+        turn(9, b6)
+        fetch_pair(2, 1, b4)
+        relu(10, b2)
+        turn(10, b0)
+        relu(11, b7)
+        turn(11, b3)
+        square(8, b5)
+        second_pair(0, 2, b5)
+        square(9, b6)
         second_pair(2, 2, b6)
-        for k, bank in ((8, b5), (9, b7), (10, b2), (11, b4)):
-            square(k, bank)
-        fetch_pair(0, 2, b3)
+        square(10, b0)
+        square(11, b3)
+        fetch_pair(0, 2, b5)
         fetch_pair(2, 2, b6)
 
         for r in range(2):
             gather_back(gated[0][r], 0, r, 0, T)
-        turn_and_add(b2, gated[0][1], gated[0][0], T)
-        nc.scalar.copy(routed_turned[0], b2[:])
+        turn_and_add(b0, gated[0][1], gated[0][0], T)
+        nc.scalar.copy(routed_turned[0], b0[:])
         for r in range(2):
             gather_back(gated[1][r], 1, r, 0, T)
         quantise_hidden(SHARED, 0, T)
-        shared_turned_product(0, b0)
-        second_product(SHARED, 1, b1[:], 0, T)
-        second_product(SHARED, 2, b5[:], 0, T)
-        nc.scalar.copy(shared_turned[0], b0[:])
-        turn_and_add(b7, shared_turned[0], routed_turned[0], T)
-        nc.scalar.copy(result[0], b7[:])
+        shared_turned_product(0, b2)
+        second_product(SHARED, 1, b7[:], 0, T)
+        second_product(SHARED, 2, b4[:], 0, T)
+        nc.scalar.copy(shared_turned[0], b2[:])
+        turn_and_add(b1, shared_turned[0], routed_turned[0], T)
+        nc.scalar.copy(result[0], b1[:])
         nc.scalar.dma_start(out=out[0:P, :], in_=result[0])
         add(routed_sum1, gated[1][0], gated[1][1])
         gather_back(gated[2][0], 2, 0, 0, T)
-        add(result[1], routed_sum1, b1[:])
+        add(result[1], routed_sum1, b7[:])
         nc.sync.dma_start(out=out[P : 2 * P, :], in_=result[1])
         gather_back(gated[2][1], 2, 1, 0, T)
         for c in (0, HALF):
-            add(part_sum2[:, c : c + HALF], gated[2][0][:, c : c + HALF], b5[:, c : c + HALF])
+            add(part_sum2[:, c : c + HALF], gated[2][0][:, c : c + HALF], b4[:, c : c + HALF])
         for c in (0, HALF):
             add(result[2][:, c : c + HALF], part_sum2[:, c : c + HALF], gated[2][1][:, c : c + HALF])
             nc.sync.dma_start(out=out[2 * P : 3 * P, c : c + HALF], in_=result[2][:, c : c + HALF])

@@ -31,6 +31,7 @@ PER_COLUMN = 16
 BANK = 512
 HALF = T // 2
 PLANES = (1, 0, 3, 2)
+RELU_ON_VECTOR = 6
 
 
 def tile_moe_shr_mlp_relu2_kernel(
@@ -49,37 +50,43 @@ def tile_moe_shr_mlp_relu2_kernel(
         offs_sb = keep.tile([P, E * C // PER_COLUMN], U16, name="offs_sb")
         pos_sb = [keep.tile([P, T // PER_COLUMN], U16, name=f"pos_sb{r}") for r in range(2)]
         ident = keep.tile([P, P], F32, name="ident")
-        x = {j: [keep.tile([P, 2, T // pieces[j]], F32, name=f"x{j}{h}", tag=f"x{j}{h}", align_bytes=64) for h in range(pieces[j])] for j in PLANES}
+        x = {
+            j: [keep.tile([P, 2, T // pieces[j]], F32, name=f"x{j}{h}", tag=f"x{j}{h}", align_bytes=64) for h in range(pieces[j])]
+            for j in PLANES
+        }
         w1 = [keep.tile([P, PASSES, 2 * H], U8, name=f"w1_{e}", align_bytes=64) for e in range(E + 1)]
         w1_sc = keep.tile([P, (E + 1) * PASSES, H], U8, name="w1_sc", align_bytes=64)
         w2 = keep.tile([P, E + 1, 2 * N], U8, name="w2", align_bytes=64)
         w2_sc = keep.tile([P, E + 1, N], U8, name="w2_sc", align_bytes=64)
         gates = keep.tile([P, 2, T], F32, name="gates")
-        table_load = keep.tile([P, 1], F32, name="table_load")
+        made_ident = keep.tile([P, P], F32, name="made_ident")
 
         pairs = [sbuf(f"pairs{s}", 2 * 2 * T, BF16) for s in range(PASSES)]
         relued = {k: sbuf(f"relued{k}", H, F32) for k in range(TILES) if k != 2}
         relued[2] = keep.tile([P, H], F32, name="relued2", tag="relued2", align_bytes=64)[:]
         strip = sbuf("strip", 8 * C, U32)
+
+        def places(first):
+            return strip[:, first * C : (first + 2) * C]
+
         woven = {(e, s): sbuf(f"woven{e}{s}", 2 * C, U32) for e, s in ((0, 0), (1, 0), (0, 1), (3, 0))}
-        woven[2, 0] = strip[:, 0 : 2 * C]
-        woven[2, 1] = strip[:, 3 * C : 5 * C]
-        woven[1, 1] = strip[:, 6 * C : 8 * C]
+        woven[2, 0] = places(0)
+        woven[2, 1] = places(3)
+        woven[1, 1] = places(6)
         woven[3, 1] = relued[3].bitcast(U32)
         room = {
             (0, 0): sbuf("first_room", 2 * C, U32),
-            (1, 0): strip[:, C : 3 * C],
-            (1, 1): strip[:, C : 3 * C],
-            (0, 1): strip[:, 3 * C : 5 * C],
-            (2, 0): strip[:, 4 * C : 6 * C],
-            (3, 0): strip[:, 2 * C : 4 * C],
-            (2, 1): strip[:, 5 * C : 7 * C],
-            (3, 1): strip[:, C : 3 * C],
+            (1, 0): places(1),
+            (1, 1): places(1),
+            (0, 1): places(3),
+            (2, 0): places(4),
+            (3, 0): places(2),
+            (2, 1): places(5),
+            (3, 1): places(1),
         }
         shared_codes = sbuf("shared_codes", PASSES * T, U32)
         shared_sc = sbuf("shared_sc", PASSES * T, U8)
-        x_codes = {(e, s): sbuf(f"x_codes{e}{s}", C, U32) for e in range(E) for s in range(PASSES) if (e, s) not in ((2, 1), (3, 1))}
-        x_codes[2, 1] = sbuf("x_codes21", C, U32)
+        x_codes = {(e, s): sbuf(f"x_codes{e}{s}", C, U32) for e in range(E) for s in range(PASSES) if (e, s) != (3, 1)}
         x_codes[3, 1] = shared_codes[:, T - C // 2 : T + C // 2]
         x_sc = {(e, s): sbuf(f"x_sc{e}{s}", C, U8) for e in range(E) for s in range(PASSES) if (e, s) not in ((0, 0), (2, 1))}
         x_sc[0, 0] = keep.tile([P, C], U8, name="x_sc00", tag="x30", align_bytes=64)[:]
@@ -93,15 +100,14 @@ def tile_moe_shr_mlp_relu2_kernel(
         gated = [[sbuf(f"gated{n}{r}", T, F32) for r in range(2)] for n in range(BLOCKS)]
         part_sum2 = sbuf("part_sum2", T, F32)
         routed_sum1 = hidden[SHARED][:, 0 : 2 * T].bitcast(F32)
-        routed_turned = [sbuf(f"routed_turned{n}", T, F32) for n in range(2)]
-        shared_turned = [sbuf(f"shared_turned{n}", T, F32) for n in range(2)]
+        routed_turned = sbuf("routed_turned", T, F32)
+        shared_turned = sbuf("shared_turned", T, F32)
         result = [sbuf(f"result{n}", T, F32) for n in range(BLOCKS)]
 
-        nc.vector.memset(table_load[:], 0.0)
-        nc.scalar.activation(table_load[:], table_load[:], RELU)
         nc.vector.memset(w1_sc[:].bitcast(I32), 0)
         nc.vector.memset(w2_sc[:].bitcast(I32), 0)
-        make_identity(nc, ident[:])
+        make_identity(nc, made_ident[:])
+        nc.scalar.activation(ident[:], made_ident[:], RELU)
 
         x_rows = xT.rearrange("(s p d) t -> s p d t", s=PASSES, d=D)
         for j in PLANES:
@@ -155,6 +161,9 @@ def tile_moe_shr_mlp_relu2_kernel(
         def weave(e, s):
             nc.vector.tensor_copy(*weave_views(woven[e, s], room[e, s], I32))
 
+        def weave_on_scalar(dst, src):
+            nc.scalar.copy(*weave_views(dst, src, U32))
+
         def quantise(codes, scales, values):
             nc.vector.quantize_mx(out=codes.bitcast(FP8X4), scales=scales, in_=values)
 
@@ -189,17 +198,12 @@ def tile_moe_shr_mlp_relu2_kernel(
             for s in passes:
                 first_pass(k, s, bank, start=(s == 0), stop=(s == PASSES - 1))
 
-        def keep_warm(bank):
-            first_pass(0, 0, bank, start=True, stop=True)
-
         def relu(k, bank):
-            nc.scalar.activation(relued[k].rearrange("m (d p) -> m d p", d=D), bank[:].rearrange("m (p d) -> m d p", d=D), RELU)
-
-        def relu_on_vector(k, bank):
-            nc.vector.tensor_scalar_max(relued[k].rearrange("m (d p) -> m d p", d=D), bank[:].rearrange("m (p d) -> m d p", d=D), 0.0)
-
-        def weave_on_scalar(e, s):
-            nc.scalar.copy(*weave_views(woven[e, s], room[e, s], U32))
+            dst, src = relued[k].rearrange("m (d p) -> m d p", d=D), bank[:].rearrange("m (p d) -> m d p", d=D)
+            if k == RELU_ON_VECTOR:
+                nc.vector.tensor_scalar_max(dst, src, 0.0)
+            else:
+                nc.scalar.activation(dst, src, RELU)
 
         def turn(k, bank):
             for d in range(D):
@@ -237,14 +241,14 @@ def tile_moe_shr_mlp_relu2_kernel(
                 nc.tensor.matmul(bank[:, c : c + P], later[:, c : c + P], ident[:], start=True, stop=False, is_transpose=True)
                 nc.tensor.matmul(bank[:, c : c + P], earlier[:, c : c + P], ident[:], start=False, stop=True, is_transpose=True)
 
-        def shared_turned_product(n, bank):
-            for c in range(0, T, P):
+        def shared_turned_product(bank, first, last):
+            for c in range(first, last, P):
                 nc.tensor.matmul_mx(
-                    out=bank[:, c : c + P],
+                    out=bank[:, c - first : c - first + P],
                     lhsT=h_codes[SHARED][:, c : c + P].bitcast(FP8X4),
                     lhsT_scale=h_sc[SHARED][:, c : c + P],
-                    rhs=w2[:, SHARED, 2 * P * n : 2 * P * (n + 1)].bitcast(FP4X4),
-                    rhs_scale=w2_sc[:, SHARED, P * n : P * (n + 1)],
+                    rhs=w2[:, SHARED, 0 : 2 * P].bitcast(FP4X4),
+                    rhs_scale=w2_sc[:, SHARED, 0:P],
                     start=True,
                     stop=True,
                 )
@@ -266,21 +270,21 @@ def tile_moe_shr_mlp_relu2_kernel(
         quantise_slots(0, 0)
         first_product(0, b0, [0])
         first_product(1, b1, [0])
-        keep_warm(b3)
-        weave_on_scalar(1, 0)
-        nc.scalar.copy(*weave_views(shared_woven[0], pairs[0], U32))
+        weave_on_scalar(woven[1, 0], room[1, 0])
+        weave_on_scalar(shared_woven[0], pairs[0])
         gather(2, 0)
-        weave_on_scalar(0, 1)
-        nc.scalar.copy(*weave_views(shared_woven[1], pairs[1], U32))
+        weave_on_scalar(woven[0, 1], room[0, 1])
+        weave_on_scalar(shared_woven[1], pairs[1])
         gather(3, 1)
         quantise_slots(1, 0)
         first_product(2, b2, [0])
         first_product(3, b6, [0])
         gather(2, 1)
-        weave_on_scalar(1, 1)
+        weave_on_scalar(woven[1, 1], room[1, 1])
         quantise_slots(0, 1)
         first_product(0, b0, [1])
         first_product(1, b1, [1])
+
         gather(0, 2)
         gather(1, 3)
         quantise_slots(1, 1)
@@ -291,8 +295,8 @@ def tile_moe_shr_mlp_relu2_kernel(
         relu(1, b1)
         turn(0, b1)
         turn(1, b4)
-        weave_on_scalar(2, 0)
-        weave_on_scalar(3, 0)
+        weave_on_scalar(woven[2, 0], room[2, 0])
+        weave_on_scalar(woven[3, 0], room[3, 0])
         gather(3, 2)
         quantise_slots(2, 0)
         gather(2, 2)
@@ -317,6 +321,7 @@ def tile_moe_shr_mlp_relu2_kernel(
         quantise_slots(3, 1)
         square(2, b5)
         square(3, b7)
+
         for k, bank in ((4, b0), (5, b3), (6, b6), (7, b1)):
             first_product(k, bank, [1])
         relu(4, b0)
@@ -324,7 +329,7 @@ def tile_moe_shr_mlp_relu2_kernel(
         relu(5, b3)
         turn(5, b4)
         quantise_hidden(1, 0, C)
-        relu_on_vector(6, b6)
+        relu(6, b6)
         turn(6, b3)
         relu(7, b1)
         turn(7, b7)
@@ -335,6 +340,7 @@ def tile_moe_shr_mlp_relu2_kernel(
         first_product(8, b2)
         for k, bank in ((5, b4), (6, b3), (7, b7)):
             square(k, bank)
+
         quantise_hidden(2, 0, C)
         quantise_hidden(3, 0, P)
         second_product(2, 0, b0[:, 0:C], 0, C)
@@ -345,6 +351,7 @@ def tile_moe_shr_mlp_relu2_kernel(
         nc.vector.tensor_copy(y[0][:, 2 * C : 3 * C + P], b0[:, 0 : C + P])
         nc.vector.tensor_copy(y[0][:, 3 * C + P : 4 * C], b5[:, C + P : 2 * C])
         fetch_pair(0, 0, b1)
+
         second_pair(0, 1, b1)
         second_pair(2, 1, b4)
         relu(8, b2)
@@ -371,17 +378,21 @@ def tile_moe_shr_mlp_relu2_kernel(
         for r in range(2):
             gather_back(gated[0][r], 0, r, 0, T)
         turn_and_add(b0, gated[0][1], gated[0][0], T)
-        nc.scalar.copy(routed_turned[0], b0[:])
+        nc.scalar.copy(routed_turned, b0[:])
         for r in range(2):
             gather_back(gated[1][r], 1, r, 0, T)
         quantise_hidden(SHARED, 0, T)
-        shared_turned_product(0, b2)
+        halves = ((0, b2, b1), (HALF, b3, b0))
+        for c, source, bank in halves:
+            shared_turned_product(source, c, c + HALF)
         second_product(SHARED, 1, b7[:], 0, T)
         second_product(SHARED, 2, b4[:], 0, T)
-        nc.scalar.copy(shared_turned[0], b2[:])
-        turn_and_add(b1, shared_turned[0], routed_turned[0], T)
-        nc.scalar.copy(result[0], b1[:])
-        nc.scalar.dma_start(out=out[0:P, :], in_=result[0])
+        for c, source, bank in halves:
+            nc.scalar.copy(shared_turned[:, c : c + HALF], source[:, 0:HALF])
+            turn_and_add(bank, shared_turned[:, c : c + HALF], routed_turned[:, c : c + HALF], HALF)
+        for c, source, bank in halves:
+            nc.scalar.copy(result[0][:, c : c + HALF], bank[:, 0:HALF])
+            nc.scalar.dma_start(out=out[0:P, c : c + HALF], in_=result[0][:, c : c + HALF])
         add(routed_sum1, gated[1][0], gated[1][1])
         gather_back(gated[2][0], 2, 0, 0, T)
         add(result[1], routed_sum1, b7[:])

@@ -31,7 +31,7 @@ PER_COLUMN = 16
 BANK = 512
 HALF = T // 2
 PLANES = (1, 0, 3, 2)
-RELU_ON_VECTOR = 6
+RELU_ON_VECTOR = (6, 7)
 
 
 def tile_moe_shr_mlp_relu2_kernel(
@@ -46,7 +46,7 @@ def tile_moe_shr_mlp_relu2_kernel(
         def sbuf(name, columns, dtype):
             return keep.tile([P, columns], dtype, name=name, align_bytes=64)[:]
 
-        pieces = {j: 2 if j in (PLANES[0], PLANES[-1]) else 1 for j in PLANES}
+        pieces = {j: 2 for j in PLANES}
         offs_sb = keep.tile([P, E * C // PER_COLUMN], U16, name="offs_sb")
         pos_sb = [keep.tile([P, T // PER_COLUMN], U16, name=f"pos_sb{r}") for r in range(2)]
         ident = keep.tile([P, P], F32, name="ident")
@@ -54,7 +54,7 @@ def tile_moe_shr_mlp_relu2_kernel(
             j: [keep.tile([P, 2, T // pieces[j]], F32, name=f"x{j}{h}", tag=f"x{j}{h}", align_bytes=64) for h in range(pieces[j])]
             for j in PLANES
         }
-        w1 = [keep.tile([P, PASSES, 2 * H], U8, name=f"w1_{e}", align_bytes=64) for e in range(E + 1)]
+        w1 = [keep.tile([P, PASSES, 2 * H], U8, name=f"w1_{e}", tag=f"w1_{e}", align_bytes=64) for e in range(E + 1)]
         w1_sc = keep.tile([P, (E + 1) * PASSES, H], U8, name="w1_sc", align_bytes=64)
         w2 = keep.tile([P, E + 1, 2 * N], U8, name="w2", align_bytes=64)
         w2_sc = keep.tile([P, E + 1, N], U8, name="w2_sc", align_bytes=64)
@@ -62,39 +62,39 @@ def tile_moe_shr_mlp_relu2_kernel(
         made_ident = keep.tile([P, P], F32, name="made_ident")
 
         pairs = [sbuf(f"pairs{s}", 2 * 2 * T, BF16) for s in range(PASSES)]
-        relued = {k: sbuf(f"relued{k}", H, F32) for k in range(TILES) if k != 2}
-        relued[2] = keep.tile([P, H], F32, name="relued2", tag="relued2", align_bytes=64)[:]
+        def reuse(name, tag, columns, dtype):
+            return keep.tile([P, columns], dtype, name=name, tag=tag, align_bytes=64)[:]
+
+        relued = {k: reuse(f"relued{k}", f"relued{k}", H, F32) for k in range(TILES)}
         strip = sbuf("strip", 8 * C, U32)
 
         def places(first):
             return strip[:, first * C : (first + 2) * C]
 
-        woven = {(e, s): sbuf(f"woven{e}{s}", 2 * C, U32) for e, s in ((0, 0), (1, 0), (0, 1), (3, 0))}
-        woven[2, 0] = places(0)
-        woven[2, 1] = places(3)
-        woven[1, 1] = places(6)
-        woven[3, 1] = relued[3].bitcast(U32)
+        shared_woven = [sbuf(f"shared_woven{s}", 2 * T, U32) for s in range(PASSES)]
+        woven = {(e, s): sbuf(f"woven{e}{s}", 2 * C, U32) for e, s in ((0, 0), (0, 1), (1, 1), (2, 0), (3, 1))}
+        woven[1, 0] = places(6)
         room = {
-            (0, 0): sbuf("first_room", 2 * C, U32),
-            (1, 0): places(1),
+            (0, 0): places(0),
             (1, 1): places(1),
-            (0, 1): places(3),
+            (1, 0): places(3),
             (2, 0): places(4),
-            (3, 0): places(2),
-            (2, 1): places(5),
-            (3, 1): places(1),
+            (3, 0): places(4),
+            (2, 1): places(6),
+            (3, 1): places(6),
+            (0, 1): reuse("room01", "room01", 2 * C, U32),
         }
-        shared_codes = sbuf("shared_codes", PASSES * T, U32)
-        shared_sc = sbuf("shared_sc", PASSES * T, U8)
+        shared_codes = [sbuf(f"shared_codes{s}", T, U32) for s in range(PASSES)]
         x_codes = {(e, s): sbuf(f"x_codes{e}{s}", C, U32) for e in range(E) for s in range(PASSES) if (e, s) != (3, 1)}
-        x_codes[3, 1] = shared_codes[:, T - C // 2 : T + C // 2]
-        x_sc = {(e, s): sbuf(f"x_sc{e}{s}", C, U8) for e in range(E) for s in range(PASSES) if (e, s) not in ((0, 0), (2, 1))}
-        x_sc[0, 0] = keep.tile([P, C], U8, name="x_sc00", tag="x30", align_bytes=64)[:]
+        x_codes[3, 1] = shared_codes[1][:, 0:C]
+        shared_sc = {1: sbuf("shared_sc1", T, U8)}
+        x_sc = {(e, s): sbuf(f"x_sc{e}{s}", C, U8) for e in range(E) for s in range(PASSES) if (e, s) not in ((1, 0), (3, 1))}
+        x_sc[3, 1] = reuse("x_sc31", "x_sc31", C, U8)
 
-        hidden = [sbuf(f"hidden{e}", D * C, BF16) for e in range(E)] + [sbuf("hidden_shared", D * T, BF16)]
-        shared_woven = [sbuf(f"shared_woven{s}", D * T, BF16) for s in range(PASSES)]
+        hidden = [reuse(f"hidden{e}", f"hidden{e}", D * C, BF16) for e in range(E)] + [sbuf("hidden_shared", D * T, BF16)]
         h_codes = [sbuf(f"h_codes{e}", C, U32) for e in range(E)] + [sbuf("h_codes_shared", T, U32)]
-        h_sc = [sbuf(f"h_sc{e}", C, U8) for e in range(E)] + [sbuf("h_sc_shared", T, U8)]
+        h_sc = {e: sbuf(f"h_sc{e}", C, U8) for e in range(E) if e != 1}
+        h_sc[SHARED] = sbuf("h_sc_shared", T, U8)
 
         y = [keep.tile([P, E * C], F32, name=f"y{n}") for n in range(BLOCKS)]
         gated = [[sbuf(f"gated{n}{r}", T, F32) for r in range(2)] for n in range(BLOCKS)]
@@ -161,8 +161,8 @@ def tile_moe_shr_mlp_relu2_kernel(
         def weave(e, s):
             nc.vector.tensor_copy(*weave_views(woven[e, s], room[e, s], I32))
 
-        def weave_on_scalar(dst, src):
-            nc.scalar.copy(*weave_views(dst, src, U32))
+        def weave_on_scalar(e, s):
+            nc.scalar.copy(*weave_views(woven[e, s], room[e, s], U32))
 
         def quantise(codes, scales, values):
             nc.vector.quantize_mx(out=codes.bitcast(FP8X4), scales=scales, in_=values)
@@ -170,9 +170,13 @@ def tile_moe_shr_mlp_relu2_kernel(
         def quantise_slots(e, s):
             quantise(x_codes[e, s], x_sc[e, s], woven[e, s].bitcast(BF16))
 
+        def shared_views(s, first):
+            tokens = slice(first, first + HALF)
+            src = pairs[s].bitcast(U32).rearrange("p (u t) -> p t u", u=2)
+            return shared_woven[s].rearrange("p (t u) -> p t u", u=2)[:, tokens, :], src[:, tokens, :]
+
         def quantise_shared(s):
-            tokens = slice(T * s, T * (s + 1))
-            quantise(shared_codes[:, tokens], shared_sc[:, tokens], shared_woven[s])
+            quantise(shared_codes[s], shared_sc[s], shared_woven[s].bitcast(BF16))
 
         def quantise_hidden(e, first, last):
             quantise(h_codes[e][:, first:last], h_sc[e][:, first:last], hidden[e][:, D * first : D * last])
@@ -182,8 +186,8 @@ def tile_moe_shr_mlp_relu2_kernel(
 
         def first_pass(k, s, bank, start, stop):
             e, column = expert_and_column(k)
-            codes, scales, first = (x_codes[e, s], x_sc[e, s], column) if e < E else (shared_codes, shared_sc, T * s + column)
-            columns = slice(first, first + P)
+            codes, scales = (x_codes[e, s], x_sc[e, s]) if e < E else (shared_codes[s], shared_sc[s])
+            columns = slice(column, column + P)
             nc.tensor.matmul_mx(
                 out=bank[:],
                 lhsT=codes[:, columns].bitcast(FP8X4),
@@ -200,7 +204,7 @@ def tile_moe_shr_mlp_relu2_kernel(
 
         def relu(k, bank):
             dst, src = relued[k].rearrange("m (d p) -> m d p", d=D), bank[:].rearrange("m (p d) -> m d p", d=D)
-            if k == RELU_ON_VECTOR:
+            if k in RELU_ON_VECTOR:
                 nc.vector.tensor_scalar_max(dst, src, 0.0)
             else:
                 nc.scalar.activation(dst, src, RELU)
@@ -261,132 +265,126 @@ def tile_moe_shr_mlp_relu2_kernel(
         for j in PLANES[1:]:
             for dst, src in cast_views(j):
                 nc.scalar.activation(dst, src, COPY)
-        for e in range(3):
-            gather(1, e)
-        for e in range(2):
-            gather(0, e)
-        weave(0, 0)
-        gather(3, 0)
+        for s, first in ((0, 0), (0, HALF), (1, 0)):
+            nc.gpsimd.tensor_copy(*shared_views(s, first))
+        for j, experts in ((1, 3), (0, 2), (3, 2), (2, 1)):
+            for e in range(experts):
+                gather(j, e)
+        weave_on_scalar(0, 0)
+        weave_on_scalar(1, 0)
+        nc.scalar.copy(*shared_views(1, HALF))
+        weave_on_scalar(0, 1)
         quantise_slots(0, 0)
         first_product(0, b0, [0])
         first_product(1, b1, [0])
-        weave_on_scalar(woven[1, 0], room[1, 0])
-        weave_on_scalar(shared_woven[0], pairs[0])
-        gather(2, 0)
-        weave_on_scalar(woven[0, 1], room[0, 1])
-        weave_on_scalar(shared_woven[1], pairs[1])
-        gather(3, 1)
-        quantise_slots(1, 0)
-        first_product(2, b2, [0])
-        first_product(3, b6, [0])
         gather(2, 1)
-        weave_on_scalar(woven[1, 1], room[1, 1])
+        gather(0, 2)
+        weave_on_scalar(1, 1)
+        weave_on_scalar(2, 0)
         quantise_slots(0, 1)
         first_product(0, b0, [1])
         first_product(1, b1, [1])
-
-        gather(0, 2)
-        gather(1, 3)
+        x_sc[1, 0] = reuse("x_sc10", "room01", C, U8)
+        quantise_slots(1, 0)
         quantise_slots(1, 1)
+        first_product(2, b2)
+        first_product(3, b3)
+        gather(3, 2)
+        gather(2, 2)
+        quantise_slots(2, 0)
+        gather(1, 3)
         gather(0, 3)
         relu(0, b0)
-        first_product(2, b2, [1])
-        first_product(3, b6, [1])
         relu(1, b1)
-        turn(0, b1)
-        turn(1, b4)
-        weave_on_scalar(woven[2, 0], room[2, 0])
-        weave_on_scalar(woven[3, 0], room[3, 0])
-        gather(3, 2)
-        quantise_slots(2, 0)
-        gather(2, 2)
-        gather(2, 3)
-        quantise_slots(3, 0)
-        first_product(4, b0, [0])
-        first_product(5, b3, [0])
-        relu(2, b2)
-        turn(2, b5)
-        relu(3, b6)
-        turn(3, b7)
-        first_product(6, b6, [0])
-        square(0, b1)
-        first_product(7, b1, [0])
-        weave(2, 1)
-        gather(3, 3)
-        x_sc[2, 1] = keep.tile([P, C], U8, name="x_sc21", tag="relued2", align_bytes=64)[:]
+        turn(0, b6)
+        turn(1, b7)
+        first_product(4, b4, [0])
+        first_product(5, b5, [0])
+        woven[2, 1] = reuse("woven21", "w1_0", 2 * C, U32)
+        weave_on_scalar(2, 1)
         quantise_slots(2, 1)
+        gather(2, 3)
+        gather(3, 3)
+        woven[3, 0] = reuse("woven30", "w1_0", 2 * C, U32)
+        weave(3, 0)
         weave(3, 1)
-        square(1, b4)
-        quantise_hidden(0, 0, C)
+        quantise_slots(3, 0)
         quantise_slots(3, 1)
-        square(2, b5)
-        square(3, b7)
-
-        for k, bank in ((4, b0), (5, b3), (6, b6), (7, b1)):
-            first_product(k, bank, [1])
-        relu(4, b0)
-        turn(4, b2)
-        relu(5, b3)
-        turn(5, b4)
-        quantise_hidden(1, 0, C)
-        relu(6, b6)
-        turn(6, b3)
-        relu(7, b1)
-        turn(7, b7)
-        second_pair(0, 0, b1)
+        shared_sc[0] = reuse("shared_sc0", "w1_0", T, U8)
         quantise_shared(0)
-        quantise_shared(1)
-        square(4, b2)
-        first_product(8, b2)
-        for k, bank in ((5, b4), (6, b3), (7, b7)):
+        relu(2, b2)
+        turn(2, b0)
+        first_product(4, b4, [1])
+        first_product(5, b5, [1])
+        relu(3, b3)
+        turn(3, b1)
+        square(0, b6)
+        square(1, b7)
+        relu(4, b4)
+        turn(4, b2)
+        first_product(6, b4)
+        relu(5, b5)
+        first_product(7, b5)
+        turn(5, b3)
+        quantise_hidden(0, 0, C)
+        relu(6, b4)
+        turn(6, b6)
+        relu(7, b5)
+        turn(7, b7)
+        for k, bank in ((2, b0), (3, b1), (4, b2), (5, b3), (6, b6), (7, b7)):
             square(k, bank)
+        h_sc[1] = reuse("h_sc1", "x_sc31", C, U8)
+        quantise_hidden(1, 0, C)
+        quantise_shared(1)
+        second_pair(0, 0, b4)
+        first_product(8, b5)
 
         quantise_hidden(2, 0, C)
         quantise_hidden(3, 0, P)
-        second_product(2, 0, b0[:, 0:C], 0, C)
-        second_product(3, 0, b0[:, C : C + P], 0, P)
-        first_product(9, b7)
+        nc.vector.tensor_copy(y[0][:, 0 : 2 * C], b4[:])
+        second_product(2, 0, b1[:, 0:C], 0, C)
+        second_product(3, 0, b1[:, C : C + P], 0, P)
+        first_product(9, b6)
         quantise_hidden(3, P, C)
-        second_product(3, 0, b5[:, C + P : 2 * C], P, C)
-        nc.vector.tensor_copy(y[0][:, 2 * C : 3 * C + P], b0[:, 0 : C + P])
-        nc.vector.tensor_copy(y[0][:, 3 * C + P : 4 * C], b5[:, C + P : 2 * C])
-        fetch_pair(0, 0, b1)
+        second_product(3, 0, b3[:, C + P : 2 * C], P, C)
+        nc.vector.tensor_copy(y[0][:, 2 * C : 3 * C + P], b1[:, 0 : C + P])
+        nc.vector.tensor_copy(y[0][:, 3 * C + P : 4 * C], b3[:, C + P : 2 * C])
 
-        second_pair(0, 1, b1)
-        second_pair(2, 1, b4)
-        relu(8, b2)
-        first_product(10, b2)
-        relu(9, b7)
-        first_product(11, b7)
-        fetch_pair(0, 1, b1)
-        turn(8, b5)
-        turn(9, b6)
-        fetch_pair(2, 1, b4)
-        relu(10, b2)
-        turn(10, b0)
-        relu(11, b7)
-        turn(11, b3)
-        square(8, b5)
-        second_pair(0, 2, b5)
-        square(9, b6)
-        second_pair(2, 2, b6)
-        square(10, b0)
-        square(11, b3)
-        fetch_pair(0, 2, b5)
-        fetch_pair(2, 2, b6)
+        second_pair(0, 1, b7)
+        second_pair(2, 1, b0)
+        relu(8, b5)
+        first_product(10, b5)
+        relu(9, b6)
+        first_product(11, b6)
+        fetch_pair(0, 1, b7)
+        turn(8, b4)
+        turn(9, b3)
+        fetch_pair(2, 1, b0)
+        relu(10, b5)
+        turn(10, b1)
+        relu(11, b6)
+        turn(11, b2)
+        square(8, b4)
+        second_pair(0, 2, b4)
+        square(9, b3)
+        second_pair(2, 2, b3)
+        square(10, b1)
+        square(11, b2)
+        fetch_pair(0, 2, b4)
+        fetch_pair(2, 2, b3)
 
         for r in range(2):
             gather_back(gated[0][r], 0, r, 0, T)
-        turn_and_add(b0, gated[0][1], gated[0][0], T)
-        nc.scalar.copy(routed_turned, b0[:])
+        turn_and_add(b1, gated[0][1], gated[0][0], T)
+        nc.scalar.copy(routed_turned, b1[:])
         for r in range(2):
             gather_back(gated[1][r], 1, r, 0, T)
         quantise_hidden(SHARED, 0, T)
-        halves = ((0, b2, b1), (HALF, b3, b0))
+        halves = ((0, b6, b5), (HALF, b2, b1))
         for c, source, bank in halves:
             shared_turned_product(source, c, c + HALF)
         second_product(SHARED, 1, b7[:], 0, T)
-        second_product(SHARED, 2, b4[:], 0, T)
+        second_product(SHARED, 2, b0[:], 0, T)
         for c, source, bank in halves:
             nc.scalar.copy(shared_turned[:, c : c + HALF], source[:, 0:HALF])
             turn_and_add(bank, shared_turned[:, c : c + HALF], routed_turned[:, c : c + HALF], HALF)
@@ -399,7 +397,7 @@ def tile_moe_shr_mlp_relu2_kernel(
         nc.sync.dma_start(out=out[P : 2 * P, :], in_=result[1])
         gather_back(gated[2][1], 2, 1, 0, T)
         for c in (0, HALF):
-            add(part_sum2[:, c : c + HALF], gated[2][0][:, c : c + HALF], b4[:, c : c + HALF])
+            add(part_sum2[:, c : c + HALF], gated[2][0][:, c : c + HALF], b0[:, c : c + HALF])
         for c in (0, HALF):
             add(result[2][:, c : c + HALF], part_sum2[:, c : c + HALF], gated[2][1][:, c : c + HALF])
             nc.sync.dma_start(out=out[2 * P : 3 * P, c : c + HALF], in_=result[2][:, c : c + HALF])

@@ -31,7 +31,7 @@ PER_COLUMN = 16
 BANK = 512
 HALF = T // 2
 PLANES = (1, 0, 3, 2)
-RELU_ON_VECTOR = (6, 7)
+RELU_ON_VECTOR = (7,)
 
 
 def tile_moe_shr_mlp_relu2_kernel(
@@ -51,50 +51,49 @@ def tile_moe_shr_mlp_relu2_kernel(
         pos_sb = [keep.tile([P, T // PER_COLUMN], U16, name=f"pos_sb{r}") for r in range(2)]
         ident = keep.tile([P, P], F32, name="ident")
         x = {
-            j: [keep.tile([P, 2, T // pieces[j]], F32, name=f"x{j}{h}", tag=f"x{j}{h}", align_bytes=64) for h in range(pieces[j])]
+            j: [keep.tile([P, 2, T // pieces[j]], F32, name=f"x{j}{h}", tag=f"x{j}{h}", align_bytes=64)[:] for h in range(pieces[j])]
             for j in PLANES
         }
         w1 = [keep.tile([P, PASSES, 2 * H], U8, name=f"w1_{e}", tag=f"w1_{e}", align_bytes=64) for e in range(E + 1)]
         w1_sc = keep.tile([P, (E + 1) * PASSES, H], U8, name="w1_sc", align_bytes=64)
-        w2 = keep.tile([P, E + 1, 2 * N], U8, name="w2", align_bytes=64)
         w2_sc = keep.tile([P, E + 1, N], U8, name="w2_sc", align_bytes=64)
-        gates = keep.tile([P, 2, T], F32, name="gates")
         made_ident = keep.tile([P, P], F32, name="made_ident")
 
-        pairs = [sbuf(f"pairs{s}", 2 * 2 * T, BF16) for s in range(PASSES)]
+        pairs = sbuf("pairs", 5 * T, U32)
         def reuse(name, tag, columns, dtype):
             return keep.tile([P, columns], dtype, name=name, tag=tag, align_bytes=64)[:]
 
         relued = {k: reuse(f"relued{k}", f"relued{k}", H, F32) for k in range(TILES)}
-        strip = sbuf("strip", 8 * C, U32)
-
-        def places(first):
-            return strip[:, first * C : (first + 2) * C]
-
-        shared_woven = [sbuf(f"shared_woven{s}", 2 * T, U32) for s in range(PASSES)]
-        woven = {(e, s): sbuf(f"woven{e}{s}", 2 * C, U32) for e, s in ((0, 0), (0, 1), (1, 1), (2, 0), (3, 1))}
-        woven[1, 0] = places(6)
-        room = {
-            (0, 0): places(0),
-            (1, 1): places(1),
-            (1, 0): places(3),
-            (2, 0): places(4),
-            (3, 0): places(4),
-            (2, 1): places(6),
-            (3, 1): places(6),
-            (0, 1): reuse("room01", "room01", 2 * C, U32),
+        strip = sbuf("strip", 20 * C, U32)
+        place = {
+            (0, 0): 0, (0, 1): 1, (2, 0): 2, (1, 0): 3, (1, 1): 4, (1, 2): 5, (3, 0): 6, (3, 1): 7,
+            (2, 1): 0, (0, 2): 2, (2, 2): 0, (3, 2): 7, (0, 3): 2, (1, 3): 11, (2, 3): 0, (3, 3): 7,
         }
-        shared_codes = [sbuf(f"shared_codes{s}", T, U32) for s in range(PASSES)]
-        x_codes = {(e, s): sbuf(f"x_codes{e}{s}", C, U32) for e in range(E) for s in range(PASSES) if (e, s) != (3, 1)}
-        x_codes[3, 1] = shared_codes[1][:, 0:C]
+        shared_woven = sbuf("shared_woven", PASSES * 2 * T, U32)
+        woven = {(e, s): sbuf(f"woven{e}{s}", 2 * C, U32) for e, s in ((0, 1), (3, 1))}
+        woven[0, 0] = strip[:, 8 * C : 10 * C]
+        woven1 = strip[:, 10 * C : 14 * C]
+        woven[2, 0] = strip[:, 13 * C : 15 * C]
+        shared_codes = sbuf("shared_codes", PASSES * T, U32)
+        x_codes = {(e, s): sbuf(f"x_codes{e}{s}", C, U32) for e in (0, 2, 3) for s in range(PASSES) if (e, s) != (3, 1)}
+        x_codes[3, 1] = shared_codes[:, T : T + C]
         shared_sc = {1: sbuf("shared_sc1", T, U8)}
-        x_sc = {(e, s): sbuf(f"x_sc{e}{s}", C, U8) for e in range(E) for s in range(PASSES) if (e, s) not in ((1, 0), (3, 1))}
+        x_sc = {(e, s): sbuf(f"x_sc{e}{s}", C, U8) for e in (0, 2, 3) for s in range(PASSES) if (e, s) != (3, 1)}
         x_sc[3, 1] = reuse("x_sc31", "x_sc31", C, U8)
+        x_codes1, x_sc1 = sbuf("x_codes1", PASSES * C, U32), sbuf("x_sc1", PASSES * C, U8)
+        for s in range(PASSES):
+            woven[1, s] = woven1[:, 2 * C * s : 2 * C * (s + 1)]
+            x_codes[1, s], x_sc[1, s] = x_codes1[:, C * s : C * (s + 1)], x_sc1[:, C * s : C * (s + 1)]
 
-        hidden = [reuse(f"hidden{e}", f"hidden{e}", D * C, BF16) for e in range(E)] + [sbuf("hidden_shared", D * T, BF16)]
-        h_codes = [sbuf(f"h_codes{e}", C, U32) for e in range(E)] + [sbuf("h_codes_shared", T, U32)]
-        h_sc = {e: sbuf(f"h_sc{e}", C, U8) for e in range(E) if e != 1}
+        hidden01, h_codes01 = sbuf("hidden01", 2 * D * C, BF16), sbuf("h_codes01", 2 * C, U32)
+        hidden = [hidden01[:, D * C * e : D * C * (e + 1)] for e in range(2)]
+        hidden += [sbuf(f"hidden{e}", D * C, BF16) for e in range(2, E)] + [sbuf("hidden_shared", D * T, BF16)]
+        h_codes = [h_codes01[:, C * e : C * (e + 1)] for e in range(2)]
+        h_codes += [sbuf(f"h_codes{e}", C, U32) for e in range(2, E)] + [sbuf("h_codes_shared", T, U32)]
+        h_sc = {e: sbuf(f"h_sc{e}", C, U8) for e in range(2, E)}
         h_sc[SHARED] = sbuf("h_sc_shared", T, U8)
+        h_sc01 = sbuf("h_sc01", 2 * C, U8)
+        h_sc[0], h_sc[1] = h_sc01[:, 0:C], h_sc01[:, C : 2 * C]
 
         y = [keep.tile([P, E * C], F32, name=f"y{n}") for n in range(BLOCKS)]
         gated = [[sbuf(f"gated{n}{r}", T, F32) for r in range(2)] for n in range(BLOCKS)]
@@ -106,6 +105,7 @@ def tile_moe_shr_mlp_relu2_kernel(
 
         nc.vector.memset(w1_sc[:].bitcast(I32), 0)
         nc.vector.memset(w2_sc[:].bitcast(I32), 0)
+        nc.vector.memset(pairs[:, 4 * T : 5 * T], 0)
         make_identity(nc, made_ident[:])
         nc.scalar.activation(ident[:], made_ident[:], RELU)
 
@@ -114,55 +114,57 @@ def tile_moe_shr_mlp_relu2_kernel(
             s, u = divmod(j, 2)
             width = T // pieces[j]
             for h in range(pieces[j]):
-                nc.sync.dma_start(out=x[j][h][:], in_=x_rows[s, :, 2 * u : 2 * u + 2, width * h : width * (h + 1)])
+                nc.sync.dma_start(out=x[j][h], in_=x_rows[s, :, 2 * u : 2 * u + 2, width * h : width * (h + 1)])
             if j == PLANES[0]:
                 nc.sync.dma_start(offs_sb[:], offs)
 
         def load_words(e):
             nc.sync.dma_start(out=w1[e][:].bitcast(I32), in_=w1_words[e].rearrange("s p b -> p s b").bitcast(I32))
 
-        def load_scales(dst, scales, first, last):
+        def load_scales(queue, dst, scales, first, last):
             rows = scales.rearrange("e s (q r) i -> q r (e s) i", q=4)
             for q in range(4):
-                nc.sync.dma_start(out=dst[32 * q : 32 * q + 4, first:last, :].bitcast(I32), in_=rows[q, :, first:last, :].bitcast(I32))
+                queue.dma_start(out=dst[32 * q : 32 * q + 4, first:last, :].bitcast(I32), in_=rows[q, :, first:last, :].bitcast(I32))
 
         load_words(0)
-        load_scales(w1_sc, w1_scales, 0, 2 * PASSES)
+        load_scales(nc.sync, w1_sc, w1_scales, 0, 2 * PASSES)
         load_words(1)
-        load_scales(w1_sc, w1_scales, 2 * PASSES, (E + 1) * PASSES)
-        for e in range(2, E):
-            load_words(e)
-        load_scales(w2_sc, w2_scales, 0, E + 1)
-        nc.sync.dma_start(out=w2[:].bitcast(I32), in_=w2_words.rearrange("e s p b -> p (e s) b").bitcast(I32))
+        load_words(2)
+        load_scales(nc.sync, w1_sc, w1_scales, 2 * PASSES, (E + 1) * PASSES)
+        load_words(3)
         load_words(SHARED)
+        load_scales(nc.sync, w2_sc, w2_scales, 0, E + 1)
         for r, positions in enumerate((pos1, pos2)):
             nc.sync.dma_start(pos_sb[r][:], positions)
-        nc.sync.dma_start(out=gates[:], in_=gate[:, 0:P, :].rearrange("g p t -> p g t"))
+
+        def plane_start(j):
+            return T * ((j + 2) % 4)
 
         def plane(j):
-            s, u = divmod(j, 2)
-            return pairs[s][:, 2 * T * u : 2 * T * (u + 1)]
+            return pairs[:, plane_start(j) : plane_start(j) + T].bitcast(BF16)
 
         def cast_views(j):
             width = 2 * T // pieces[j]
             return [
-                (plane(j)[:, width * h : width * (h + 1)].rearrange("p (t d) -> p t d", d=2), x[j][h][:].rearrange("p d t -> p t d"))
+                (plane(j)[:, width * h : width * (h + 1)].rearrange("p (t d) -> p t d", d=2), x[j][h].rearrange("p d t -> p t d"))
                 for h in range(pieces[j])
             ]
 
-        def gather(j, e):
-            s, u = divmod(j, 2)
-            slots = offs_sb[:, e * C // PER_COLUMN : (e + 1) * C // PER_COLUMN]
-            nc.vector.tensor_copy(room[e, s][:, C * u : C * (u + 1)], plane(j).bitcast(U32).indirect(slots))
+        def gather(j, e, experts=1):
+            slots = offs_sb[:, e * C // PER_COLUMN : (e + experts) * C // PER_COLUMN]
+            window = pairs[:, plane_start(j) : plane_start(j) + (T if experts == 1 else 2 * T)]
+            nc.vector.tensor_copy(strip[:, C * place[j, e] : C * (place[j, e] + experts)], window.indirect(slots))
 
-        def weave_views(dst, src, dtype):
-            return dst.bitcast(dtype).rearrange("p (c u) -> p c u", u=2), src.bitcast(dtype).rearrange("p (u c) -> p c u", u=2)
+        def weave_views(e, s, dtype):
+            even, odd = C * place[2 * s, e], C * place[2 * s + 1, e]
+            src = strip[:, even : 2 * odd - even].bitcast(dtype).rearrange("p (u c) -> p c u", u=2)[:, 0:C, :]
+            return woven[e, s].bitcast(dtype).rearrange("p (c u) -> p c u", u=2), src
 
         def weave(e, s):
-            nc.vector.tensor_copy(*weave_views(woven[e, s], room[e, s], I32))
+            nc.vector.tensor_copy(*weave_views(e, s, I32))
 
         def weave_on_scalar(e, s):
-            nc.scalar.copy(*weave_views(woven[e, s], room[e, s], U32))
+            nc.scalar.copy(*weave_views(e, s, U32))
 
         def quantise(codes, scales, values):
             nc.vector.quantize_mx(out=codes.bitcast(FP8X4), scales=scales, in_=values)
@@ -172,11 +174,12 @@ def tile_moe_shr_mlp_relu2_kernel(
 
         def shared_views(s, first):
             tokens = slice(first, first + HALF)
-            src = pairs[s].bitcast(U32).rearrange("p (u t) -> p t u", u=2)
-            return shared_woven[s].rearrange("p (t u) -> p t u", u=2)[:, tokens, :], src[:, tokens, :]
+            src = pairs[:, plane_start(2 * s) : plane_start(2 * s) + 2 * T].rearrange("p (u t) -> p t u", u=2)
+            dst = shared_woven[:, 2 * T * s : 2 * T * (s + 1)].rearrange("p (t u) -> p t u", u=2)
+            return dst[:, tokens, :], src[:, tokens, :]
 
         def quantise_shared(s):
-            quantise(shared_codes[s], shared_sc[s], shared_woven[s].bitcast(BF16))
+            quantise(shared_codes[:, T * s : T * (s + 1)], shared_sc[s], shared_woven[:, 2 * T * s : 2 * T * (s + 1)].bitcast(BF16))
 
         def quantise_hidden(e, first, last):
             quantise(h_codes[e][:, first:last], h_sc[e][:, first:last], hidden[e][:, D * first : D * last])
@@ -186,7 +189,7 @@ def tile_moe_shr_mlp_relu2_kernel(
 
         def first_pass(k, s, bank, start, stop):
             e, column = expert_and_column(k)
-            codes, scales = (x_codes[e, s], x_sc[e, s]) if e < E else (shared_codes[s], shared_sc[s])
+            codes, scales = (x_codes[e, s], x_sc[e, s]) if e < E else (shared_codes[:, T * s : T * (s + 1)], shared_sc[s])
             columns = slice(column, column + P)
             nc.tensor.matmul_mx(
                 out=bank[:],
@@ -265,113 +268,116 @@ def tile_moe_shr_mlp_relu2_kernel(
         for j in PLANES[1:]:
             for dst, src in cast_views(j):
                 nc.scalar.activation(dst, src, COPY)
+        gates = keep.tile([P, 2, T], F32, name="gates", tag="x20", align_bytes=64)
+        nc.scalar.dma_start(out=gates[:], in_=gate[:, 0:P, :].rearrange("g p t -> p g t"))
         for s, first in ((0, 0), (0, HALF), (1, 0)):
             nc.gpsimd.tensor_copy(*shared_views(s, first))
         for j, experts in ((1, 3), (0, 2), (3, 2), (2, 1)):
-            for e in range(experts):
-                gather(j, e)
+            gather(j, 0, experts)
         weave_on_scalar(0, 0)
         weave_on_scalar(1, 0)
-        nc.scalar.copy(*shared_views(1, HALF))
+        w2 = keep.tile([P, E + 1, 2 * N], U8, name="w2", tag="x21", align_bytes=64)
+        nc.scalar.dma_start(out=w2[:].bitcast(I32), in_=w2_words.rearrange("e s p b -> p (e s) b").bitcast(I32))
         weave_on_scalar(0, 1)
         quantise_slots(0, 0)
         first_product(0, b0, [0])
         first_product(1, b1, [0])
         gather(2, 1)
-        gather(0, 2)
         weave_on_scalar(1, 1)
-        weave_on_scalar(2, 0)
+        nc.scalar.copy(*shared_views(1, HALF))
         quantise_slots(0, 1)
         first_product(0, b0, [1])
         first_product(1, b1, [1])
-        x_sc[1, 0] = reuse("x_sc10", "room01", C, U8)
-        quantise_slots(1, 0)
-        quantise_slots(1, 1)
+        gather(0, 2)
+        quantise(x_codes1, x_sc1, woven1.bitcast(BF16))
         first_product(2, b2)
         first_product(3, b3)
+        nc.gpsimd.tensor_copy(*weave_views(2, 0, U32))
         gather(3, 2)
         gather(2, 2)
-        quantise_slots(2, 0)
         gather(1, 3)
+        quantise_slots(2, 0)
         gather(0, 3)
         relu(0, b0)
         relu(1, b1)
         turn(0, b6)
         turn(1, b7)
+        relu(2, b2)
+        turn(2, b0)
         first_product(4, b4, [0])
         first_product(5, b5, [0])
-        woven[2, 1] = reuse("woven21", "w1_0", 2 * C, U32)
+        woven[2, 1] = reuse("woven21", "w1_1", 2 * C, U32)
         weave_on_scalar(2, 1)
         quantise_slots(2, 1)
-        gather(2, 3)
         gather(3, 3)
-        woven[3, 0] = reuse("woven30", "w1_0", 2 * C, U32)
+        gather(2, 3)
+        woven[3, 0] = reuse("woven30", "w1_1", 2 * C, U32)
         weave(3, 0)
         weave(3, 1)
         quantise_slots(3, 0)
         quantise_slots(3, 1)
-        shared_sc[0] = reuse("shared_sc0", "w1_0", T, U8)
+        shared_sc[0] = reuse("shared_sc0", "w1_1", T, U8)
         quantise_shared(0)
-        relu(2, b2)
-        turn(2, b0)
         first_product(4, b4, [1])
         first_product(5, b5, [1])
         relu(3, b3)
-        turn(3, b1)
         square(0, b6)
+        turn(3, b6)
         square(1, b7)
+        square(2, b0)
         relu(4, b4)
         turn(4, b2)
         first_product(6, b4)
         relu(5, b5)
         first_product(7, b5)
         turn(5, b3)
-        quantise_hidden(0, 0, C)
+        square(3, b6)
+        quantise(h_codes01, h_sc01, hidden01)
+        square(4, b2)
+        first_product(8, b2, [0])
         relu(6, b4)
-        turn(6, b6)
+        turn(6, b7)
         relu(7, b5)
-        turn(7, b7)
-        for k, bank in ((2, b0), (3, b1), (4, b2), (5, b3), (6, b6), (7, b7)):
-            square(k, bank)
-        h_sc[1] = reuse("h_sc1", "x_sc31", C, U8)
-        quantise_hidden(1, 0, C)
+        turn(7, b4)
         quantise_shared(1)
-        second_pair(0, 0, b4)
-        first_product(8, b5)
-
+        square(5, b3)
+        square(6, b7)
+        square(7, b4)
+        second_pair(0, 0, b5)
+        first_product(8, b2, [1])
         quantise_hidden(2, 0, C)
-        quantise_hidden(3, 0, P)
-        nc.vector.tensor_copy(y[0][:, 0 : 2 * C], b4[:])
         second_product(2, 0, b1[:, 0:C], 0, C)
+        first_product(9, b7)
+        quantise_hidden(3, 0, P)
         second_product(3, 0, b1[:, C : C + P], 0, P)
-        first_product(9, b6)
         quantise_hidden(3, P, C)
-        second_product(3, 0, b3[:, C + P : 2 * C], P, C)
+        second_product(3, 0, b0[:, C + P : 2 * C], P, C)
         nc.vector.tensor_copy(y[0][:, 2 * C : 3 * C + P], b1[:, 0 : C + P])
-        nc.vector.tensor_copy(y[0][:, 3 * C + P : 4 * C], b3[:, C + P : 2 * C])
+        nc.vector.tensor_copy(y[0][:, 3 * C + P : 4 * C], b0[:, C + P : 2 * C])
+        fetch_pair(0, 0, b5)
 
-        second_pair(0, 1, b7)
-        second_pair(2, 1, b0)
-        relu(8, b5)
-        first_product(10, b5)
-        relu(9, b6)
-        first_product(11, b6)
-        fetch_pair(0, 1, b7)
-        turn(8, b4)
-        turn(9, b3)
-        fetch_pair(2, 1, b0)
-        relu(10, b5)
+        second_pair(0, 1, b4)
+        second_pair(2, 1, b3)
+        relu(8, b2)
+        first_product(10, b2)
+        relu(9, b7)
+        first_product(11, b7)
+        fetch_pair(0, 1, b4)
+        turn(8, b5)
+        turn(9, b6)
+        fetch_pair(2, 1, b3)
+        relu(10, b2)
         turn(10, b1)
-        relu(11, b6)
-        turn(11, b2)
-        square(8, b4)
-        second_pair(0, 2, b4)
-        square(9, b3)
-        second_pair(2, 2, b3)
+        relu(11, b7)
+        turn(11, b0)
+        square(8, b5)
+        second_pair(0, 2, b5)
+        square(9, b6)
+        second_pair(2, 2, b6)
         square(10, b1)
-        square(11, b2)
-        fetch_pair(0, 2, b4)
-        fetch_pair(2, 2, b3)
+        square(11, b0)
+        fetch_pair(0, 2, b5)
+        fetch_pair(2, 2, b6)
 
         for r in range(2):
             gather_back(gated[0][r], 0, r, 0, T)
@@ -380,11 +386,11 @@ def tile_moe_shr_mlp_relu2_kernel(
         for r in range(2):
             gather_back(gated[1][r], 1, r, 0, T)
         quantise_hidden(SHARED, 0, T)
-        halves = ((0, b6, b5), (HALF, b2, b1))
+        halves = ((0, b2, b4), (HALF, b0, b1))
         for c, source, bank in halves:
             shared_turned_product(source, c, c + HALF)
         second_product(SHARED, 1, b7[:], 0, T)
-        second_product(SHARED, 2, b0[:], 0, T)
+        second_product(SHARED, 2, b3[:], 0, T)
         for c, source, bank in halves:
             nc.scalar.copy(shared_turned[:, c : c + HALF], source[:, 0:HALF])
             turn_and_add(bank, shared_turned[:, c : c + HALF], routed_turned[:, c : c + HALF], HALF)
@@ -397,7 +403,7 @@ def tile_moe_shr_mlp_relu2_kernel(
         nc.sync.dma_start(out=out[P : 2 * P, :], in_=result[1])
         gather_back(gated[2][1], 2, 1, 0, T)
         for c in (0, HALF):
-            add(part_sum2[:, c : c + HALF], gated[2][0][:, c : c + HALF], b0[:, c : c + HALF])
+            add(part_sum2[:, c : c + HALF], gated[2][0][:, c : c + HALF], b3[:, c : c + HALF])
         for c in (0, HALF):
             add(result[2][:, c : c + HALF], part_sum2[:, c : c + HALF], gated[2][1][:, c : c + HALF])
             nc.sync.dma_start(out=out[2 * P : 3 * P, c : c + HALF], in_=result[2][:, c : c + HALF])

@@ -67,10 +67,12 @@ def tile_moe_shr_mlp_relu2_kernel(
         strip = sbuf("strip", 20 * C, U32)
         place = {
             (0, 0): 0, (0, 1): 1, (2, 0): 2, (1, 0): 3, (1, 1): 4, (1, 2): 5, (3, 0): 6, (3, 1): 7,
-            (2, 1): 0, (0, 2): 2, (2, 2): 0, (3, 2): 7, (0, 3): 2, (1, 3): 11, (2, 3): 0, (3, 3): 7,
+            (2, 1): 0, (0, 2): 2, (2, 2): 0, (3, 2): 7, (0, 3): 2, (1, 3): 11, (2, 3): 0, (3, 3): 5,
         }
         shared_woven = sbuf("shared_woven", PASSES * 2 * T, U32)
-        woven = {(e, s): sbuf(f"woven{e}{s}", 2 * C, U32) for e, s in ((0, 1), (3, 1))}
+        woven = {(e, s): sbuf(f"woven{e}{s}", 2 * C, U32) for e, s in ((0, 1),)}
+        woven[3, 1] = reuse("woven31", "woven31", 2 * C, U32)
+        woven[3, 0] = strip[:, 7 * C : 9 * C]
         woven[0, 0] = strip[:, 8 * C : 10 * C]
         woven1 = strip[:, 10 * C : 14 * C]
         woven[2, 0] = strip[:, 13 * C : 15 * C]
@@ -92,13 +94,12 @@ def tile_moe_shr_mlp_relu2_kernel(
         h_codes += [sbuf(f"h_codes{e}", C, U32) for e in range(2, E)] + [sbuf("h_codes_shared", T, U32)]
         h_sc = {e: sbuf(f"h_sc{e}", C, U8) for e in range(2, E)}
         h_sc[SHARED] = sbuf("h_sc_shared", T, U8)
-        h_sc01 = sbuf("h_sc01", 2 * C, U8)
-        h_sc[0], h_sc[1] = h_sc01[:, 0:C], h_sc01[:, C : 2 * C]
 
-        y = [keep.tile([P, E * C], F32, name=f"y{n}") for n in range(BLOCKS)]
+        y = [keep.tile([P, E * C], F32, name=f"y{n}") for n in range(BLOCKS - 1)]
         gated = [[sbuf(f"gated{n}{r}", T, F32) for r in range(2)] for n in range(BLOCKS)]
         part_sum2 = sbuf("part_sum2", T, F32)
-        routed_sum1 = hidden[SHARED][:, 0 : 2 * T].bitcast(F32)
+        routed_sum1 = gated[0][1]
+        fetched = gated[0][0]
         routed_turned = sbuf("routed_turned", T, F32)
         shared_turned = sbuf("shared_turned", T, F32)
         result = [sbuf(f"result{n}", T, F32) for n in range(BLOCKS)]
@@ -298,6 +299,7 @@ def tile_moe_shr_mlp_relu2_kernel(
         gather(1, 3)
         quantise_slots(2, 0)
         gather(0, 3)
+        gather(3, 3)
         relu(0, b0)
         relu(1, b1)
         turn(0, b6)
@@ -309,14 +311,12 @@ def tile_moe_shr_mlp_relu2_kernel(
         woven[2, 1] = reuse("woven21", "w1_1", 2 * C, U32)
         weave_on_scalar(2, 1)
         quantise_slots(2, 1)
-        gather(3, 3)
-        gather(2, 3)
-        woven[3, 0] = reuse("woven30", "w1_1", 2 * C, U32)
         weave(3, 0)
-        weave(3, 1)
+        gather(2, 3)
         quantise_slots(3, 0)
+        weave(3, 1)
         quantise_slots(3, 1)
-        shared_sc[0] = reuse("shared_sc0", "w1_1", T, U8)
+        shared_sc[0] = reuse("shared_sc0", "woven31", T, U8)
         quantise_shared(0)
         first_product(4, b4, [1])
         first_product(5, b5, [1])
@@ -327,14 +327,19 @@ def tile_moe_shr_mlp_relu2_kernel(
         square(2, b0)
         relu(4, b4)
         turn(4, b2)
-        first_product(6, b4)
+        first_product(6, b4, [0])
         relu(5, b5)
-        first_product(7, b5)
+        first_product(7, b5, [0])
+        first_product(6, b4, [1])
+        first_product(7, b5, [1])
         turn(5, b3)
         square(3, b6)
+        h_sc01 = sbuf("h_sc01", 2 * C, U8)
+        h_sc[0], h_sc[1] = h_sc01[:, 0:C], h_sc01[:, C : 2 * C]
         quantise(h_codes01, h_sc01, hidden01)
         square(4, b2)
         first_product(8, b2, [0])
+        first_product(9, b6, [0])
         relu(6, b4)
         turn(6, b7)
         relu(7, b5)
@@ -347,7 +352,7 @@ def tile_moe_shr_mlp_relu2_kernel(
         first_product(8, b2, [1])
         quantise_hidden(2, 0, C)
         second_product(2, 0, b1[:, 0:C], 0, C)
-        first_product(9, b7)
+        first_product(9, b6, [1])
         quantise_hidden(3, 0, P)
         second_product(3, 0, b1[:, C : C + P], 0, P)
         quantise_hidden(3, P, C)
@@ -360,23 +365,22 @@ def tile_moe_shr_mlp_relu2_kernel(
         second_pair(2, 1, b3)
         relu(8, b2)
         first_product(10, b2)
-        relu(9, b7)
-        first_product(11, b7)
+        relu(9, b6)
+        first_product(11, b6)
         fetch_pair(0, 1, b4)
         turn(8, b5)
-        turn(9, b6)
+        turn(9, b7)
         fetch_pair(2, 1, b3)
         relu(10, b2)
         turn(10, b1)
-        relu(11, b7)
+        second_pair(0, 2, b2)
+        relu(11, b6)
         turn(11, b0)
-        square(8, b5)
-        second_pair(0, 2, b5)
-        square(9, b6)
         second_pair(2, 2, b6)
-        square(10, b1)
-        square(11, b0)
-        fetch_pair(0, 2, b5)
+        for k, bank in ((8, b5), (9, b7), (10, b1), (11, b0)):
+            square(k, bank)
+        y.append(keep.tile([P, E * C], F32, name="y2", tag="relued11", align_bytes=64))
+        fetch_pair(0, 2, b2)
         fetch_pair(2, 2, b6)
 
         for r in range(2):
@@ -386,24 +390,25 @@ def tile_moe_shr_mlp_relu2_kernel(
         for r in range(2):
             gather_back(gated[1][r], 1, r, 0, T)
         quantise_hidden(SHARED, 0, T)
-        halves = ((0, b2, b4), (HALF, b0, b1))
+        halves = ((0, b7, b4), (HALF, b0, b1))
         for c, source, bank in halves:
             shared_turned_product(source, c, c + HALF)
-        second_product(SHARED, 1, b7[:], 0, T)
+        second_product(SHARED, 1, b5[:], 0, T)
         second_product(SHARED, 2, b3[:], 0, T)
         for c, source, bank in halves:
             nc.scalar.copy(shared_turned[:, c : c + HALF], source[:, 0:HALF])
             turn_and_add(bank, shared_turned[:, c : c + HALF], routed_turned[:, c : c + HALF], HALF)
+        nc.scalar.activation(fetched, y[2][:].indirect(pos_sb[1][:]), COPY)
         for c, source, bank in halves:
             nc.scalar.copy(result[0][:, c : c + HALF], bank[:, 0:HALF])
             nc.scalar.dma_start(out=out[0:P, c : c + HALF], in_=result[0][:, c : c + HALF])
         add(routed_sum1, gated[1][0], gated[1][1])
         gather_back(gated[2][0], 2, 0, 0, T)
-        add(result[1], routed_sum1, b7[:])
+        add(result[1], routed_sum1, b5[:])
         nc.sync.dma_start(out=out[P : 2 * P, :], in_=result[1])
-        gather_back(gated[2][1], 2, 1, 0, T)
+        add(part_sum2, gated[2][0], b3[:])
         for c in (0, HALF):
-            add(part_sum2[:, c : c + HALF], gated[2][0][:, c : c + HALF], b3[:, c : c + HALF])
+            nc.vector.tensor_tensor(gated[2][1][:, c : c + HALF], fetched[:, c : c + HALF], gates[:, 1, c : c + HALF], MULT)
         for c in (0, HALF):
             add(result[2][:, c : c + HALF], part_sum2[:, c : c + HALF], gated[2][1][:, c : c + HALF])
             nc.sync.dma_start(out=out[2 * P : 3 * P, c : c + HALF], in_=result[2][:, c : c + HALF])

@@ -31,7 +31,7 @@ PER_COLUMN = 16
 BANK = 512
 HALF = T // 2
 PLANES = (1, 0, 3, 2)
-RELU_ON_VECTOR = (7,)
+RELU_ON_VECTOR = (6,)
 
 
 def tile_moe_shr_mlp_relu2_kernel(
@@ -66,22 +66,22 @@ def tile_moe_shr_mlp_relu2_kernel(
         relued = {k: reuse(f"relued{k}", f"relued{k}", H, F32) for k in range(TILES)}
         strip = sbuf("strip", 20 * C, U32)
         place = {
-            (0, 0): 0, (0, 1): 1, (2, 0): 2, (1, 0): 3, (1, 1): 4, (1, 2): 5, (3, 0): 6, (3, 1): 7,
-            (2, 1): 0, (0, 2): 2, (2, 2): 0, (3, 2): 7, (0, 3): 2, (1, 3): 11, (2, 3): 0, (3, 3): 5,
+            (0, 0): 0, (0, 1): 2, (2, 0): 4, (1, 0): 6, (1, 1): 8, (1, 2): 10, (3, 0): 12, (3, 1): 14,
+            (2, 1): 0, (0, 2): 4, (3, 2): 14, (0, 3): 20, (1, 3): 22, (2, 2): 3, (2, 3): 5, (3, 3): 10,
         }
         shared_woven = sbuf("shared_woven", PASSES * 2 * T, U32)
         woven = {(e, s): sbuf(f"woven{e}{s}", 2 * C, U32) for e, s in ((0, 1),)}
-        woven[3, 1] = reuse("woven31", "woven31", 2 * C, U32)
-        woven[3, 0] = strip[:, 7 * C : 9 * C]
+        woven[3, 1] = strip[:, 7 * C : 9 * C]
         woven[0, 0] = strip[:, 8 * C : 10 * C]
         woven1 = strip[:, 10 * C : 14 * C]
-        woven[2, 0] = strip[:, 13 * C : 15 * C]
+        woven[2, 0] = woven[3, 0] = strip[:, 13 * C : 15 * C]
         shared_codes = sbuf("shared_codes", PASSES * T, U32)
         x_codes = {(e, s): sbuf(f"x_codes{e}{s}", C, U32) for e in (0, 2, 3) for s in range(PASSES) if (e, s) != (3, 1)}
         x_codes[3, 1] = shared_codes[:, T : T + C]
         shared_sc = {1: sbuf("shared_sc1", T, U8)}
-        x_sc = {(e, s): sbuf(f"x_sc{e}{s}", C, U8) for e in (0, 2, 3) for s in range(PASSES) if (e, s) != (3, 1)}
+        x_sc = {(e, s): sbuf(f"x_sc{e}{s}", C, U8) for e in (0, 2, 3) for s in range(PASSES) if (e, s) not in ((2, 1), (3, 0), (3, 1))}
         x_sc[3, 1] = reuse("x_sc31", "x_sc31", C, U8)
+        x_sc[2, 1] = reuse("x_sc21", "x_sc21", C, U8)
         x_codes1, x_sc1 = sbuf("x_codes1", PASSES * C, U32), sbuf("x_sc1", PASSES * C, U8)
         for s in range(PASSES):
             woven[1, s] = woven1[:, 2 * C * s : 2 * C * (s + 1)]
@@ -154,10 +154,10 @@ def tile_moe_shr_mlp_relu2_kernel(
         def gather(j, e, experts=1):
             slots = offs_sb[:, e * C // PER_COLUMN : (e + experts) * C // PER_COLUMN]
             window = pairs[:, plane_start(j) : plane_start(j) + (T if experts == 1 else 2 * T)]
-            nc.vector.tensor_copy(strip[:, C * place[j, e] : C * (place[j, e] + experts)], window.indirect(slots))
+            nc.vector.tensor_copy(strip[:, P * place[j, e] : P * place[j, e] + C * experts], window.indirect(slots))
 
         def weave_views(e, s, dtype):
-            even, odd = C * place[2 * s, e], C * place[2 * s + 1, e]
+            even, odd = P * place[2 * s, e], P * place[2 * s + 1, e]
             src = strip[:, even : 2 * odd - even].bitcast(dtype).rearrange("p (u c) -> p c u", u=2)[:, 0:C, :]
             return woven[e, s].bitcast(dtype).rearrange("p (c u) -> p c u", u=2), src
 
@@ -295,105 +295,104 @@ def tile_moe_shr_mlp_relu2_kernel(
         first_product(3, b3)
         nc.gpsimd.tensor_copy(*weave_views(2, 0, U32))
         gather(3, 2)
-        gather(2, 2)
         gather(1, 3)
-        quantise_slots(2, 0)
         gather(0, 3)
+        quantise_slots(2, 0)
+        nc.gpsimd.tensor_copy(*weave_views(3, 0, U32))
+        gather(2, 2)
         gather(3, 3)
+        gather(2, 3)
         relu(0, b0)
         relu(1, b1)
         turn(0, b6)
         turn(1, b7)
         relu(2, b2)
-        turn(2, b0)
         first_product(4, b4, [0])
         first_product(5, b5, [0])
-        woven[2, 1] = reuse("woven21", "w1_1", 2 * C, U32)
+        relu(3, b3)
+        turn(2, b0)
+        turn(3, b1)
+        square(0, b6)
+        woven[2, 1] = reuse("woven21", "relued1", 2 * C, U32)
         weave_on_scalar(2, 1)
+        square(1, b7)
         quantise_slots(2, 1)
-        weave(3, 0)
-        gather(2, 3)
-        quantise_slots(3, 0)
-        weave(3, 1)
-        quantise_slots(3, 1)
-        shared_sc[0] = reuse("shared_sc0", "woven31", T, U8)
-        quantise_shared(0)
         first_product(4, b4, [1])
         first_product(5, b5, [1])
-        relu(3, b3)
-        square(0, b6)
-        turn(3, b6)
-        square(1, b7)
+        weave(3, 1)
+        x_sc[3, 0] = reuse("x_sc30", "relued1", C, U8)
+        quantise_slots(3, 0)
+        quantise_slots(3, 1)
+        for s in range(PASSES):
+            first_product(6, b6, [s])
+            first_product(7, b7, [s])
+        shared_sc[0] = reuse("shared_sc0", "x_sc21", T, U8)
+        quantise_shared(0)
         square(2, b0)
+        square(3, b1)
         relu(4, b4)
         turn(4, b2)
-        first_product(6, b4, [0])
         relu(5, b5)
-        first_product(7, b5, [0])
-        first_product(6, b4, [1])
-        first_product(7, b5, [1])
         turn(5, b3)
-        square(3, b6)
-        h_sc01 = sbuf("h_sc01", 2 * C, U8)
+        relu(6, b6)
+        turn(6, b4)
+        first_product(8, b6, [0])
+        relu(7, b7)
+        square(4, b2)
+        h_sc01 = reuse("h_sc01", "x_sc31", 2 * C, U8)
         h_sc[0], h_sc[1] = h_sc01[:, 0:C], h_sc01[:, C : 2 * C]
         quantise(h_codes01, h_sc01, hidden01)
-        square(4, b2)
-        first_product(8, b2, [0])
-        first_product(9, b6, [0])
-        relu(6, b4)
-        turn(6, b7)
-        relu(7, b5)
-        turn(7, b4)
+        second_pair(0, 0, b1)
+        turn(7, b5)
         quantise_shared(1)
         square(5, b3)
-        square(6, b7)
-        square(7, b4)
-        second_pair(0, 0, b5)
-        first_product(8, b2, [1])
+        square(6, b4)
+        square(7, b5)
+        first_product(8, b6, [1])
         quantise_hidden(2, 0, C)
-        second_product(2, 0, b1[:, 0:C], 0, C)
-        first_product(9, b6, [1])
+        second_product(2, 0, b0[:, 0:C], 0, C)
+        first_product(9, b2)
+        nc.vector.tensor_copy(y[0][:, 0 : 2 * C], b1[:])
         quantise_hidden(3, 0, P)
-        second_product(3, 0, b1[:, C : C + P], 0, P)
+        second_product(3, 0, b0[:, C : C + P], 0, P)
         quantise_hidden(3, P, C)
-        second_product(3, 0, b0[:, C + P : 2 * C], P, C)
-        nc.vector.tensor_copy(y[0][:, 2 * C : 3 * C + P], b1[:, 0 : C + P])
-        nc.vector.tensor_copy(y[0][:, 3 * C + P : 4 * C], b0[:, C + P : 2 * C])
-        fetch_pair(0, 0, b5)
+        second_product(3, 0, b7[:, C + P : 2 * C], P, C)
+        nc.vector.tensor_copy(y[0][:, 2 * C : 3 * C + P], b0[:, 0 : C + P])
+        nc.vector.tensor_copy(y[0][:, 3 * C + P : 4 * C], b7[:, C + P : 2 * C])
 
-        second_pair(0, 1, b4)
+        second_pair(0, 1, b5)
         second_pair(2, 1, b3)
-        relu(8, b2)
-        first_product(10, b2)
-        relu(9, b6)
-        first_product(11, b6)
-        fetch_pair(0, 1, b4)
-        turn(8, b5)
-        turn(9, b7)
+        relu(8, b6)
+        first_product(10, b6)
+        relu(9, b2)
+        first_product(11, b2)
+        fetch_pair(0, 1, b5)
+        turn(8, b1)
+        turn(9, b4)
         fetch_pair(2, 1, b3)
-        relu(10, b2)
-        turn(10, b1)
-        second_pair(0, 2, b2)
-        relu(11, b6)
-        turn(11, b0)
-        second_pair(2, 2, b6)
-        for k, bank in ((8, b5), (9, b7), (10, b1), (11, b0)):
+        relu(10, b6)
+        turn(10, b0)
+        second_pair(0, 2, b6)
+        relu(11, b2)
+        turn(11, b7)
+        second_pair(2, 2, b2)
+        for k, bank in ((8, b1), (9, b4), (10, b0), (11, b7)):
             square(k, bank)
         y.append(keep.tile([P, E * C], F32, name="y2", tag="relued11", align_bytes=64))
-        fetch_pair(0, 2, b2)
-        fetch_pair(2, 2, b6)
+        fetch_pair(0, 2, b6)
+        fetch_pair(2, 2, b2)
 
         for r in range(2):
             gather_back(gated[0][r], 0, r, 0, T)
-        turn_and_add(b1, gated[0][1], gated[0][0], T)
-        nc.scalar.copy(routed_turned, b1[:])
+        turn_and_add(b0, gated[0][1], gated[0][0], T)
+        nc.scalar.copy(routed_turned, b0[:])
         for r in range(2):
             gather_back(gated[1][r], 1, r, 0, T)
         quantise_hidden(SHARED, 0, T)
-        halves = ((0, b7, b4), (HALF, b0, b1))
+        halves = ((0, b4, b5), (HALF, b7, b0))
         for c, source, bank in halves:
             shared_turned_product(source, c, c + HALF)
-        second_product(SHARED, 1, b5[:], 0, T)
+        second_product(SHARED, 1, b1[:], 0, T)
         second_product(SHARED, 2, b3[:], 0, T)
         for c, source, bank in halves:
             nc.scalar.copy(shared_turned[:, c : c + HALF], source[:, 0:HALF])
@@ -404,11 +403,12 @@ def tile_moe_shr_mlp_relu2_kernel(
             nc.scalar.dma_start(out=out[0:P, c : c + HALF], in_=result[0][:, c : c + HALF])
         add(routed_sum1, gated[1][0], gated[1][1])
         gather_back(gated[2][0], 2, 0, 0, T)
-        add(result[1], routed_sum1, b5[:])
+        add(result[1], routed_sum1, b1[:])
         nc.sync.dma_start(out=out[P : 2 * P, :], in_=result[1])
         add(part_sum2, gated[2][0], b3[:])
-        for c in (0, HALF):
-            nc.vector.tensor_tensor(gated[2][1][:, c : c + HALF], fetched[:, c : c + HALF], gates[:, 1, c : c + HALF], MULT)
-        for c in (0, HALF):
-            add(result[2][:, c : c + HALF], part_sum2[:, c : c + HALF], gated[2][1][:, c : c + HALF])
-            nc.sync.dma_start(out=out[2 * P : 3 * P, c : c + HALF], in_=result[2][:, c : c + HALF])
+        last_pieces = (slice(0, HALF), slice(HALF, T))
+        for piece in last_pieces:
+            nc.vector.tensor_tensor(gated[2][1][:, piece], fetched[:, piece], gates[:, 1, piece], MULT)
+        for piece in last_pieces:
+            add(result[2][:, piece], part_sum2[:, piece], gated[2][1][:, piece])
+            nc.sync.dma_start(out=out[2 * P : 3 * P, piece], in_=result[2][:, piece])

@@ -336,14 +336,14 @@ def tile_moe_shr_mlp_relu2_kernel(
         turn(5, b3)
         relu(6, b6)
         turn(6, b4)
-        first_product(8, b6, [0])
         relu(7, b7)
+        turn(7, b5)
+        first_product(8, b6, [0])
         square(4, b2)
         h_sc01 = reuse("h_sc01", "x_sc31", 2 * C, U8)
         h_sc[0], h_sc[1] = h_sc01[:, 0:C], h_sc01[:, C : 2 * C]
         quantise(h_codes01, h_sc01, hidden01)
         second_pair(0, 0, b1)
-        turn(7, b5)
         quantise_shared(1)
         square(5, b3)
         square(6, b4)

from contextlib import ExitStack

import concourse.mybir as mybir
from concourse.masks import make_identity

K, T, E, C, H, N = 1024, 512, 4, 256, 512, 384
FLOPS = 2 * (E * C + T) * H * (K + N)

F32 = mybir.dt.float32
BF16 = mybir.dt.bfloat16
I32 = mybir.dt.int32
U32 = mybir.dt.uint32
U16 = mybir.dt.uint16
U8 = mybir.dt.uint8
FP8X4 = mybir.dt.float8_e4m3fn_x4
FP4X4 = mybir.dt.float4_e2m1fn_x4
RELU = mybir.ActivationFunctionType.Relu
SQUARE = mybir.ActivationFunctionType.Square
COPY = mybir.ActivationFunctionType.Copy
MULT = mybir.AluOpType.mult
ADD = mybir.AluOpType.add

P = 128
D = 4
PASSES = K // (P * D)
BLOCKS = N // P
SHARED = E
ROUTED_TILES = E * C // P
TILES = ROUTED_TILES + T // P
PER_COLUMN = 16
BANK = 512
HALF = T // 2
PLANES = (1, 0, 3, 2)
RELU_ON_VECTOR = (6,)


def tile_moe_shr_mlp_relu2_kernel(
    tc, xT, w1_words, w1_scales, w2_words, w2_scales, gate, offs, pos1, pos2, out
):
    nc = tc.nc
    with ExitStack() as ctx:
        keep = ctx.enter_context(tc.tile_pool(name="keep", bufs=1))
        psum = ctx.enter_context(tc.psum_pool(name="psum", bufs=1))
        b0, b1, b2, b3, b4, b5, b6, b7 = [psum.tile([P, BANK], F32, name=f"bank{b}") for b in range(8)]

        def sbuf(name, columns, dtype):
            return keep.tile([P, columns], dtype, name=name, align_bytes=64)[:]

        pieces = {j: 2 for j in PLANES}
        offs_sb = keep.tile([P, E * C // PER_COLUMN], U16, name="offs_sb")
        pos_sb = [keep.tile([P, T // PER_COLUMN], U16, name=f"pos_sb{r}") for r in range(2)]
        ident = keep.tile([P, P], F32, name="ident")
        x = {
            j: [keep.tile([P, 2, T // pieces[j]], F32, name=f"x{j}{h}", tag=f"x{j}{h}", align_bytes=64)[:] for h in range(pieces[j])]
            for j in PLANES
        }
        w1 = [keep.tile([P, PASSES, 2 * H], U8, name=f"w1_{e}", tag=f"w1_{e}", align_bytes=64) for e in range(E + 1)]
        w1_sc = keep.tile([P, (E + 1) * PASSES, H], U8, name="w1_sc", align_bytes=64)
        w2_sc = keep.tile([P, E + 1, N], U8, name="w2_sc", align_bytes=64)
        made_ident = keep.tile([P, P], F32, name="made_ident")

        pairs = sbuf("pairs", 5 * T, U32)
        def reuse(name, tag, columns, dtype):
            return keep.tile([P, columns], dtype, name=name, tag=tag, align_bytes=64)[:]

        relued = {k: reuse(f"relued{k}", f"relued{k}", H, F32) for k in range(TILES)}
        strip = sbuf("strip", 20 * C, U32)
        place = {
            (0, 0): 0, (0, 1): 2, (2, 0): 4, (1, 0): 6, (1, 1): 8, (1, 2): 10, (3, 0): 12, (3, 1): 14,
            (2, 1): 0, (0, 2): 4, (3, 2): 14, (0, 3): 20, (1, 3): 22, (2, 2): 3, (2, 3): 5, (3, 3): 10,
        }
        shared_woven = sbuf("shared_woven", PASSES * 2 * T, U32)
        woven = {(e, s): sbuf(f"woven{e}{s}", 2 * C, U32) for e, s in ((0, 1),)}
        woven[3, 1] = strip[:, 7 * C : 9 * C]
        woven[0, 0] = strip[:, 8 * C : 10 * C]
        woven1 = strip[:, 10 * C : 14 * C]
        woven[2, 0] = woven[3, 0] = strip[:, 13 * C : 15 * C]
        shared_codes = sbuf("shared_codes", PASSES * T, U32)
        x_codes = {(e, s): sbuf(f"x_codes{e}{s}", C, U32) for e in (0, 2, 3) for s in range(PASSES) if (e, s) != (3, 1)}
        x_codes[3, 1] = shared_codes[:, T : T + C]
        shared_sc = {1: sbuf("shared_sc1", T, U8)}
        x_sc = {(e, s): sbuf(f"x_sc{e}{s}", C, U8) for e in (0, 2, 3) for s in range(PASSES) if (e, s) not in ((2, 1), (3, 0), (3, 1))}
        x_sc[3, 1] = reuse("x_sc31", "x_sc31", C, U8)
        x_sc[2, 1] = reuse("x_sc21", "x_sc21", C, U8)
        x_codes1, x_sc1 = sbuf("x_codes1", PASSES * C, U32), sbuf("x_sc1", PASSES * C, U8)
        for s in range(PASSES):
            woven[1, s] = woven1[:, 2 * C * s : 2 * C * (s + 1)]
            x_codes[1, s], x_sc[1, s] = x_codes1[:, C * s : C * (s + 1)], x_sc1[:, C * s : C * (s + 1)]

        hidden01, h_codes01 = sbuf("hidden01", 2 * D * C, BF16), sbuf("h_codes01", 2 * C, U32)
        hidden = [hidden01[:, D * C * e : D * C * (e + 1)] for e in range(2)]
        hidden += [sbuf(f"hidden{e}", D * C, BF16) for e in range(2, E)] + [sbuf("hidden_shared", D * T, BF16)]
        h_codes = [h_codes01[:, C * e : C * (e + 1)] for e in range(2)]
        h_codes += [sbuf(f"h_codes{e}", C, U32) for e in range(2, E)] + [sbuf("h_codes_shared", T, U32)]
        h_sc = {e: sbuf(f"h_sc{e}", C, U8) for e in range(2, E)}
        h_sc[SHARED] = sbuf("h_sc_shared", T, U8)

        y = [keep.tile([P, E * C], F32, name=f"y{n}") for n in range(BLOCKS - 1)]
        gated = [[sbuf(f"gated{n}{r}", T, F32) for r in range(2)] for n in range(BLOCKS)]
        part_sum2 = sbuf("part_sum2", T, F32)
        routed_sum1 = gated[0][1]
        fetched = gated[0][0]
        routed_turned = sbuf("routed_turned", T, F32)
        shared_turned = sbuf("shared_turned", T, F32)
        result = [sbuf(f"result{n}", T, F32) for n in range(BLOCKS)]

        nc.vector.memset(w1_sc[:].bitcast(I32), 0)
        nc.vector.memset(w2_sc[:].bitcast(I32), 0)
        nc.vector.memset(pairs[:, 4 * T : 5 * T], 0)
        make_identity(nc, made_ident[:])
        nc.scalar.activation(ident[:], made_ident[:], RELU)

        x_rows = xT.rearrange("(s p d) t -> s p d t", s=PASSES, d=D)
        for j in PLANES:
            s, u = divmod(j, 2)
            width = T // pieces[j]
            for h in range(pieces[j]):
                nc.sync.dma_start(out=x[j][h], in_=x_rows[s, :, 2 * u : 2 * u + 2, width * h : width * (h + 1)])
            if j == PLANES[0]:
                nc.sync.dma_start(offs_sb[:], offs)

        def load_words(e):
            nc.sync.dma_start(out=w1[e][:].bitcast(I32), in_=w1_words[e].rearrange("s p b -> p s b").bitcast(I32))

        def load_scales(queue, dst, scales, first, last):
            rows = scales.rearrange("e s (q r) i -> q r (e s) i", q=4)
            for q in range(4):
                queue.dma_start(out=dst[32 * q : 32 * q + 4, first:last, :].bitcast(I32), in_=rows[q, :, first:last, :].bitcast(I32))

        load_words(0)
        load_scales(nc.sync, w1_sc, w1_scales, 0, 2 * PASSES)
        load_words(1)
        load_words(2)
        load_scales(nc.sync, w1_sc, w1_scales, 2 * PASSES, (E + 1) * PASSES)
        load_words(3)
        load_words(SHARED)
        load_scales(nc.sync, w2_sc, w2_scales, 0, E + 1)
        for r, positions in enumerate((pos1, pos2)):
            nc.sync.dma_start(pos_sb[r][:], positions)

        def plane_start(j):
            return T * ((j + 2) % 4)

        def plane(j):
            return pairs[:, plane_start(j) : plane_start(j) + T].bitcast(BF16)

        def cast_views(j):
            width = 2 * T // pieces[j]
            return [
                (plane(j)[:, width * h : width * (h + 1)].rearrange("p (t d) -> p t d", d=2), x[j][h].rearrange("p d t -> p t d"))
                for h in range(pieces[j])
            ]

        def gather(j, e, experts=1):
            slots = offs_sb[:, e * C // PER_COLUMN : (e + experts) * C // PER_COLUMN]
            window = pairs[:, plane_start(j) : plane_start(j) + (T if experts == 1 else 2 * T)]
            nc.vector.tensor_copy(strip[:, P * place[j, e] : P * place[j, e] + C * experts], window.indirect(slots))

        def weave_views(e, s, dtype):
            even, odd = P * place[2 * s, e], P * place[2 * s + 1, e]
            src = strip[:, even : 2 * odd - even].bitcast(dtype).rearrange("p (u c) -> p c u", u=2)[:, 0:C, :]
            return woven[e, s].bitcast(dtype).rearrange("p (c u) -> p c u", u=2), src

        def weave(e, s):
            nc.vector.tensor_copy(*weave_views(e, s, I32))

        def weave_on_scalar(e, s):
            nc.scalar.copy(*weave_views(e, s, U32))

        def quantise(codes, scales, values):
            nc.vector.quantize_mx(out=codes.bitcast(FP8X4), scales=scales, in_=values)

        def quantise_slots(e, s):
            quantise(x_codes[e, s], x_sc[e, s], woven[e, s].bitcast(BF16))

        def shared_views(s, first):
            tokens = slice(first, first + HALF)
            src = pairs[:, plane_start(2 * s) : plane_start(2 * s) + 2 * T].rearrange("p (u t) -> p t u", u=2)
            dst = shared_woven[:, 2 * T * s : 2 * T * (s + 1)].rearrange("p (t u) -> p t u", u=2)
            return dst[:, tokens, :], src[:, tokens, :]

        def quantise_shared(s):
            quantise(shared_codes[:, T * s : T * (s + 1)], shared_sc[s], shared_woven[:, 2 * T * s : 2 * T * (s + 1)].bitcast(BF16))

        def quantise_hidden(e, first, last):
            quantise(h_codes[e][:, first:last], h_sc[e][:, first:last], hidden[e][:, D * first : D * last])

        def expert_and_column(k):
            return divmod(P * k, C) if k < ROUTED_TILES else (SHARED, P * (k - ROUTED_TILES))

        def first_pass(k, s, bank, start, stop):
            e, column = expert_and_column(k)
            codes, scales = (x_codes[e, s], x_sc[e, s]) if e < E else (shared_codes[:, T * s : T * (s + 1)], shared_sc[s])
            columns = slice(column, column + P)
            nc.tensor.matmul_mx(
                out=bank[:],
                lhsT=codes[:, columns].bitcast(FP8X4),
                lhsT_scale=scales[:, columns],
                rhs=w1[e][:, s, :].bitcast(FP4X4),
                rhs_scale=w1_sc[:, PASSES * e + s, :],
                start=start,
                stop=stop,
            )

        def first_product(k, bank, passes=range(PASSES)):
            for s in passes:
                first_pass(k, s, bank, start=(s == 0), stop=(s == PASSES - 1))

        def relu(k, bank):
            dst, src = relued[k].rearrange("m (d p) -> m d p", d=D), bank[:].rearrange("m (p d) -> m d p", d=D)
            if k in RELU_ON_VECTOR:
                nc.vector.tensor_scalar_max(dst, src, 0.0)
            else:
                nc.scalar.activation(dst, src, RELU)

        def turn(k, bank):
            for d in range(D):
                nc.tensor.transpose(bank[:, P * d : P * (d + 1)], relued[k][:, P * d : P * (d + 1)], ident[:])

        def square(k, bank):
            e, column = expert_and_column(k)
            dst = hidden[e][:, D * column : D * (column + P)]
            nc.scalar.activation(dst.rearrange("p (m d) -> p m d", d=D), bank[:].rearrange("p (d m) -> p m d", d=D), SQUARE)

        def second_product(e, n, dst, first, last):
            nc.tensor.matmul_mx(
                out=dst,
                lhsT=w2[:, e, 2 * P * n : 2 * P * (n + 1)].bitcast(FP4X4),
                lhsT_scale=w2_sc[:, e, P * n : P * (n + 1)],
                rhs=h_codes[e][:, first:last].bitcast(FP8X4),
                rhs_scale=h_sc[e][:, first:last],
                start=True,
                stop=True,
            )

        def second_pair(e, n, bank):
            second_product(e + 1, n, bank[:, C : 2 * C], 0, C)
            second_product(e, n, bank[:, 0:C], 0, C)

        def fetch_pair(e, n, bank):
            nc.scalar.copy(y[n][:, e * C : (e + 2) * C], bank[:])

        def gather_back(dst, n, r, first, last):
            positions = pos_sb[r][:, first // PER_COLUMN : last // PER_COLUMN]
            nc.vector.tensor_tensor(dst, y[n][:].indirect(positions), gates[:, r, first:last], MULT)

        def turn_and_add(bank, later, earlier, width):
            for c in range(0, width, P):
                nc.tensor.matmul(bank[:, c : c + P], later[:, c : c + P], ident[:], start=True, stop=False, is_transpose=True)
                nc.tensor.matmul(bank[:, c : c + P], earlier[:, c : c + P], ident[:], start=False, stop=True, is_transpose=True)

        def shared_turned_product(bank, first, last):
            for c in range(first, last, P):
                nc.tensor.matmul_mx(
                    out=bank[:, c - first : c - first + P],
                    lhsT=h_codes[SHARED][:, c : c + P].bitcast(FP8X4),
                    lhsT_scale=h_sc[SHARED][:, c : c + P],
                    rhs=w2[:, SHARED, 0 : 2 * P].bitcast(FP4X4),
                    rhs_scale=w2_sc[:, SHARED, 0:P],
                    start=True,
                    stop=True,
                )

        def add(dst, left, right):
            nc.vector.tensor_tensor(dst, left, right, ADD)

        for dst, src in cast_views(PLANES[0]):
            nc.vector.tensor_copy(out=dst, in_=src)
        for j in PLANES[1:]:
            for dst, src in cast_views(j):
                nc.scalar.activation(dst, src, COPY)
        gates = keep.tile([P, 2, T], F32, name="gates", tag="x20", align_bytes=64)
        nc.scalar.dma_start(out=gates[:], in_=gate[:, 0:P, :].rearrange("g p t -> p g t"))
        for s, first in ((0, 0), (0, HALF), (1, 0)):
            nc.gpsimd.tensor_copy(*shared_views(s, first))
        for j, experts in ((1, 3), (0, 2), (3, 2), (2, 1)):
            gather(j, 0, experts)
        weave_on_scalar(0, 0)
        weave_on_scalar(1, 0)
        w2 = keep.tile([P, E + 1, 2 * N], U8, name="w2", tag="x21", align_bytes=64)
        nc.scalar.dma_start(out=w2[:].bitcast(I32), in_=w2_words.rearrange("e s p b -> p (e s) b").bitcast(I32))
        weave_on_scalar(0, 1)
        quantise_slots(0, 0)
        first_product(0, b0, [0])
        first_product(1, b1, [0])
        gather(2, 1)
        weave_on_scalar(1, 1)
        nc.scalar.copy(*shared_views(1, HALF))
        quantise_slots(0, 1)
        first_product(0, b0, [1])
        first_product(1, b1, [1])
        gather(0, 2)
        quantise(x_codes1, x_sc1, woven1.bitcast(BF16))
        first_product(2, b2)
        first_product(3, b3)
        nc.gpsimd.tensor_copy(*weave_views(2, 0, U32))
        gather(3, 2)
        gather(1, 3)
        gather(0, 3)
        quantise_slots(2, 0)
        nc.gpsimd.tensor_copy(*weave_views(3, 0, U32))
        gather(2, 2)
        gather(3, 3)
        gather(2, 3)
        relu(0, b0)
        relu(1, b1)
        turn(0, b6)
        turn(1, b7)
        relu(2, b2)
        first_product(4, b4, [0])
        first_product(5, b5, [0])
        relu(3, b3)
        turn(2, b0)
        turn(3, b1)
        square(0, b6)
        woven[2, 1] = reuse("woven21", "relued1", 2 * C, U32)
        weave_on_scalar(2, 1)
        square(1, b7)
        quantise_slots(2, 1)
        first_product(4, b4, [1])
        first_product(5, b5, [1])
        weave(3, 1)
        x_sc[3, 0] = reuse("x_sc30", "relued1", C, U8)
        quantise_slots(3, 0)
        quantise_slots(3, 1)
        for s in range(PASSES):
            first_product(6, b6, [s])
            first_product(7, b7, [s])
        shared_sc[0] = reuse("shared_sc0", "x_sc21", T, U8)
        quantise_shared(0)
        square(2, b0)
        square(3, b1)
        relu(4, b4)
        turn(4, b2)
        relu(5, b5)
        turn(5, b3)
        relu(6, b6)
        turn(6, b4)
        relu(7, b7)
        turn(7, b5)
        first_product(8, b6, [0])
        square(4, b2)
        h_sc01 = reuse("h_sc01", "x_sc31", 2 * C, U8)
        h_sc[0], h_sc[1] = h_sc01[:, 0:C], h_sc01[:, C : 2 * C]
        quantise(h_codes01, h_sc01, hidden01)
        second_pair(0, 0, b1)
        quantise_shared(1)
        square(5, b3)
        square(6, b4)
        square(7, b5)
        first_product(8, b6, [1])
        quantise_hidden(2, 0, C)
        second_product(2, 0, b0[:, 0:C], 0, C)
        first_product(9, b2)
        nc.vector.tensor_copy(y[0][:, 0 : 2 * C], b1[:])
        quantise_hidden(3, 0, P)
        second_product(3, 0, b0[:, C : C + P], 0, P)
        quantise_hidden(3, P, C)
        second_product(3, 0, b7[:, C + P : 2 * C], P, C)
        nc.vector.tensor_copy(y[0][:, 2 * C : 3 * C + P], b0[:, 0 : C + P])
        nc.vector.tensor_copy(y[0][:, 3 * C + P : 4 * C], b7[:, C + P : 2 * C])

        second_pair(0, 1, b5)
        second_pair(2, 1, b3)
        relu(8, b6)
        first_product(10, b6)
        relu(9, b2)
        first_product(11, b2)
        fetch_pair(0, 1, b5)
        turn(8, b1)
        turn(9, b4)
        fetch_pair(2, 1, b3)
        relu(10, b6)
        turn(10, b0)
        second_pair(0, 2, b6)
        relu(11, b2)
        turn(11, b7)
        second_pair(2, 2, b2)
        for k, bank in ((8, b1), (9, b4), (10, b0), (11, b7)):
            square(k, bank)
        y.append(keep.tile([P, E * C], F32, name="y2", tag="relued11", align_bytes=64))
        fetch_pair(0, 2, b6)
        fetch_pair(2, 2, b2)

        for r in range(2):
            gather_back(gated[0][r], 0, r, 0, T)
        turn_and_add(b0, gated[0][1], gated[0][0], T)
        nc.scalar.copy(routed_turned, b0[:])
        for r in range(2):
            gather_back(gated[1][r], 1, r, 0, T)
        quantise_hidden(SHARED, 0, T)
        halves = ((0, b4, b5), (HALF, b7, b0))
        for c, source, bank in halves:
            shared_turned_product(source, c, c + HALF)
        second_product(SHARED, 1, b1[:], 0, T)
        second_product(SHARED, 2, b3[:], 0, T)
        for c, source, bank in halves:
            nc.scalar.copy(shared_turned[:, c : c + HALF], source[:, 0:HALF])
            turn_and_add(bank, shared_turned[:, c : c + HALF], routed_turned[:, c : c + HALF], HALF)
        nc.scalar.activation(fetched, y[2][:].indirect(pos_sb[1][:]), COPY)
        for c, source, bank in halves:
            nc.scalar.copy(result[0][:, c : c + HALF], bank[:, 0:HALF])
            nc.scalar.dma_start(out=out[0:P, c : c + HALF], in_=result[0][:, c : c + HALF])
        add(routed_sum1, gated[1][0], gated[1][1])
        gather_back(gated[2][0], 2, 0, 0, T)
        add(result[1], routed_sum1, b1[:])
        nc.sync.dma_start(out=out[P : 2 * P, :], in_=result[1])
        add(part_sum2, gated[2][0], b3[:])
        last_pieces = (slice(0, HALF), slice(HALF, T))
        for piece in last_pieces:
            nc.vector.tensor_tensor(gated[2][1][:, piece], fetched[:, piece], gates[:, 1, piece], MULT)
        for piece in last_pieces:
            add(result[2][:, piece], part_sum2[:, piece], gated[2][1][:, piece])
            nc.sync.dma_start(out=out[2 * P : 3 * P, piece], in_=result[2][:, piece])
